import numpy as np, ml_dtypes
CORES = [2,7,18,23,34]
N = 5
BF = ml_dtypes.bfloat16
W, L, S, J, TB, D = 4096, 256, 16, 32, 2, 3
NE = (TB + 1) // 2 * L
def cands(u, k):
    return ((u * u >> 5)[..., None] + (2 * np.arange(J) + 1) * u[..., None] + k) & (W - 1)
def pairs(rng, n, pen):
    s = np.arange(W) % S
    kv = rng.random(W) + pen * ((s < TB) & (s % 2 == 0)); ky = rng.random(W) + pen * ((s < TB) & (s % 2 == 1))
    row = np.full(W, -1, np.int64); row[rng.permutation(np.argsort(kv)[:n])] = np.argsort(ky)[:n]
    return row
def filled(rng, lo, hi):
    return np.stack([np.stack([pairs(rng, int(W * (lo + (hi - lo) * rng.random())), 0.6) for g in range(8)]) for r in range(N)])
def pack(x, a, w):
    b = np.full((N, 8, W), -1, np.int64)
    for r in range(N):
        for g in range(8):
            v = np.flatnonzero(a[r, g] >= 0); b[(r + 1) % N, g, a[r, g, v]] = v
    return {"x": np.ascontiguousarray(x).reshape(N, 128, W).astype(np.float32).astype(BF), "pa": a.astype(np.int32), "pb": b.astype(np.int32), "wt": np.ascontiguousarray(w).reshape(N, 128, 1).astype(np.int32)}
def some(rng, m):
    us = np.flatnonzero(m)
    return int(us[int(rng.integers(0, us.size))]) if us.size else 0
def hashed(z, w, u):
    z = np.array(z); z[:2] = 0; rho = (u - int(np.sum(w * z))) & (W - 1); z[0] = rho & 255; z[1] = rho >> 8
    return z
def firststep(x, a, w, r):
    q = (r + 1) % N; v = S * np.arange(L); z = x[r][:, :, v]; u = np.sum(w[q][:, :, None] * z, axis=1) & (W - 1); c = cands(u, 0)
    col = np.take_along_axis(x[q], c.reshape(8, 1, L * J), 2).reshape(8, 16, L, J); key = np.sum(np.abs(col - z[..., None]), axis=1) * W + c
    y = np.take_along_axis(c, np.argmin(key, axis=2)[..., None], 2)[..., 0]; taken = np.zeros((8, W), bool)
    for g in range(8): taken[g, a[r, g][a[r, g] >= 0]] = True
    return y, (a[r][:, v] < 0) & ~np.take_along_axis(taken, y, 1), taken
def setup_inputs(rng):
    return pack(rng.integers(0, 256, (N, 8, 16, W)), filled(rng, 0.4, 0.85), rng.integers(1, 4096, (N, 8, 16)))
def setup_inputs_spread(rng):
    x = np.minimum(np.exp2(8 * rng.random((N, 8, 1, W))) * rng.random((N, 8, 16, W)) * 1.25, 255).astype(np.int64) * (rng.random((N, 8, 1, W)) > 0.0625)
    w = np.minimum(np.maximum(np.exp2(12 * rng.random((N, 8, 16))).astype(np.int64), 1), 4095)
    return pack(x, filled(rng, 0.05, 0.95), w)
def setup_inputs_ties(rng):
    recs = rng.integers(0, 256, (1, 8, 16, 12)); recs[..., 0] = 0; recs[..., 1] = 0; recs[:, :, 0, 1] = 1
    pick = rng.integers(0, 12, (N, 8, W)); w = rng.integers(1, 4096, (N, 8, 16)); w[:, :, 0] = 2048
    x = np.take_along_axis(np.ascontiguousarray(np.broadcast_to(recs, (N, 8, 16, 12))), pick[:, :, None, :], 3)
    return pack(x, filled(rng, 0.3, 0.9), w)
def setup_inputs_corners(rng):
    x = rng.integers(0, 256, (N, 8, 16, W)); col = rng.random((N, 8, 1, W)); x = np.where(col < 0.06, 0, np.where(col > 0.94, 255, x))
    w = rng.integers(1, 4096, (N, 8, 16)); k = rng.integers(0, 4, (N, 8, 1)); w = np.where(k == 0, 1, np.where(k == 1, 4095, w))
    off = int(rng.integers(0, 8)); a = np.full((N, 8, W), -1, np.int64); s = np.arange(W)
    for r in range(N):
        for g in range(8):
            m = (r + g + off) % 8
            if m == 1: a[r, g] = rng.permutation(W)
            elif m == 2: a[r, g] = pairs(rng, W - NE, 2.0)
            elif m == 3: a[r, g, np.delete(s, W - S)] = rng.permutation(W - 1)
            elif m == 4 or m == 5:
                v = np.flatnonzero(pairs(rng, W // 2 if m == 4 else 3 * W // 4, 0.6) >= 0); a[r, g, v] = v if m == 4 else W - 1 - v
            elif m == 6:
                a[r, g] = pairs(rng, 3 * W // 4, 2.0); rec = rng.integers(0, 256, (16, 1))
                for t in range(0, TB, 2): x[r, g][:, t::S] = rec
    tab = cands(np.arange(W), 0); starter = (s % S < TB) & (s % S % 2 == 0)
    for r in range(N):
        g = (7 - r - off) % 8; q = (r + 1) % N; w[q, g, 0] = 1; w[q, g, 1] = 256
        lanes = np.concatenate([np.arange(0, 32, 2 - r % 2), np.arange(32, 96)]); pl = np.where(lanes < 32, 97 + lanes, 128 + lanes)
        held = a[r - 1, g]; held = held[held >= 0]; held = held[held % S >= TB]; h = rng.permutation(held)[:lanes.size]
        row = np.full(W, -1, np.int64); row[h] = pl[:h.size]; fv = ~starter; fv[h] = False; fy = np.ones(W, bool); fy[96:129] = False; fy[160:224] = False
        row[rng.permutation(np.flatnonzero(fv))[:W // 2]] = rng.permutation(np.flatnonzero(fy))[:W // 2]; a[r, g] = row
        for e in range(h.size):
            k = int(lanes[e]); P = int(pl[e]); z = hashed(rng.integers(0, 256, 16), w[q, g], some(rng, np.any(tab == P, axis=1)))
            if k < 32: there = z; back = np.zeros(16, np.int64)
            else:
                kk = (k - 32) >> 1 if r % 2 == 1 else 2 * ((k - 32) >> 2)
                hit = ((tab + 97 + kk) & (W - 1)) == P; there = hashed(z, w[q, g], some(rng, np.any(hit, axis=1) & ~np.all(hit, axis=1))); back = there
            x[r, g][:, S * k] = z; x[q, g][:, P] = there; x[r, g][:, int(h[e])] = back
    for r in range(0, N, 2):
        g = (7 - r - off) % 8; y, go, taken = firststep(x, a, w, r); n = 0
        for b in range(8): n = n + int(np.unique(y[b][go[b]]).size)
        if n % 2 == 1:
            cnt = np.bincount(y[g][go[g]], minlength=W); one = np.flatnonzero(go[g] & (cnt[y[g]] == 1) & (np.arange(L) >= 96))
            fr = ~taken[g]; fr[y[g]] = False; fr[96:129] = False; fr[160:224] = False; fr = np.flatnonzero(fr)
            if one.size and fr.size: a[r, g, S * int(one[int(rng.integers(0, one.size))])] = int(fr[int(rng.integers(0, fr.size))])
    return pack(x, a, w)
def setup_inputs_ends(rng):
    kind = (7 - np.arange(8)[None, :] + N - 1 - np.arange(N)[:, None]) % 4
    w = np.where(rng.random((N, 8, 16)) < 0.5, 1, 4095); w[kind == 0] = 4095; w[kind == 3] = 1
    x = 255 * (rng.random((N, 8, 16, W)) < rng.choice(np.array([0.0, 0.25, 0.5, 0.75, 1.0]), (N, 8, 1, W))).astype(np.int64)
    pick = rng.random((N, 8, L)) < 0.25; pick[:, :, L - 1] = True; x[:, :, :, ::S] = np.where(pick[:, :, None, :], 255, x[:, :, :, ::S])
    tab = cands(np.arange(W), 0); top = np.max(tab, axis=1); pool = np.flatnonzero(top == np.max(top))
    a = np.full((N, 8, W), -1, np.int64); n = 3 * W // 8
    for r in range(N):
        for g in range(8):
            if kind[r, g] == 1:
                need = int(pool[int(rng.integers(0, pool.size))]) * 3839; i = int(rng.integers(0, 16)); o = (i + 1) % 16; w[r, g, i] = 0
                if (need - int(np.sum(w[r, g]))) & (W - 1) == 0: w[r, g, o] = 4096 - w[r, g, o]
                w[r, g, i] = (need - int(np.sum(w[r, g]))) & (W - 1)
            c = cands(np.array([255 * int(np.sum(w[r, g])) & (W - 1)]), 0)[0]; c = c[c % S != 0]
            if c.size:
                x[r, g][:, c] = 0
                if kind[r, g] == 2: x[r, g][:, int(np.max(c))] = 255
            v = rng.permutation(W); v = v[(v != 0) & (v != W - 1) & (v != W - S)][:n]; y = rng.permutation(W); y = y[(y != 0) & (y != W - 1)][:n]
            a[r, g, v] = y
            if g % 2 == 0: a[r, g, 0] = W - 1; a[r, g, W - 1] = 0
    return pack(x, a, w)
def setup_inputs_paths(rng):
    x = rng.integers(0, 256, (N, 8, 16, W)); w = rng.integers(1, 4096, (N, 8, 16)); w[:, :, 0] = 1; w[:, :, 1] = 256
    tab = cands(np.arange(W), 0); s = np.arange(W); gs = rng.permutation(8); lanes = np.argsort(rng.random((N, 8, L)), axis=-1); cnt = np.zeros((N, 8), np.int64)
    use = np.zeros((N, 8, W), bool); use[:, :, s % S < TB] = True; use[:, :, 1850:1920] = True; use[:, :, 3770:3840] = True
    for o in range(0, W, 1024): use[:, :, o + 96:o + 256] = True
    fv = [[[] for g in range(8)] for r in range(N)]; fy = [[[] for g in range(8)] for r in range(N)]; link = [[[] for g in range(8)] for r in range(N)]
    k0 = np.zeros(N, np.int64); k1 = np.zeros(N, np.int64)
    def start(r, g):
        v = S * int(lanes[r, g, cnt[r, g]]); cnt[r, g] += 1; fv[r][g].append(v)
        return v
    def spot(r, g):
        c = np.flatnonzero(~use[r, g]); p = int(c[int(rng.integers(0, c.size))]); use[r, g, p] = True
        return p
    def reach(r, g, k, v=None, u=0):
        z = rng.integers(0, 256, 16)
        for e in range(40):
            z = rng.integers(0, 256, 16)
            if v is not None: z = hashed(z, v, u)
            c = cands(np.array([int(np.sum(w[r, g] * z)) & (W - 1)]), k)[0]; c = c[~use[r, g, c]]
            if c.size:
                p = int(c[int(rng.integers(0, c.size))]); use[r, g, p] = True
                return z, p
        return z, -1
    def visit(r, g, P, rec, b):
        q = (r + 1) % N; m = np.any(tab == P, axis=1)
        if not np.any(m): return None
        z = hashed(rng.integers(0, 256, 16), w[q, g], some(rng, m)); v = start(r, g)
        if b < 0: b = spot(r, g)
        x[r, g][:, v] = z; x[q, g][:, P] = z; x[r, g][:, b] = rec; link[r][g].append((b, P))
        return z
    for r in range(N):
        q = (r + 1) % N; g = int(gs[0])
        for i in range(L):
            z, p = reach(q, g, 0)
            if p >= 0: x[r, g][:, S * i] = z; x[q, g][:, p] = z; fv[r][g].append(S * i); fy[r][g].append(p); k0[q] += 1
        g = int(gs[1]); xq = x[q, g]
        z = hashed(rng.integers(200, 256, 16), w[q, g], 4095); x[r, g][:, start(r, g)] = z; c = cands(np.array([4095]), 0)[0]
        j = 2 * int(rng.integers(1, J // 2)); xq[:, c] = 0; xq[5, c[j]] = 8; xq[5, c[j - 1]] = 8; fy[r][g].append(int(c[j])); fy[r][g].append(int(c[j - 1]))
        z = hashed(rng.integers(200, 256, 16), w[q, g], 2047); x[r, g][:, start(r, g)] = z; c = cands(np.array([2047]), 0)[0]
        xq[:, c] = 0; xq[6, c] = (int(np.sum(z)) - 4) & 15; xq[5, c[0]] = 1; fy[r][g].append(int(c[0])); k0[q] += 2
    ka = [int(k) & 31 for k in k0]
    for r in range(N):
        q = (r + 1) % N; g = int(gs[2])
        if q % 2 == 1:
            w[q, g, 2] = 0; need = (1024 + 2048 * int(rng.integers(0, 2))) * 3839
            if (need - int(np.sum(w[q, g]))) & (W - 1) == 0: w[q, g, 3] += 1 if w[q, g, 3] < 4095 else -1
            w[q, g, 2] = (need - int(np.sum(w[q, g]))) & (W - 1)
            if visit(r, g, 1024 + 97 + ka[q], np.full(16, 255, np.int64), -1) is not None:
                x[q, g][:, 3072 + 97 + ka[q]] = 0; fy[r][g].append(3072 + 97 + ka[q]); k1[q] += 1
        g = int(gs[4])
        if r % 2 == 1:
            for o in (0, 2048):
                rb, b = reach(r, g, 97 + ka[r], w[q, g], o); z, p = reach(r, g, 0)
                if b >= 0 and p >= 0 and visit(r, g, o + 97 + ka[q], rb, b) is not None:
                    fy[r][g].append(o + 194); v = start(r - 1, g); e = spot(r - 1, g)
                    x[r - 1, g][:, v] = z; x[r, g][:, p] = z; x[r - 1, g][:, e] = rb; link[r - 1][g].append((e, p)); fy[r - 1][g].append(b); k1[r] += 1
    kb = [int(k) & 31 for k in k1]
    for r in range(N):
        q = (r + 1) % N; g = int(gs[3])
        for o in (0, 2048):
            if visit(r, g, o + 97 + ka[q], hashed(rng.integers(0, 256, 16), w[q, g], o), -1) is not None: fy[r][g].append(o + 194 + kb[q])
        g = int(gs[5]); z1, p = reach(q, g, 97 + ka[q])
        if p >= 0:
            z = visit(r, g, 1024 + 194 + kb[q], z1, -1)
            if z is not None:
                z = hashed(z, w[q, g], 1024); b = spot(r, g); x[q, g][:, p] = z1; x[r, g][:, b] = z; link[r][g].append((b, p))
                x[q, g][:, 3072 + 194 + kb[q]] = np.where(z < 128, 255, 0); fy[r][g].append(3072 + 194 + kb[q])
    a = np.full((N, 8, W), -1, np.int64)
    for r in range(N):
        for g in range(8):
            mv = np.ones(W, bool); my = np.ones(W, bool); mv[np.array(fv[r][g], np.int64)] = False; my[np.array(fy[r][g], np.int64)] = False
            for v, y in link[r][g]: mv[v] = False; my[y] = False; a[r, g, v] = y
            vs = np.flatnonzero(mv); vs = np.concatenate([vs[vs % S == 0], rng.permutation(vs[vs % S != 0])[:W // 2]])
            a[r, g, vs] = rng.permutation(np.flatnonzero(my))[:vs.size]
    return pack(x, a, w)
def check_inputs(d):
    bad = []; xx = np.asarray(d["x"]).astype(np.float32)
    if not (np.min(xx) >= 0 and np.max(xx) <= 255): bad.append("range of x")
    if np.any(xx != np.floor(xx)): bad.append("x not whole")
    for k, lo, hi in (("pa", -1, W - 1), ("pb", -1, W - 1), ("wt", 1, 4095)):
        if not (np.min(d[k]) >= lo and np.max(d[k]) <= hi): bad.append("range of " + k)
    own = np.arange(W)[None, :]; off = False
    for r in range(N):
        a = np.asarray(d["pa"])[r].astype(np.int64); b = np.asarray(d["pb"])[(r + 1) % N].astype(np.int64)
        for c, e in ((a, b), (b, a)):
            if np.any((c >= 0) & (np.take_along_axis(e, np.clip(c, 0, W - 1), 1) != own)): off = True
    if off: bad.append("pa and pb not mutual")
    return bad
def reference(x, pa, pb, wt):
    X = x.astype(np.float32).astype(np.int32).reshape(N, 8, 16, W); A = pa.astype(np.int64); B = pb.astype(np.int64); w = wt.astype(np.int64).reshape(N, 8, 16, 1)
    kap = np.zeros(N, np.int64); lane = np.arange(L)
    for t in range(TB):
        q = (np.arange(N) + (1 if t % 2 == 0 else -1)) % N
        near, far = (A, B) if t % 2 == 0 else (B, A)
        v = S * lane + t; x0 = X[:, :, :, v]; z = x0; live = near[:, :, v] < 0; last = np.full((N, 8, L), -1, np.int64)
        for d in range(D):
            u = np.sum(w[q] * z, axis=2) & (W - 1)
            c = cands(u, (97 * d + kap[q])[:, None, None, None])
            col = np.take_along_axis(X[q], c.reshape(N, 8, 1, L * J), 3).reshape(N, 8, 16, L, J)
            dist = np.sum(np.abs(col - z[..., None]), axis=2)
            key = np.where(c == last[..., None], 2 ** 24, dist.astype(np.int64) * W + c)
            y = np.take_along_axis(c, np.argmin(key, axis=3)[..., None], 3)[..., 0]
            go = live & (np.take_along_axis(far[q], y, 2) < 0)
            rr, gg, ii = np.nonzero(go); low = np.full((N, 8, W), L, np.int64); np.minimum.at(low, (rr, gg, y[go]), ii)
            win = go & (np.take_along_axis(low, y, 2) == lane)
            rr, gg, ii = np.nonzero(win); yy = y[win]; qq = q[rr]; vv = S * ii + t
            X[qq, gg, :, yy] = (X[qq, gg, :, yy] + x0[rr, gg, :, ii]) >> 1
            far[qq, gg, yy] = vv; near[rr, gg, vv] = yy
            live = live & ~win; kap = np.bincount(qq, minlength=N).astype(np.int64) & 31; last = y
            p = np.maximum(np.take_along_axis(far[q], y, 2), 0)
            z = np.where(live[:, :, None, :], np.take_along_axis(X, p[:, :, None, :], 3), z)
    return {"yx": X.reshape(N, 128, W).astype(np.float32).astype(BF), "ya": A.astype(np.float32), "yb": B.astype(np.float32)}

@@ -1,0 +1,488 @@
+from concourse.mybir import AluOpType as OP, AxisListType, ActivationFunctionType as AF
+
+N = 5
+WN = 4096
+WD = 4352
+STEPS = 3
+NR = 4
+SCH = [[(4, 8)], [(8, 12)], [(12, 16)], [(16, 20)], [(20, 24)], [(24, 28)], [(28, 30), (30, 32)]]
+EARLY = 3
+PORTIONS = ((0, 128, "pc", "pt"), (128, 512, "pla", "ph"))
+
+SCRATCH = {}
+for _n, _c, _d in (
+        ("X", WD, "bfloat16"), ("XR0", WD, "bfloat16"), ("XR1", WD, "bfloat16"), ("OA", WD, "float32"), ("OB", WD, "float32"),
+        ("IOTA", WD + 8, "float32"), ("A", 8192, "bfloat16"), ("M", 8192, "bfloat16"), ("zb", 256, "bfloat16"),
+        ("pai", 256, "int32"), ("pbi", 256, "int32"), ("wti", 1, "int32"), ("wf", 1, "float32"), ("wg", 1, "float32"),
+        ("pidx", 1, "int32"), ("pmi", 1, "int32"), ("pgi", 1, "int32"), ("pidf", 1, "float32"), ("pmf", 1, "float32"), ("pgf", 1, "float32"), ("pg15", 1, "float32"),
+        ("kc", 8, "float32"),
+        ("col", 256, "float32"), ("colL", 512, "float32"), ("colJ", 512, "float32"), ("colg", 128, "float32"), ("dl", 512, "float32"),
+        ("E8", 144, "bfloat16"), ("E4n", 144, "bfloat16"), ("WG", 8, "float16"), ("GS", 8, "bfloat16"), ("CK", 2, "bfloat16"),
+        ("I16", 128, "float16"), ("IB", 128, "bfloat16"), ("IB8", 128, "bfloat16"), ("INB", 128, "bfloat16"), ("IBAR", 128, "bfloat16"), ("BO", 128, "bfloat16"), ("TRI", 128, "bfloat16"), ("ONE", 512, "bfloat16"),
+        ("DM", 256, "float32"), ("DMD", 256, "float32"), ("OFFB", 256, "bfloat16"), ("SEG", 256, "float32"), ("SEGB", 256, "float32"),
+        ("RH", 512, "float16"), ("RU", 512, "float16"), ("RZ", 512, "float16"), ("RK", 512, "bfloat16"), ("RO", 512, "bfloat16"), ("KC", 128, "bfloat16"), ("KT", 128, "bfloat16"), ("vr0", 256, "float32"), ("vr1", 256, "float32"), ("DC", 16, "float32"),
+        ("ui", 128, "int32"), ("u", 128, "int32"), ("sq", 128, "int32"), ("hm", 128, "int32"), ("UT", 128, "float16"), ("HT", 128, "float16"), ("ZT", 128, "float16"), ("LT", 128, "float16"), ("TB", 16, "float16"),
+        ("RR", 512, "bfloat16"), ("LST", 512, "uint16"), ("c16", 512, "float16"), ("bar", 512, "bfloat16"),
+        ("ym", 16, "float32"), ("yi", 16, "int32"), ("y", 16, "int32"), ("yc", 16, "float32"), ("yl", 16, "uint16"), ("Yr", 256, "uint16"), ("Or", 256, "bfloat16"),
+        ("XG", 256, "bfloat16"), ("sm", 256, "float16"), ("t2", 256, "float32"), ("qs", 256, "float32"), ("nw", 16, "float32"), ("EQ", 2176, "bfloat16"),
+        ("lf", 16, "float32"), ("pm", 256, "float32"), ("ps", 256, "float32"), ("pl16", 16, "uint16"), ("PLf", 16, "float32"), ("wb", 16, "bfloat16"), ("wd", 16, "float32"),
+        ("k1", 1, "float32"), ("kr", 1, "float32"), ("kf", 1, "float32")):
+    SCRATCH[_n] = ("sbuf", [128, _c], _d)
+for _t in range(2):
+    for _n, _c, _d in (("SS", 256, "bfloat16"), ("SR", 256, "bfloat16"), ("DS", 16, "float32"), ("DR", 16, "float32"), ("PS", 16, "uint16"), ("PR", 16, "uint16")):
+        SCRATCH["%s%d" % (_n, _t)] = ("sbuf", [128, _c], _d)
+    for _s in range(STEPS):
+        SCRATCH["XN%d" % _s] = ("sbuf", [128, 256], "bfloat16")
+        SCRATCH["L2%d" % _s] = ("sbuf", [128, 16], "uint16")
+        if _s < STEPS - 1:
+            SCRATCH["XI%d%d" % (_t, _s)] = ("sbuf", [128, 256], "bfloat16")
+            SCRATCH["LI%d%d" % (_t, _s)] = ("sbuf", [128, 16], "uint16")
+SCRATCH["oad"] = ("dram", [8, WN], "float32")
+SCRATCH["obd"] = ("dram", [8, WN], "float32")
+for _n, _c in (("pz", 1024), ("ph", 512), ("pt", 512), ("pc", 512), ("pla", 512), ("pk", 512), ("pq", 512)):
+    SCRATCH[_n] = ("psum", [128, _c], "float32")
+PARTS = ("ym", "RO", "RZ", "A0")
+PSUM = ("pz", "ph", "pt", "pc", "pla", "pk", "pq")
+
+MSG = []
+for _t in range(2):
+    MSG += ["S%d" % _t, "B%d" % _t, "D%d" % _t, "P%d" % _t]
+    for _s in range(STEPS - 1):
+        MSG += ["X%d%d" % (_t, _s), "L%d%d" % (_t, _s)]
+SEMAPHORES = ["cv", "cs", "cp", "cg", "ldx", "ldw", "lda", "ldb", "sta", "stb", "roa", "rob", "outx", "outa", "outb"]
+SEMAPHORES += ["a" + m for m in MSG] + ["d" + m for m in MSG]
+
+
+def rank_program(g, core, T, topo):
+    me = T.rank_of(core)
+    if me is None:
+        return
+    queues = {"v": g.vector, "s": g.scalar, "p": g.tensor, "g": g, "y": g.sync}
+    csem = {"v": "cv", "s": "cs", "p": "cp", "g": "cg"}
+    count, waited, wr, rd = {}, {q: {} for q in queues}, {}, {}
+
+    def wait(q, toks):
+        for _, sem, val in toks:
+            if waited[q].get(sem, 0) < val:
+                waited[q][sem] = val
+                queues[q].wait_ge(T.sem[sem], val)
+
+    def before(q, reads, writes):
+        toks = []
+        for x in reads:
+            toks += wr.get(x, [])
+            if x in PSUM:
+                toks += [k for k in rd.get(x, []) if k[0] != q]
+        for x in writes:
+            toks += [k for k in wr.get(x, []) if k[0] != q or (q != "p" and x not in PARTS)]
+            toks += [k for k in rd.get(x, []) if k[0] != q]
+        best = {}
+        for k in toks:
+            if k[1] not in best or best[k[1]][2] < k[2]:
+                best[k[1]] = k
+        wait(q, best.values())
+
+    def after(tok, reads, writes):
+        for x in reads:
+            if x not in writes:
+                rd.setdefault(x, [])
+                rd[x] = [k for k in rd[x] if k[1] != tok[1]] + [tok]
+        for x in writes:
+            wr[x] = [tok]
+            rd[x] = []
+
+    def op(q, fn, reads, writes, **kw):
+        before(q, reads, writes)
+        sem = csem[q]
+        fn(**kw).then_inc(T.sem[sem], 1)
+        count[sem] = count.get(sem, 0) + 1
+        after((q, sem, count[sem]), reads, writes)
+
+    def dma(q, sem, pairs, reads, writes):
+        before(q, reads, writes)
+        for out, in_ in pairs:
+            queues[q].dma_start(out, in_).then_inc(T.sem[sem], 16)
+            count[sem] = count.get(sem, 0) + 16
+        after(("dma" + sem, sem, count[sem]), reads, writes)
+
+    def send(msg, dst, out, in_, reads):
+        before("g", reads, [])
+        eng = topo.engines(core, dst)[:8]
+        rid, pid, _ = topo.addr(dst)
+        g.remote_dma(out, in_, T.sem["a" + msg], T.sem["d" + msg], pid, rid, sum(1 << e for e in eng))
+        count["d" + msg] = len(eng)
+        after(("rdma" + msg, "d" + msg, len(eng)), reads, [])
+
+    def arrives(msg, src, buf):
+        n = len(topo.engines(src, core)[:8])
+        count["a" + msg] = n
+        after(("arr" + msg, "a" + msg, n), [], [buf])
+
+    def ts(out, w, in0, r, s1, op0, s2=None, op1=None, cols=()):
+        kw = {"out": out, "in0": in0, "scalar1": s1, "scalar2": s2, "op0": op0}
+        if op1 is not None:
+            kw["op1"] = op1
+        op("v", g.vector.tensor_scalar, list(r) + list(cols), w, **kw)
+
+    def tt(out, w, in0, in1, r, o):
+        op("v", g.vector.tensor_tensor, r, w, out=out, in0=in0, in1=in1, op=o)
+
+    def cp(out, w, in_, r):
+        op("v", g.vector.tensor_copy, r, w, out=out, in_=in_)
+
+    def mm(out, w, lhsT, rhs, r, start, stop):
+        op("p", g.tensor.matmul, r, w, out=out, lhsT=lhsT, rhs=rhs, start=start, stop=stop)
+
+    def act(out, w, in_, r, func, **kw):
+        op("s", g.scalar.activation, r, w, out=out, in_=in_, func=func, **kw)
+
+    def scan(out, w, d0, d1, r, init, o0, o1):
+        op("v", g.vector.tensor_tensor_scan, r, w, out=out, data0=d0, data1=d1, initial=init, op0=o0, op1=o1)
+
+    up, down = T.cores[(me + 1) % N], T.cores[(me - 1) % N]
+
+    dma("s", "ldx", [(T.X[:, 0:WN], T.x[:])], [], ["X"])
+    dma("y", "ldw", [(T.wti[:], T.wt[:])], [], ["wti"])
+    dma("y", "lda", [(T.pai[:], T.pa[:])], [], ["pai"])
+    dma("y", "ldb", [(T.pbi[:], T.pb[:])], [], ["pbi"])
+
+    def iota(name, pattern, base, mult, n):
+        kw = {"out": T[name][:, 0:n], "pattern": pattern, "base": base, "channel_multiplier": mult}
+        if name != "pidx":
+            kw["allow_small_or_imprecise_dtypes"] = True
+        op("g", g.iota, [], [name], **kw)
+
+    iota("pidx", [[0, 1]], 0, 1, 1)
+    iota("col", [[1, 256]], 0, 0, 256)
+    iota("colL", [[0, 32], [1, 16]], 0, 0, 512)
+    iota("colg", [[1, 8], [0, 16]], 0, 0, 128)
+    iota("colJ", [[2, 32], [0, 16]], 1, 0, 512)
+
+    def send_starts(t, dst):
+        act(T["SS%d" % t][:], ["SS%d" % t], T.X[:, t:WN:16], ["X"], AF.Copy)
+        send("S%d" % t, dst, T["SR%d" % t][:], T["SS%d" % t][:], ["SS%d" % t])
+        send("B%d" % t, dst, T["XR%d" % t][:, 0:WN], T.X[:, 0:WN], ["X"])
+
+    send_starts(0, up)
+    arrives("S0", down, "SR0")
+    arrives("B0", down, "XR0")
+    iota("IOTA", [[1, WD]], 0, 0, WD)
+
+    def fill(ap, w, c):
+        before("v", [], [w])
+        g.vector.memset(ap, c).then_inc(T.sem.cv, 1)
+        count["cv"] = count.get("cv", 0) + 1
+        after(("v", "cv", count["cv"]), [], [w])
+
+    fill(T.X[:, WN:WD], "Xd", 0.0)
+    fill(T.OA[:, WN:WD], "OAd", 0.0)
+    fill(T.OB[:, WN:WD], "OBd", 0.0)
+    fill(T.IOTA[:, WD:WD + 8], "IOTAd", -1.0)
+    fill(T.ONE[:], "ONE", 1.0)
+    fill(T.KT[:], "KT", 0.0)
+    fill(T.CK[:], "CK", -15.5 / 128)
+    fill(T.PLf[:], "PLf", 8192.0)
+    ts(T.pmi[:], ["pmi"], T.pidx[:], ["pidx"], 15, OP.bitwise_and)
+    ts(T.pgi[:], ["pgi"], T.pidx[:], ["pidx"], 4, OP.arith_shift_right)
+    cp(T.pidf[:], ["pidf"], T.pidx[:], ["pidx"])
+    cp(T.pmf[:], ["pmf"], T.pmi[:], ["pmi"])
+    cp(T.pgf[:], ["pgf"], T.pgi[:], ["pgi"])
+    ts(T.pg15[:], ["pg15"], T.pgf[:], ["pgf"], 16.0, OP.mult, 15.0, OP.add)
+    for nm, val in (("E8", 8192.0), ("E4n", -4096.0)):
+        ts(T[nm][:], [nm], T.col[:, 0:144], ["col"], T.pg15[:], OP.is_equal, val, OP.mult, cols=["pg15"])
+    ts(T.GS[:], ["GS"], T.col[:, 0:8], ["col"], T.pgf[:], OP.is_equal, cols=["pgf"])
+    for nm, val in (("I16", 1.0), ("IB", 1.0), ("INB", -1.0), ("IBAR", 16777216.0)):
+        ts(T[nm][:], [nm], T.col[:, 0:128], ["col"], T.pidf[:], OP.is_equal, val, OP.mult, cols=["pidf"])
+    ts(T.dl[:], ["dl"], T.colL[:], ["colL"], T.pmf[:], OP.is_equal, cols=["pmf"])
+    cp(T.RH[:], ["RH"], T.dl[:], ["dl"])
+    tt(T.RU[:], ["RU"], T.colJ[:], T.dl[:], ["colJ", "dl"], OP.mult)
+    h0, g1, g3, e1, r1, r2, kv, rv = [T.kc[:, i:i + 1] for i in range(8)]
+    ts(h0, ["h0"], T.pidf[:], ["pidf"], 0.0, OP.is_equal, 0.5, OP.mult)
+    ts(g1, ["g1"], T.pidf[:], ["pidf"], 1.0, OP.is_ge, 2048.0, OP.mult)
+    ts(g3, ["g3"], T.pidf[:], ["pidf"], 3.0, OP.is_ge, -8.0, OP.mult)
+    ts(e1, ["e1"], T.pidf[:], ["pidf"], 1.0, OP.is_equal, -1.0, OP.mult)
+    ts(r1, ["r1"], T.pidf[:], ["pidf"], 1.0, OP.is_ge, -4096.0, OP.mult)
+    ts(r2, ["r2"], T.pidf[:], ["pidf"], 2.0, OP.is_ge, -4096.0, OP.mult)
+    tt(kv, ["kv"], h0, g1, ["h0", "g1"], OP.add)
+    ts(rv, ["rv"], T.pidf[:], ["pidf"], 0.0, OP.is_equal, e1, OP.add, cols=["e1"])
+    tt(kv, ["kv"], kv, g3, ["kv", "g3"], OP.add)
+    ts(T.RK[:], ["RK"], T.ONE[:], ["ONE"], rv, OP.mult, cols=["rv"])
+    ts(T.KC[:], ["KC"], T.ONE[:, 0:128], ["ONE"], kv, OP.mult, cols=["kv"])
+    cp(T.wf[:], ["wf"], T.wti[:], ["wti"])
+    ts(T.wg[:], ["wg"], T.wf[:], ["wf"], 2048.0, OP.is_gt, -4096.0, OP.mult)
+    tt(T.wg[:], ["wg"], T.wg[:], T.wf[:], ["wg", "wf"], OP.add)
+    ts(T.WG[:], ["WG"], T.GS[:], ["GS"], T.wg[:], OP.mult, cols=["wg"])
+    c0 = 16 * NR
+    ts(T.RO[:, c0:512], ["RO"], T.ONE[:, c0:512], ["ONE"], r1, OP.mult, cols=["r1"])
+    ts(T.RO[:, 0:c0], ["RO"], T.ONE[:, 0:c0], ["ONE"], r2, OP.mult, cols=["r2"])
+    ts(T.RZ[:, c0:512], ["RZ"], T.RH[:, c0:512], ["RH"], -4096.0, OP.mult)
+    ts(T.RZ[:, 0:c0], ["RZ"], T.RH[:, 0:c0], ["RH"], 0.0, OP.mult)
+    cp(T.qs[:], ["qs"], T.pai[:], ["pai"])
+    cp(T.t2[:], ["t2"], T.pbi[:], ["pbi"])
+    dma("y", "sta", [(T.oad[:], T.qs[:])], ["qs"], ["oad"])
+    dma("y", "stb", [(T.obd[:], T.t2[:])], ["t2"], ["obd"])
+    dma("y", "roa", [(T.OA[m::16, 0:WN], T.oad[:]) for m in range(16)], ["oad"], ["OA"])
+    dma("y", "rob", [(T.OB[m::16, 0:WN], T.obd[:]) for m in range(16)], ["obd"], ["OB"])
+
+    def late_constants():
+        ts(T.IB8[:], ["IB8"], T.IB[:], ["IB"], 8192.0, OP.mult)
+        ts(T.BO[:], ["BO"], T.colg[:], ["colg"], T.pgf[:], OP.is_equal, 8192.0, OP.mult, cols=["pgf"])
+        ts(T.TRI[:], ["TRI"], T.colL[:, 0:128], ["colL"], T.pmf[:], OP.is_gt, cols=["pmf"])
+        tt(T.TRI[:], ["TRI"], T.TRI[:], T.BO[:], ["TRI", "BO"], OP.mult)
+        ts(T.DM[:], ["DM"], T.colL[:, 0:256], ["colL"], T.pmf[:], OP.is_equal, cols=["pmf"])
+        ts(T.OFFB[:], ["OFFB"], T.colL[:, 0:256], ["colL"], T.pmf[:], OP.not_equal, 1073741824.0, OP.mult, cols=["pmf"])
+        ts(T.OFFB[:], ["OFFB"], T.OFFB[:], ["OFFB"], 8192.0, OP.add)
+        ts(T.SEG[:], ["SEG"], T.colL[:, 0:256], ["colL"], 0.0, OP.not_equal)
+        ts(T.SEGB[:], ["SEGB"], T.colL[:, 0:256], ["colL"], 0.0, OP.is_equal, 2.0e10, OP.mult)
+        ts(T.SEGB[:], ["SEGB"], T.SEGB[:], ["SEGB"], -1.0e10, OP.add)
+        ts(T.DMD[:], ["DMD"], T.col[:], ["col"], 4097.0, OP.add)
+        tt(T.DMD[:], ["DMD"], T.DMD[:], T.DM[:], ["DMD", "DM"], OP.mult)
+        ts(T.vr0[:], ["vr0"], T.col[:], ["col"], 16.0, OP.mult)
+        ts(T.vr1[:], ["vr1"], T.col[:], ["col"], 16.0, OP.mult, 1.0, OP.add)
+        ts(T.DC[:], ["DC"], T.col[:, 0:16], ["col"], 16.0, OP.mult, T.pmf[:], OP.add, cols=["pmf"])
+        ts(T.DC[:], ["DC"], T.DC[:], ["DC"], 4096.0, OP.add)
+
+    late_constants()
+
+    def run_flags(t, near, dst):
+        ts(T.pm[:], ["pm"], T[near][:, t:WN:16], [near], 0.0, OP.is_ge)
+        tt(T.pm[:], ["pm"], T.pm[:], T.DMD[:], ["pm", "DMD"], OP.mult)
+        scan(T.ps[:], ["ps"], T.SEG[:], T.pm[:], ["SEG", "pm"], 0.0, OP.mult, OP.add)
+        ts(T["DS%d" % t][:], ["DS%d" % t], T.ps[:, 15:256:16], ["ps"], -1.0, OP.add)
+        send("D%d" % t, dst, T["DR%d" % t][:], T["DS%d" % t][:], ["DS%d" % t])
+
+    def near_update(t, near):
+        tab = T[near][:, t:WN:16]
+        tt(tab, [near], T.IOTA[:, 0:WD + 8].indirect(T["PR%d" % t][:]), tab, ["IOTA", "IOTAd", "PR%d" % t, near], OP.max)
+
+    def search(t, d, z, zr, hooks):
+        for l in range(16):
+            mm(T.ph[0:16, l:128:16], ["ph"], z[:, l:256:16], T.WG[:], ["WG", zr], True, True)
+        for l in range(16):
+            mm(T.pq[0:16, l:128:16], ["pq"], z[:, l:256:16], T.GS[:], ["GS", zr], True, True)
+
+        def raw1(a, b, bank):
+            mm(T[bank][:, a:b], [bank], T.KC[0:4, :], T.RK[0:4, a:b], ["KC", "RK"], True, False)
+            mm(T[bank][:, a:b], [bank], T.KT[0:1, :], T.ONE[0:1, a:b], ["KT", "ONE"], False, False)
+
+        def raw2(a, b, bank):
+            mm(T[bank][:, a:b], [bank], T.UT[0:16, :], T.RU[0:16, a:b], ["UT", "RU"], False, False)
+
+        def raw3(a, b, bank, stop):
+            mm(T[bank][:, a:b], [bank], T.HT[0:16, :], T.RH[0:16, a:b], ["HT", "RH"], False, stop)
+
+        (a0, b0, s0, e0), (a1, b1, s1, e1) = PORTIONS
+        raw1(a0, b0, s0)
+        raw1(a1, b1, s1)
+        raw1(a0, b0, e0)
+        cp(T.ui[0:16, :], ["ui"], T.ph[0:16, 0:128], ["ph"])
+        ts(T.u[0:16, :], ["u"], T.ui[0:16, :], ["ui"], 4095, OP.bitwise_and)
+        tt(T.sq[0:16, :], ["sq"], T.u[0:16, :], T.u[0:16, :], ["u"], OP.mult)
+        ts(T.UT[0:16, :], ["UT"], T.u[0:16, :], ["u"], -2048.0, OP.add)
+        ts(T.hm[0:16, :], ["hm"], T.sq[0:16, :], ["sq"], 5, OP.arith_shift_right, 4095, OP.bitwise_and)
+        ts(T.HT[0:16, :], ["HT"], T.hm[0:16, :], ["hm"], -2048.0, OP.add)
+        raw2(a0, b0, s0)
+        raw2(a1, b1, s1)
+        raw2(a0, b0, e0)
+        raw3(a0, b0, s0, True)
+        raw3(a0, b0, e0, False)
+        raw3(a1, b1, s1, True)
+
+        def near(i):
+            a, b, bank, rest = PORTIONS[i]
+            ts(T.RR[:, a:b], ["RR%d" % i], T[bank][:, a:b], [bank], 51539607552.0, OP.add, -51539607552.0, OP.add)
+            mm(T[rest][:, a:b], [rest], T.INB[:], T.RR[:, a:b], ["INB", "RR%d" % i], False, True)
+
+        def lists(i):
+            a, b, _, rest = PORTIONS[i]
+            ts(T.LST[:, a:b], ["LST%d" % i], T[rest][:, a:b], [rest], 2047.5, OP.add)
+
+        near(0)
+        raw1(a1, b1, e1)
+        raw2(a1, b1, e1)
+        raw3(a1, b1, e1, False)
+        ts(T.ZT[0:16, :], ["ZT"], T.pq[0:16, 0:128], ["pq"], -2048.0, OP.add)
+        for i in range(4):
+            mm(T.pz[:, 256 * i:256 * i + 256], ["pz"], T.IB[:], z[:], ["IB", zr], True, True)
+        lists(0)
+        near(1)
+        win = T.X[:, 0:WN]
+        for pieces in SCH:
+            for j0, j1 in pieces:
+                if 16 * j1 <= PORTIONS[0][1]:
+                    act(T.A[:, 256 * j0:256 * j1], ["A%d" % j0], win.indirect(T.LST[:, 16 * j0:16 * j1]), ["X", "LST0"], AF.Copy)
+        mm(T.pk[:], ["pk"], T.KC[0:4, :], T.RO[0:4, :], ["KC", "RO"], True, False)
+        mm(T.pk[:], ["pk"], T.ZT[0:16, :], T.RZ[0:16, :], ["ZT", "RZ"], False, False)
+        if d > 0:
+            mm(T.pc[:], ["pc"], T.LT[0:16, :], T.RH[0:16, :], ["LT", "RH"], True, True)
+
+        def sums(src, sel, pieces):
+            j0, j1 = pieces[0][0], pieces[-1][1]
+            for l in range(16):
+                mm(T.pk[:, 16 * j0:16 * j1], ["pk"], T[sel][:, 15 - l:143 - l], T[src][:, 256 * j0 + l:256 * j1:16], [sel] + ["%s%d" % (src, a) for a, _ in pieces], False, False)
+
+        if NR:
+            for j in range(NR):
+                if j == NR // 2:
+                    lists(1)
+                    for pieces in SCH:
+                        for j0, j1 in pieces:
+                            if 16 * j1 > PORTIONS[0][1]:
+                                act(T.A[:, 256 * j0:256 * j1], ["A%d" % j0], win.indirect(T.LST[:, 16 * j0:16 * j1]), ["X", "LST1"], AF.Copy)
+                tt(T.A[:, 256 * j:256 * j + 256], ["A0"], win.indirect(T.LST[:, 16 * j:16 * j + 16]), z[:], ["X", "LST0", zr], OP.subtract)
+            ts(T.M[:, 0:256 * NR], ["M0"], T.A[:, 0:256 * NR], ["A0"], 0.0, OP.max)
+        sums("A", "E4n", SCH[0])
+        if NR:
+            sums("A", "E4n", [(0, NR)])
+            sums("M", "E8", [(0, NR)])
+        ts(T.c16[:], ["c16"], T.LST[:], ["LST0", "LST1"], -2048.0, OP.add)
+        if d > 0:
+            tt(T.bar[:], ["bar"], T.c16[:], T.pc[:], ["c16", "pc"], OP.is_equal)
+        else:
+            ts(T.sm[:], ["sm"], z[:], [zr], -0.5, OP.add)
+        for k, pieces in enumerate(SCH):
+            for j0, j1 in pieces:
+                tt(T.M[:, 256 * j0:256 * j1], ["M%d" % j0], T.A[:, 256 * j0:256 * j1], T.pz[:, 0:256 * (j1 - j0)], ["A%d" % j0, "pz"], OP.max)
+            if k == 0 and d > 0:
+                mm(T.pk[:], ["pk"], T.IBAR[:], T.bar[:], ["IBAR", "bar"], False, False)
+            if k < EARLY:
+                sums("A", "E4n", SCH[k + 1])
+            sums("M", "E8", pieces)
+            if k == len(SCH) - 2:
+                mm(T.pk[:, 0:16 * SCH[-1][0][0]], ["pk"], T.I16[:], T.c16[:, 0:16 * SCH[-1][0][0]], ["I16", "c16"], False, False)
+            if EARLY <= k < len(SCH) - 1:
+                sums("A", "E4n", SCH[k + 1])
+            if k == 4:
+                for h in hooks:
+                    h()
+        mm(T.pk[:, 16 * SCH[-1][0][0]:512], ["pk"], T.I16[:], T.c16[:, 16 * SCH[-1][0][0]:512], ["I16", "c16"], False, True)
+        for L in range(16):
+            op("v", g.vector.tensor_reduce, ["pk"], ["ym"], out=T.ym[:, L:L + 1], in_=T.pk[:, L:512:16], axis=AxisListType.X, op=OP.min)
+
+    def pair(t, d, far, kd):
+        xn, l2 = "XN%d" % d, "L2%d" % d
+        dr = "DR%d" % t
+        ts(T.yi[:], ["yi"], T.ym[:], ["ym"], 2048.0, OP.add)
+        ts(T.y[:], ["y"], T.yi[:], ["yi"], 4095, OP.bitwise_and)
+        tt(T.yc[:], ["yc"], T.y[:], T[dr][:], ["y", dr], OP.max)
+        cp(T.yl[:], ["yl"], T.yc[:], ["yc"])
+        ow = T[far][:, 0:WD]
+        act(T.XG[:], ["XG"], T.X[:, 0:WD].indirect(T.yl[:]), ["X", "Xd", "yl"], AF.Copy)
+        cp(T.Yr[:], ["Yr"], T.IOTA[:, 0:WD].indirect(T.yl[:]), ["IOTA", "yl"])
+        mm(T.pq[:, 0:256], ["pq"], T.IB[:], T.OFFB[:], ["IB", "OFFB"], True, False)
+        mm(T.ph[:, 0:256], ["ph"], T.I16[:], T.sm[:], ["I16", "sm"], True, False)
+        mm(T.ph[:, 0:256], ["ph"], T.IB[:], T.XG[:], ["IB", "XG"], False, True)
+        act(T.t2[:], ["t2"], T.ph[:, 0:256], ["ph"], AF.Copy, bias=8388608.0, scale=0.5)
+        act(T[xn][:], [xn], T.t2[:], ["t2"], AF.Copy, bias=-8388608.0)
+        act(T.Or[:], ["Or"], ow.indirect(T.yl[:]), [far, far + "d", "yl"], AF.Copy)
+        base = 0
+        for L in range(16):
+            n = 256 - 16 * L
+            e = "EQ%d" % L
+            ts(T.EQ[:, base:base + n], [e], T.Yr[:, 16 * L:256], ["Yr"], T.yc[:, L:L + 1], OP.is_equal, cols=["yc"])
+            if n > 16:
+                mm(T.pq[:, 16 * L + 16:256], ["pq"], T.BO[:], T.EQ[:, base + 16:base + n], ["BO", e], False, False)
+            if L == 15:
+                mm(T.pq[:, 0:256], ["pq"], T.IB8[:], T.Or[:], ["IB8", "Or"], False, False)
+            mm(T.pq[:, 16 * L:16 * L + 16], ["pq"], T.TRI[:], T.EQ[:, base:base + 16], ["TRI", e], False, L == 15)
+            base += n
+        tell = d < STEPS - 1
+        dst = up if t == 0 else down
+        if tell:
+            send("X%d%d" % (t, d), dst, T["XI%d%d" % (t, d)][:], T[xn][:], [xn])
+        scan(T.qs[:], ["qs"], T.SEGB[:], T.pq[:, 0:256], ["SEGB", "pq"], 1.0e10, OP.max, OP.min)
+        tt(T.nw[:], ["nw"], T.qs[:, 15:256:16], T.DC[:], ["qs", "DC"], OP.min)
+        tt(T.lf[:], ["lf"], T.yc[:], T.nw[:], ["yc", "nw"], OP.max)
+        cp(T[l2][:], [l2], T.lf[:], ["lf"])
+        if tell:
+            send("L%d%d" % (t, d), dst, T["LI%d%d" % (t, d)][:], T[l2][:], [l2])
+
+        def home():
+            tt(T.PLf[:], ["PLf"], T.PLf[:], T.lf[:], ["PLf", "lf"], OP.min)
+            if d == STEPS - 1:
+                ts(T.wd[:], ["wd"], T.PLf[:], ["PLf"], float(WN), OP.is_ge, 8192.0, OP.mult)
+                tt(T.wd[:], ["wd"], T.wd[:], T.PLf[:], ["wd", "PLf"], OP.max)
+                ts(T["PS%d" % t][:], ["PS%d" % t], T.wd[:], ["wd"], float(WD), OP.min)
+                fill(T.PLf[:], "PLf", 8192.0)
+
+        def put_records():
+            cp(T.X[:, 0:WD].indirect(T[l2][:]), ["X", "Xd"], T[xn][:], [xn, l2])
+
+        def put_far():
+            cp(ow.indirect(T[l2][:]), [far, far + "d"], T["vr%d" % t][:], ["vr%d" % t, l2])
+
+        def small():
+            if tell:
+                ts(T.TB[:], ["TB"], T.y[:], ["y"], -2048.0, OP.add)
+                mm(T.pc[0:16, 0:128], ["pc"], T.TB[:], T.I16[:], ["TB", "I16"], True, True)
+                tt(T.wd[:], ["wd"], T.DC[:], T.nw[:], ["DC", "nw"], OP.subtract)
+                cp(T.LT[0:16, :], ["LT"], T.pc[0:16, 0:128], ["pc"])
+                tt(T[dr][:], [dr], T[dr][:], T.wd[:], [dr, "wd"], OP.max)
+
+        def kappa():
+            act(T.wb[:], ["wb"], T.qs[:, 15:256:16], ["qs"], AF.Relu, bias=1.0, scale=-1.0)
+            mm(T.pt[:, 0:1], ["pt"], T.ONE[:, 0:128], T.CK[:, 0:1], ["ONE", "CK"], True, False)
+            for L in range(16):
+                mm(T.pt[:, 0:1], ["pt"], T.ONE[:, 0:128], T.wb[:, L:L + 1], ["ONE", "wb"], False, L == 15)
+            act(T.k1[:], ["k1"], T.pt[:, 0:1], ["pt"], AF.Identity, bias=402653184.0)
+            act(T.kr[:], ["kr"], T.k1[:], ["k1"], AF.Copy, bias=402653184.0, scale=-1.0)
+            act(T.kf[:], ["kf"], T.pt[:, 0:1], ["pt", "kr"], AF.Identity, bias=T.kr[:])
+            act(T.KT[0:1, :], ["KT"], T.ONE[0:1, 0:128], ["ONE", "kf"], AF.Identity, bias=T.kf[0:1, :], scale=float(kd) + 15.5)
+
+        return home, put_records, put_far, small, kappa
+
+    def next_z(t, d):
+        src = down if t == 0 else up
+        xr = "XR%d" % t
+        arrives("X%d%d" % (t, d), src, "XI%d%d" % (t, d))
+        arrives("L%d%d" % (t, d), src, "LI%d%d" % (t, d))
+        cp(T[xr][:, 0:WD].indirect(T["LI%d%d" % (t, d)][:]), [xr], T["XI%d%d" % (t, d)][:], [xr, "XI%d%d" % (t, d), "LI%d%d" % (t, d)])
+        act(T.zb[:], ["zb"], T[xr][:, 0:WN].indirect(T.pl16[:]), [xr, "pl16"], AF.Copy)
+
+    for t in range(2):
+        far = "OB" if t == 0 else "OA"
+        near = "OA" if t == 0 else "OB"
+        for d in range(STEPS):
+            hooks = []
+            if (t, d) == (0, 0):
+                hooks.append(lambda: run_flags(0, "OA", up))
+                hooks.append(lambda: arrives("D0", down, "DR0"))
+            if (t, d) == (1, 0):
+                hooks.append(lambda: near_update(0, "OA"))
+            zn = "SR%d" % t if d == 0 else "zb"
+            search(t, d, T[zn], zn, hooks)
+            home, put_records, put_far, small, kappa = pair(t, d, far, 97 * (d + 1) if d < STEPS - 1 else 0)
+            if d < STEPS - 1:
+                put_far()
+                tt(T.pm[:], ["pm"], T[far][:, 0:WD].indirect(T.yl[:]), T.DM[:], [far, far + "d", "yl", "DM"], OP.mult)
+                scan(T.ps[:], ["ps"], T.SEG[:], T.pm[:], ["SEG", "pm"], 0.0, OP.mult, OP.add)
+                cp(T.pl16[:], ["pl16"], T.ps[:, 15:256:16], ["ps"])
+                kappa()
+                small()
+                home()
+                next_z(t, d)
+                put_records()
+            elif t == 0:
+                put_records()
+                send_starts(1, down)
+                kappa()
+                put_far()
+                home()
+                send("P0", down, T.PR0[:], T.PS0[:], ["PS0"])
+                run_flags(1, "OB", down)
+                arrives("S1", up, "SR1")
+                arrives("B1", up, "XR1")
+                arrives("D1", up, "DR1")
+                arrives("P0", up, "PR0")
+            else:
+                put_records()
+                dma("y", "outx", [(T.yx[:], T.X[:, 0:WN])], ["X"], [])
+                home()
+                send("P1", up, T.PR1[:], T.PS1[:], ["PS1"])
+                arrives("P1", down, "PR1")
+                put_far()
+                dma("y", "outa", [(T.ya[:], T.OA[0:128:16, 0:WN])], ["OA"], [])
+                near_update(1, "OB")
+                dma("y", "outb", [(T.yb[:], T.OB[0:128:16, 0:WN])], ["OB"], [])
+    for sem in sorted(count):
+        wait("g", [("", sem, count[sem])])

@@ -4,52 +4,64 @@ N = 5
 WN = 4096
 WD = 4352
 STEPS = 3
-NR = 4
-SCH = [[(4, 8)], [(8, 12)], [(12, 16)], [(16, 20)], [(20, 24)], [(24, 28)], [(28, 30), (30, 32)]]
-EARLY = 3
-PORTIONS = ((0, 128, "pc", "pt"), (128, 512, "pla", "ph"))
+CHUNKS = ((8, (("s", 8), ("c", 8), ("s", 8), ("c", 8))),
+          (8, (("s", 8), ("s", 8), ("s", 8), ("s", 4), ("s", 4))))
+PORT = ((0, 64, "pr", "pk0"), (64, 192, "pk1", "ph"), (192, 512, "z1a", "z1b"))
+ORDER = """hash Z0 <x1 u Y0 W0 E0 h0 N0 W1 T0 h1 L0 G0 E1 h2 N1 T1 W2 L1 G2 E2 V1.0 N2 T2 O0 last A0 V1.1 L2 R1 G4 X0 M0 A2
+           V3.0 V3.1 M1 Z1 R3 G5 c16 X2 M2 bar M3 B0 C0 O1 B1 A4 extra X4 H0 G6 F0 P0 A5 M4 X5 Q0 G7 G8 U0 f0
+           A6 M5 X6 X7 A7.8 M6 X8 M7.8 C1 P1"""
+NEXT = "r0 H1 F1 Q1 U1 count f1 fp kappa tb x0 lt ahead won pl dead r1 z"
+END = ("x0 H1 F1 Q1 U1 x1 starts count f1 kappa ahead won home flags whole",
+       "x0 H1 F1 Q1 U1 won home x1 outx outa outb")
+WIDE = 192
+ZS = 8
+ZP = 512
+FRAC = 1.0 / 16384
+NC = len(CHUNKS)
+START = [sum(c[0] for c in CHUNKS[:k]) for k in range(NC + 1)]
+MBASE = [sum(16 * c[0] + 8 * ((c[0] + 7) // 8) for c in CHUNKS[:k]) for k in range(NC + 1)]
 
 SCRATCH = {}
 for _n, _c, _d in (
-        ("X", WD, "bfloat16"), ("XR0", WD, "bfloat16"), ("XR1", WD, "bfloat16"), ("OA", WD, "float32"), ("OB", WD, "float32"),
-        ("IOTA", WD + 8, "float32"), ("A", 8192, "bfloat16"), ("M", 8192, "bfloat16"), ("zb", 256, "bfloat16"),
+        ("X", WD, "bfloat16"), ("XR0", WD, "bfloat16"), ("XR1", WD, "bfloat16"), ("FA", WD, "float32"), ("FB", WD, "float32"),
+        ("PA", WD, "float32"), ("PB", WN, "float32"), ("IO", WD + 8, "float32"), ("A", 8192, "bfloat16"), ("M", 8192, "bfloat16"),
+        ("zb", 256, "bfloat16"), ("zp", 1024, "bfloat16"),
         ("pai", 256, "int32"), ("pbi", 256, "int32"), ("wti", 1, "int32"), ("wf", 1, "float32"), ("wg", 1, "float32"),
-        ("pidx", 1, "int32"), ("pmi", 1, "int32"), ("pgi", 1, "int32"), ("pidf", 1, "float32"), ("pmf", 1, "float32"), ("pgf", 1, "float32"), ("pg15", 1, "float32"),
-        ("kc", 8, "float32"),
-        ("col", 256, "float32"), ("colL", 512, "float32"), ("colJ", 512, "float32"), ("colg", 128, "float32"), ("dl", 512, "float32"),
-        ("E8", 144, "bfloat16"), ("E4n", 144, "bfloat16"), ("WG", 8, "float16"), ("GS", 8, "bfloat16"), ("CK", 2, "bfloat16"),
-        ("I16", 128, "float16"), ("IB", 128, "bfloat16"), ("IB8", 128, "bfloat16"), ("INB", 128, "bfloat16"), ("IBAR", 128, "bfloat16"), ("BO", 128, "bfloat16"), ("TRI", 128, "bfloat16"), ("ONE", 512, "bfloat16"),
-        ("DM", 256, "float32"), ("DMD", 256, "float32"), ("OFFB", 256, "bfloat16"), ("SEG", 256, "float32"), ("SEGB", 256, "float32"),
-        ("RH", 512, "float16"), ("RU", 512, "float16"), ("RZ", 512, "float16"), ("RK", 512, "bfloat16"), ("RO", 512, "bfloat16"), ("KC", 128, "bfloat16"), ("KT", 128, "bfloat16"), ("vr0", 256, "float32"), ("vr1", 256, "float32"), ("DC", 16, "float32"),
-        ("ui", 128, "int32"), ("u", 128, "int32"), ("sq", 128, "int32"), ("hm", 128, "int32"), ("UT", 128, "float16"), ("HT", 128, "float16"), ("ZT", 128, "float16"), ("LT", 128, "float16"), ("TB", 16, "float16"),
+        ("pidx", 1, "int32"), ("pmi", 1, "int32"), ("pgi", 1, "int32"), ("poi", 1, "int32"), ("kc", 24, "float32"),
+        ("col", 512, "float32"), ("colL", 512, "bfloat16"), ("colJ", 512, "bfloat16"), ("colg", 128, "bfloat16"), ("coll", 256, "bfloat16"),
+        ("SEL", 2048, "bfloat16"), ("hi", 256, "bfloat16"), ("lo", 256, "bfloat16"), ("FR", 512, "float16"), ("cf", 256, "float32"), ("cp0", 256, "float32"), ("cp1", 256, "float32"),
+        ("TD", 32, "float32"), ("TE", 32, "float32"), ("colb", 144, "bfloat16"),
+        ("E8", 144, "bfloat16"), ("E4n", 144, "bfloat16"), ("E4", 144, "bfloat16"), ("WG", 8, "float16"), ("GS", 8, "bfloat16"), ("CK", 2, "float32"),
+        ("I16", 128, "float16"), ("IB", 128, "bfloat16"), ("I32", 128, "float32"), ("INB", 128, "bfloat16"), ("IBAR", 128, "bfloat16"),
+        ("BO", 128, "bfloat16"), ("TRI", 128, "bfloat16"), ("ONE", 512, "bfloat16"), ("MH", 144, "bfloat16"),
+        ("OFFB", 256, "bfloat16"), ("SEG", 256, "float32"), ("DX", 256, "bfloat16"), ("DY", 256, "bfloat16"),
+        ("RH", 512, "bfloat16"), ("RQ", 512, "float32"), ("RU", 512, "bfloat16"), ("RZ", 512, "bfloat16"), ("RO", 512, "bfloat16"), ("KT", 128, "bfloat16"),
+        ("vr0", 256, "float32"), ("vs0", 256, "float32"), ("vs1", 256, "float32"),
+        ("ri", 128, "int32"), ("hm", 128, "int32"), ("HT", 128, "float16"), ("UF", 128, "float32"), ("UZ", 128, "float16"), ("SQ", 128, "float32"), ("LT", 128, "float16"), ("TB", 16, "float16"),
         ("RR", 512, "bfloat16"), ("LST", 512, "uint16"), ("c16", 512, "float16"), ("bar", 512, "bfloat16"),
-        ("ym", 16, "float32"), ("yi", 16, "int32"), ("y", 16, "int32"), ("yc", 16, "float32"), ("yl", 16, "uint16"), ("Yr", 256, "uint16"), ("Or", 256, "bfloat16"),
-        ("XG", 256, "bfloat16"), ("sm", 256, "float16"), ("t2", 256, "float32"), ("qs", 256, "float32"), ("nw", 16, "float32"), ("EQ", 2176, "bfloat16"),
-        ("lf", 16, "float32"), ("pm", 256, "float32"), ("ps", 256, "float32"), ("pl16", 16, "uint16"), ("PLf", 16, "float32"), ("wb", 16, "bfloat16"), ("wd", 16, "float32"),
-        ("k1", 1, "float32"), ("kr", 1, "float32"), ("kf", 1, "float32")):
+        ("ym", 16, "int32"), ("y", 16, "int32"), ("yc", 16, "float32"), ("yl", 16, "uint16"), ("FG", 256, "float32"), ("FP", 256, "float32"),
+        ("XG", 256, "bfloat16"), ("qs", 256, "float32"), ("ps", 256, "float32"), ("EQ", 2176, "bfloat16"),
+        ("pl16", 16, "uint16"), ("DD", 16, "bfloat16"), ("PL", 16, "float32"), ("PLl", 16, "uint16"), ("wb", 16, "float32"),
+        ("k0", 1, "float32"), ("k1", 1, "float32"), ("kr", 1, "float32"), ("kf", 1, "float32")):
     SCRATCH[_n] = ("sbuf", [128, _c], _d)
 for _t in range(2):
     for _n, _c, _d in (("SS", 256, "bfloat16"), ("SR", 256, "bfloat16"), ("DS", 16, "float32"), ("DR", 16, "float32"), ("PS", 16, "uint16"), ("PR", 16, "uint16")):
         SCRATCH["%s%d" % (_n, _t)] = ("sbuf", [128, _c], _d)
     for _s in range(STEPS):
-        SCRATCH["XN%d" % _s] = ("sbuf", [128, 256], "bfloat16")
-        SCRATCH["L2%d" % _s] = ("sbuf", [128, 16], "uint16")
+        SCRATCH["MO%d" % _s] = ("sbuf", [128, MBASE[NC]], "uint16")
         if _s < STEPS - 1:
-            SCRATCH["XI%d%d" % (_t, _s)] = ("sbuf", [128, 256], "bfloat16")
-            SCRATCH["LI%d%d" % (_t, _s)] = ("sbuf", [128, 16], "uint16")
-SCRATCH["oad"] = ("dram", [8, WN], "float32")
-SCRATCH["obd"] = ("dram", [8, WN], "float32")
-for _n, _c in (("pz", 1024), ("ph", 512), ("pt", 512), ("pc", 512), ("pla", 512), ("pk", 512), ("pq", 512)):
-    SCRATCH[_n] = ("psum", [128, _c], "float32")
-PARTS = ("ym", "RO", "RZ", "A0")
-PSUM = ("pz", "ph", "pt", "pc", "pla", "pk", "pq")
+            SCRATCH["MI%d%d" % (_t, _s)] = ("sbuf", [128, MBASE[NC]], "uint16")
+SCRATCH["fad"] = ("dram", [8, WN], "float32")
+PSUM = ("z0a", "z0b", "z1a", "z1b", "pk0", "pk1", "ph", "pr")
+SCRATCH["acc"] = ("psum", [128, 512 * len(PSUM)], "float32")
+PARTS = tuple("SEL%d" % _i for _i in range(8)) + ("RO", "RZ", "MH", "colL", "colJ", "FB", "TD", "IO")
 
 MSG = []
 for _t in range(2):
     MSG += ["S%d" % _t, "B%d" % _t, "D%d" % _t, "P%d" % _t]
     for _s in range(STEPS - 1):
-        MSG += ["X%d%d" % (_t, _s), "L%d%d" % (_t, _s)]
-SEMAPHORES = ["cv", "cs", "cp", "cg", "ldx", "ldw", "lda", "ldb", "sta", "stb", "roa", "rob", "outx", "outa", "outb"]
+        MSG += ["M%d%d%d" % (_t, _s, _k) for _k in range(NC)]
+SEMAPHORES = ["cv", "cs", "cp", "cg", "ldx", "ldw", "lda", "ldb", "sta", "roa", "rob", "ga", "gb", "ha", "hb", "outx", "outa", "outb"]
 SEMAPHORES += ["a" + m for m in MSG] + ["d" + m for m in MSG]
 
 
@@ -75,7 +87,7 @@ def rank_program(g, core, T, topo):
                 toks += [k for k in rd.get(x, []) if k[0] != q]
         for x in writes:
             toks += [k for k in wr.get(x, []) if k[0] != q or (q != "p" and x not in PARTS)]
-            toks += [k for k in rd.get(x, []) if k[0] != q]
+            toks += [k for k in rd.get(x, []) if k[0] != q or (q != "p" and x not in PARTS)]
         best = {}
         for k in toks:
             if k[1] not in best or best[k[1]][2] < k[2]:
@@ -118,11 +130,11 @@ def rank_program(g, core, T, topo):
         count["a" + msg] = n
         after(("arr" + msg, "a" + msg, n), [], [buf])
 
-    def ts(out, w, in0, r, s1, op0, s2=None, op1=None, cols=()):
+    def ts(out, w, in0, r, s1, op0, s2=None, op1=None):
         kw = {"out": out, "in0": in0, "scalar1": s1, "scalar2": s2, "op0": op0}
         if op1 is not None:
             kw["op1"] = op1
-        op("v", g.vector.tensor_scalar, list(r) + list(cols), w, **kw)
+        op("v", g.vector.tensor_scalar, r, w, **kw)
 
     def tt(out, w, in0, in1, r, o):
         op("v", g.vector.tensor_tensor, r, w, out=out, in0=in0, in1=in1, op=o)
@@ -139,350 +151,509 @@ def rank_program(g, core, T, topo):
     def scan(out, w, d0, d1, r, init, o0, o1):
         op("v", g.vector.tensor_tensor_scan, r, w, out=out, data0=d0, data1=d1, initial=init, op0=o0, op1=o1)
 
+    def fill(ap, w, c, over=()):
+        before("v", over, [w])
+        g.vector.memset(ap, c).then_inc(T.sem.cv, 1)
+        count["cv"] = count.get("cv", 0) + 1
+        after(("v", "cv", count["cv"]), over, [w])
+
+    def iota(out, w, pattern, base, mult=0, whole=False):
+        kw = {"out": out, "pattern": pattern, "base": base, "channel_multiplier": mult}
+        if not whole:
+            kw["allow_small_or_imprecise_dtypes"] = True
+        op("g", g.iota, [], [w], **kw)
+
+    def ps(bank, a, b, step=1, p0=0, p1=128):
+        o = 512 * PSUM.index(bank)
+        return T.acc[p0:p1, o + a:o + b:step]
+
+    def zbanks(k, n=1024):
+        return ["z%d%s" % (k % 2, x) for x in "ab"[:(n + 511) // 512]]
+
     up, down = T.cores[(me + 1) % N], T.cores[(me - 1) % N]
 
+    pieces = []
+    for k, (nl, parts) in enumerate(CHUNKS):
+        c = 32 * START[k]
+        for eng, nj in parts:
+            pieces.append((k, eng, c, c + nj * nl))
+            c += nj * nl
+    runs = []
+    for _, eng, c0, c1 in pieces:
+        if runs and runs[-1][0] == eng:
+            runs[-1][2] = c1
+        else:
+            runs.append([eng, c0, c1])
+
+    def lst(c0, c1, name="LST"):
+        return ["%s%d" % (name, i) for i, p in enumerate(PORT) if p[0] < c1 and c0 < p[1]]
+
+    dma("s", "lda", [(T.pai[:], T.pa[:])], [], ["pai"])
+    dma("y", "ldb", [(T.pbi[:], T.pb[:])], [], ["pbi"])
     dma("s", "ldx", [(T.X[:, 0:WN], T.x[:])], [], ["X"])
     dma("y", "ldw", [(T.wti[:], T.wt[:])], [], ["wti"])
-    dma("y", "lda", [(T.pai[:], T.pa[:])], [], ["pai"])
-    dma("y", "ldb", [(T.pbi[:], T.pb[:])], [], ["pbi"])
 
-    def iota(name, pattern, base, mult, n):
-        kw = {"out": T[name][:, 0:n], "pattern": pattern, "base": base, "channel_multiplier": mult}
-        if name != "pidx":
-            kw["allow_small_or_imprecise_dtypes"] = True
-        op("g", g.iota, [], [name], **kw)
+    iota(T.pidx[:], "pidx", [[0, 1]], 0, 1, True)
+    iota(T.colg[:], "colg", [[16, 8], [0, 16]], 0)
+    iota(T.col[:], "col", [[1, 512]], 0)
+    for k, (nl, _) in enumerate(CHUNKS):
+        iota(T.colL[:, 32 * START[k]:32 * START[k + 1]], "colL", [[0, 32], [1, nl]], START[k])
+    pid, pm, pg16, pg, pg15, ev, od, p32, pf, up20, dn20, nd20, pm1, dc, one, r16, r17, rs, rv = [T.kc[:, i:i + 1] for i in range(19)]
+    fill(T.ONE[:], "ONE", 1.0)
+    fill(T.MH[:, 128:144], "MH", 0.0)
+    fill(T.MH[:, 0:128], "MH", -0.5)
+    ts(T.pmi[:], ["pmi"], T.pidx[:], ["pidx"], 15, OP.bitwise_and)
+    ts(T.poi[:], ["poi"], T.pidx[:], ["pidx"], 16, OP.bitwise_and)
+    ts(T.pgi[:], ["pgi"], T.pidx[:], ["pidx"], 4, OP.arith_shift_right)
+    cp(pid, ["pid"], T.pidx[:], ["pidx"])
+    cp(pm, ["pm"], T.pmi[:], ["pmi"])
+    cp(pg, ["pg"], T.pgi[:], ["pgi"])
+    ts(od, ["od"], T.poi[:], ["poi"], -1.0 / 16, OP.mult)
+    ts(ev, ["ev"], T.poi[:], ["poi"], 1.0 / 16, OP.mult, -1.0, OP.add)
+    def selectors(a, b):
+        for m in range(a, b):
+            ts(T.SEL[:, 128 * m:128 * m + 128], ["SEL%d" % (m // 2)], T.colg[:], ["colg", "pid"], float(m), OP.add, pid, OP.is_equal)
 
-    iota("pidx", [[0, 1]], 0, 1, 1)
-    iota("col", [[1, 256]], 0, 0, 256)
-    iota("colL", [[0, 32], [1, 16]], 0, 0, 512)
-    iota("colg", [[1, 8], [0, 16]], 0, 0, 128)
-    iota("colJ", [[2, 32], [0, 16]], 1, 0, 512)
+    selectors(0, 4)
+    ts(T.FR[0:1, :], ["FR"], T.col[0:1, :], ["col"], FRAC, OP.mult)
+    act(T.FB[:, WN:WD], ["FBd"], T.ONE[:, 0:256], ["ONE"], AF.Silu, scale=2.0)
+    ts(T.hi[:], ["hi"], T.pbi[:], ["pbi"], 805306368.0, OP.add, -805306368.0, OP.add)
+    ts(pg16, ["pg16"], pg, ["pg"], 16.0, OP.mult)
+    tt(T.lo[:], ["lo"], T.pbi[:], T.hi[:], ["pbi", "hi"], OP.subtract)
+    selectors(4, 8)
+
+    ts(T.TD[:, 0:16], ["TD"], T.pai[:, 0:256:16], ["pai", "ev"], 0.5, OP.add, ev, OP.mult)
+    ts(T.TD[:, 16:32], ["TD"], T.pai[:, 0:256:16], ["pai", "od"], 0.5, OP.add, od, OP.mult)
+    ts(pg15, ["pg15"], pg, ["pg"], 16.0, OP.mult, 15.0, OP.add)
+    op("v", g.vector.transpose, ["TD"], ["TE"], out=T.TE[:], in_=T.TD[:])
+    cp(T.colb[:], ["colb"], T.col[:, 0:144], ["col"])
+    tt(T.DS0[:], ["DS0"], T.TE[:, 0:16], T.TE[:, 16:32], ["TE"], OP.add)
+    send("D0", up, T.DR0[:], T.DS0[:], ["DS0"])
+    arrives("D0", down, "DR0")
+    ts(p32, ["p32"], pid, ["pid"], -32.0, OP.add)
+    selectors(8, 16)
+    for k, (nl, _) in enumerate(CHUNKS):
+        iota(T.colJ[:, 32 * START[k]:32 * START[k + 1]], "colJ", [[8192, 32], [0, nl]], 129 * 4096)
+
+    def spread_b(i):
+        bank = PSUM[i % 6]
+        mm(ps(bank, 0, 512), [bank], T.ONE[0:1, 0:128], T.FR[0:1, :], ["ONE", "FR"], True, False)
+        for h in range(2):
+            m = 2 * i + h
+            mm(ps(bank, 256 * h, 256 * h + 256), [bank], T.SEL[:, 128 * m:128 * m + 128], T.lo[:], ["SEL%d" % i, "lo"], False, False)
+            mm(ps(bank, 256 * h, 256 * h + 256), [bank], T.SEL[:, 128 * m:128 * m + 128], T.hi[:], ["SEL%d" % i, "hi"], False, h == 1)
+        act(T.FB[:, 512 * i:512 * i + 512], ["FB"], ps(bank, 0, 512), [bank], AF.Copy, bias=1.0 + 512 * i * FRAC)
 
     def send_starts(t, dst):
         act(T["SS%d" % t][:], ["SS%d" % t], T.X[:, t:WN:16], ["X"], AF.Copy)
         send("S%d" % t, dst, T["SR%d" % t][:], T["SS%d" % t][:], ["SS%d" % t])
+
+    def send_all(t, dst):
         send("B%d" % t, dst, T["XR%d" % t][:, 0:WN], T.X[:, 0:WN], ["X"])
 
-    send_starts(0, up)
+    for i in range(8):
+        if i == 2:
+            send_starts(0, up)
+            send_all(0, up)
+        spread_b(i)
     arrives("S0", down, "SR0")
     arrives("B0", down, "XR0")
-    iota("IOTA", [[1, WD]], 0, 0, WD)
+    iota(T.coll[:], "coll", [[0, 16], [1, 16]], 0)
+    iota(T.SEG[:], "SEG", [[0, 256]], -4)
+    iota(T.X[:, WN:WD], "Xd", [[0, 256]], 0)
+    for t in range(2):
+        iota(T["vs%d" % t][:], "vs%d" % t, [[16, 256]], t + 1)
+    iota(T.vr0[:], "vr0", [[16, 256]], 1)
+    iota(T.FA[:, WN:WD], "FAd", [[0, 256]], 1)
+    iota(T.IO[:, WN + 1:WD + 8], "IO", [[0, WD + 7 - WN]], 0)
 
-    def fill(ap, w, c):
-        before("v", [], [w])
-        g.vector.memset(ap, c).then_inc(T.sem.cv, 1)
-        count["cv"] = count.get("cv", 0) + 1
-        after(("v", "cv", count["cv"]), [], [w])
-
-    fill(T.X[:, WN:WD], "Xd", 0.0)
-    fill(T.OA[:, WN:WD], "OAd", 0.0)
-    fill(T.OB[:, WN:WD], "OBd", 0.0)
-    fill(T.IOTA[:, WD:WD + 8], "IOTAd", -1.0)
-    fill(T.ONE[:], "ONE", 1.0)
-    fill(T.KT[:], "KT", 0.0)
-    fill(T.CK[:], "CK", -15.5 / 128)
-    fill(T.PLf[:], "PLf", 8192.0)
-    ts(T.pmi[:], ["pmi"], T.pidx[:], ["pidx"], 15, OP.bitwise_and)
-    ts(T.pgi[:], ["pgi"], T.pidx[:], ["pidx"], 4, OP.arith_shift_right)
-    cp(T.pidf[:], ["pidf"], T.pidx[:], ["pidx"])
-    cp(T.pmf[:], ["pmf"], T.pmi[:], ["pmi"])
-    cp(T.pgf[:], ["pgf"], T.pgi[:], ["pgi"])
-    ts(T.pg15[:], ["pg15"], T.pgf[:], ["pgf"], 16.0, OP.mult, 15.0, OP.add)
-    for nm, val in (("E8", 8192.0), ("E4n", -4096.0)):
-        ts(T[nm][:], [nm], T.col[:, 0:144], ["col"], T.pg15[:], OP.is_equal, val, OP.mult, cols=["pg15"])
-    ts(T.GS[:], ["GS"], T.col[:, 0:8], ["col"], T.pgf[:], OP.is_equal, cols=["pgf"])
-    for nm, val in (("I16", 1.0), ("IB", 1.0), ("INB", -1.0), ("IBAR", 16777216.0)):
-        ts(T[nm][:], [nm], T.col[:, 0:128], ["col"], T.pidf[:], OP.is_equal, val, OP.mult, cols=["pidf"])
-    ts(T.dl[:], ["dl"], T.colL[:], ["colL"], T.pmf[:], OP.is_equal, cols=["pmf"])
-    cp(T.RH[:], ["RH"], T.dl[:], ["dl"])
-    tt(T.RU[:], ["RU"], T.colJ[:], T.dl[:], ["colJ", "dl"], OP.mult)
-    h0, g1, g3, e1, r1, r2, kv, rv = [T.kc[:, i:i + 1] for i in range(8)]
-    ts(h0, ["h0"], T.pidf[:], ["pidf"], 0.0, OP.is_equal, 0.5, OP.mult)
-    ts(g1, ["g1"], T.pidf[:], ["pidf"], 1.0, OP.is_ge, 2048.0, OP.mult)
-    ts(g3, ["g3"], T.pidf[:], ["pidf"], 3.0, OP.is_ge, -8.0, OP.mult)
-    ts(e1, ["e1"], T.pidf[:], ["pidf"], 1.0, OP.is_equal, -1.0, OP.mult)
-    ts(r1, ["r1"], T.pidf[:], ["pidf"], 1.0, OP.is_ge, -4096.0, OP.mult)
-    ts(r2, ["r2"], T.pidf[:], ["pidf"], 2.0, OP.is_ge, -4096.0, OP.mult)
-    tt(kv, ["kv"], h0, g1, ["h0", "g1"], OP.add)
-    ts(rv, ["rv"], T.pidf[:], ["pidf"], 0.0, OP.is_equal, e1, OP.add, cols=["e1"])
-    tt(kv, ["kv"], kv, g3, ["kv", "g3"], OP.add)
-    ts(T.RK[:], ["RK"], T.ONE[:], ["ONE"], rv, OP.mult, cols=["rv"])
-    ts(T.KC[:], ["KC"], T.ONE[:, 0:128], ["ONE"], kv, OP.mult, cols=["kv"])
     cp(T.wf[:], ["wf"], T.wti[:], ["wti"])
+    ts(T.GS[:], ["GS"], T.col[:, 0:8], ["col", "pg"], pg, OP.is_equal, 1.0 / 4096, OP.mult)
     ts(T.wg[:], ["wg"], T.wf[:], ["wf"], 2048.0, OP.is_gt, -4096.0, OP.mult)
+    fill(T.KT[:], "KTc", 3.0 / 32)
     tt(T.wg[:], ["wg"], T.wg[:], T.wf[:], ["wg", "wf"], OP.add)
-    ts(T.WG[:], ["WG"], T.GS[:], ["GS"], T.wg[:], OP.mult, cols=["wg"])
-    c0 = 16 * NR
-    ts(T.RO[:, c0:512], ["RO"], T.ONE[:, c0:512], ["ONE"], r1, OP.mult, cols=["r1"])
-    ts(T.RO[:, 0:c0], ["RO"], T.ONE[:, 0:c0], ["ONE"], r2, OP.mult, cols=["r2"])
-    ts(T.RZ[:, c0:512], ["RZ"], T.RH[:, c0:512], ["RH"], -4096.0, OP.mult)
-    ts(T.RZ[:, 0:c0], ["RZ"], T.RH[:, 0:c0], ["RH"], 0.0, OP.mult)
-    cp(T.qs[:], ["qs"], T.pai[:], ["pai"])
-    cp(T.t2[:], ["t2"], T.pbi[:], ["pbi"])
-    dma("y", "sta", [(T.oad[:], T.qs[:])], ["qs"], ["oad"])
-    dma("y", "stb", [(T.obd[:], T.t2[:])], ["t2"], ["obd"])
-    dma("y", "roa", [(T.OA[m::16, 0:WN], T.oad[:]) for m in range(16)], ["oad"], ["OA"])
-    dma("y", "rob", [(T.OB[m::16, 0:WN], T.obd[:]) for m in range(16)], ["obd"], ["OB"])
+    ts(T.RH[:], ["RH"], T.colL[:], ["colL", "pid"], pid, OP.is_equal)
+    ts(T.WG[:], ["WG"], T.GS[:], ["GS", "wg"], T.wg[:], OP.mult)
+    fill(T.KT[0:1, :], "KT", 0.0, ["KTc"])
+    ts(T.RQ[:, 0:WIDE], ["RQ"], T.RH[:, 0:WIDE], ["RH"], 524288.0, OP.mult)
+    for nm, val in (("IB", 1.0), ("INB", -1.0), ("I16", 1.0), ("IBAR", 16777216.0), ("I32", 1.0)):
+        ts(T[nm][:], [nm], T.colb[:, 0:128], ["colb", "pid"], pid, OP.is_equal, val, OP.mult)
+    tt(T.RU[:], ["RU"], T.colJ[:], T.RH[:], ["colJ", "RH"], OP.mult)
+    for nm, val in (("E8", 8192.0), ("E4n", -4096.0), ("E4", 4096.0)):
+        ts(T[nm][:], [nm], T.colb[:], ["colb", "pg15"], pg15, OP.is_equal, val, OP.mult)
+    ts(r17, ["r17"], pid, ["pid"], 17.0, OP.is_equal, -69632.0, OP.mult)
+    ts(r16, ["r16"], pid, ["pid"], 16.0, OP.is_equal, 16777216.0, OP.mult)
+    ts(T.RO[:], ["RO"], T.colL[:], ["colL", "p32"], p32, OP.is_equal, -16777216.0, OP.mult)
+    ts(rs, ["rs"], r16, ["r16", "r17"], 3.0, OP.mult, r17, OP.add)
+    ts(rv, ["rv"], r16, ["r16", "r17"], 2.0, OP.mult, r17, OP.add)
+    for eng, c0, c1 in runs:
+        ts(T.RZ[:, c0:c1], ["RZ"], T.RO[:, c0:c1], ["RO", "rs", "rv"], float(eng == "s"), OP.mult, rs if eng == "s" else rv, OP.add)
+    ts(T.BO[:], ["BO"], T.colg[:], ["colg", "pg16"], pg16, OP.is_equal)
+    ts(T.TRI[:], ["TRI"], T.coll[:, 0:128], ["coll", "pm"], pm, OP.is_gt)
+    ts(T.OFFB[:], ["OFFB"], T.coll[:], ["coll", "pm"], pm, OP.not_equal, 4.0, OP.mult)
+    ts(dc, ["dc"], pm, ["pm"], float(WN), OP.add, FRAC, OP.mult)
+    tt(T.TRI[:], ["TRI"], T.TRI[:], T.BO[:], ["TRI", "BO"], OP.mult)
+    ts(T.SEG[:, 0:256:16], ["SEG"], T.col[:, 0:16], ["col", "dc"], 16 * FRAC, OP.mult, dc, OP.add)
 
     def late_constants():
-        ts(T.IB8[:], ["IB8"], T.IB[:], ["IB"], 8192.0, OP.mult)
-        ts(T.BO[:], ["BO"], T.colg[:], ["colg"], T.pgf[:], OP.is_equal, 8192.0, OP.mult, cols=["pgf"])
-        ts(T.TRI[:], ["TRI"], T.colL[:, 0:128], ["colL"], T.pmf[:], OP.is_gt, cols=["pmf"])
-        tt(T.TRI[:], ["TRI"], T.TRI[:], T.BO[:], ["TRI", "BO"], OP.mult)
-        ts(T.DM[:], ["DM"], T.colL[:, 0:256], ["colL"], T.pmf[:], OP.is_equal, cols=["pmf"])
-        ts(T.OFFB[:], ["OFFB"], T.colL[:, 0:256], ["colL"], T.pmf[:], OP.not_equal, 1073741824.0, OP.mult, cols=["pmf"])
-        ts(T.OFFB[:], ["OFFB"], T.OFFB[:], ["OFFB"], 8192.0, OP.add)
-        ts(T.SEG[:], ["SEG"], T.colL[:, 0:256], ["colL"], 0.0, OP.not_equal)
-        ts(T.SEGB[:], ["SEGB"], T.colL[:, 0:256], ["colL"], 0.0, OP.is_equal, 2.0e10, OP.mult)
-        ts(T.SEGB[:], ["SEGB"], T.SEGB[:], ["SEGB"], -1.0e10, OP.add)
-        ts(T.DMD[:], ["DMD"], T.col[:], ["col"], 4097.0, OP.add)
-        tt(T.DMD[:], ["DMD"], T.DMD[:], T.DM[:], ["DMD", "DM"], OP.mult)
-        ts(T.vr0[:], ["vr0"], T.col[:], ["col"], 16.0, OP.mult)
-        ts(T.vr1[:], ["vr1"], T.col[:], ["col"], 16.0, OP.mult, 1.0, OP.add)
-        ts(T.DC[:], ["DC"], T.col[:, 0:16], ["col"], 16.0, OP.mult, T.pmf[:], OP.add, cols=["pmf"])
-        ts(T.DC[:], ["DC"], T.DC[:], ["DC"], 4096.0, OP.add)
+        for t, v in enumerate((1.278465, 2.217715)):
+            fill(T["vs%d" % t][:, 0:1], "vs%d" % t, v)
+        fill(T.PL[:], "PL", 1.0)
+        fill(T.CK[:, 0:1], "CK0", -15.5 / 128)
+        fill(T.CK[:, 1:2], "CK1", 0.5)
+        fill(one, "one", 1.0)
+        ts(pm1, ["pm1"], pm, ["pm"], 1.0, OP.add)
+        ts(up20, ["up20"], pm, ["pm"], 15.0, OP.is_equal, 1.0 - 2.0 ** -20, OP.mult)
+        ts(T.DY[:], ["DY"], T.coll[:], ["coll", "pm1"], pm1, OP.is_equal, 1048576.0, OP.mult)
+        ts(T.DX[:], ["DX"], T.coll[:], ["coll", "pm"], pm, OP.not_equal)
+        ts(dn20, ["dn20"], up20, ["up20"], 2.0 ** -20, OP.add)
+        tt(T.DX[:], ["DX"], T.DX[:], T.DY[:], ["DX", "DY"], OP.max)
+        ts(nd20, ["nd20"], dn20, ["dn20"], -1.0, OP.mult)
 
-    late_constants()
+    def store_a():
+        ts(pf, ["pf"], pm, ["pm"], 256 * FRAC, OP.mult, 1.0, OP.add)
+        ts(T.cf[:], ["cf"], T.col[:, 0:256], ["col", "pf"], FRAC, OP.mult, pf, OP.add)
+        tt(T.cp0[:], ["cp0"], T.pai[:], T.cf[:], ["pai", "cf"], OP.add)
+        dma("y", "sta", [(T.fad[:], T.cp0[:])], ["cp0"], ["fad"])
 
-    def run_flags(t, near, dst):
-        ts(T.pm[:], ["pm"], T[near][:, t:WN:16], [near], 0.0, OP.is_ge)
-        tt(T.pm[:], ["pm"], T.pm[:], T.DMD[:], ["pm", "DMD"], OP.mult)
-        scan(T.ps[:], ["ps"], T.SEG[:], T.pm[:], ["SEG", "pm"], 0.0, OP.mult, OP.add)
-        ts(T["DS%d" % t][:], ["DS%d" % t], T.ps[:, 15:256:16], ["ps"], -1.0, OP.add)
-        send("D%d" % t, dst, T["DR%d" % t][:], T["DS%d" % t][:], ["DS%d" % t])
+    def spread_a(h):
+        dma("y", "ro" + "ab"[h], [(T.FA[m::16, 0:WN], T.fad[:]) for m in range(8 * h, 8 * h + 8)], ["fad", "LST0"], ["FA%d" % h])
 
-    def near_update(t, near):
-        tab = T[near][:, t:WN:16]
-        tt(tab, [near], T.IOTA[:, 0:WD + 8].indirect(T["PR%d" % t][:]), tab, ["IOTA", "IOTAd", "PR%d" % t, near], OP.max)
+    def dead(t):
+        ts(T.DD[:], ["DD"], T["DR%d" % t][:], ["DR%d" % t], 0.25, OP.is_lt, float(WN), OP.mult)
 
-    def search(t, d, z, zr, hooks):
-        for l in range(16):
-            mm(T.ph[0:16, l:128:16], ["ph"], z[:, l:256:16], T.WG[:], ["WG", zr], True, True)
-        for l in range(16):
-            mm(T.pq[0:16, l:128:16], ["pq"], z[:, l:256:16], T.GS[:], ["GS", zr], True, True)
+    def plain_in(tab, i):
+        dma("y", "g" + "ab"[i], [(T["cp%d" % i][:], T[tab][0:128:16, 0:WN])], [tab], ["cp%d" % i])
 
-        def raw1(a, b, bank):
-            mm(T[bank][:, a:b], [bank], T.KC[0:4, :], T.RK[0:4, a:b], ["KC", "RK"], True, False)
-            mm(T[bank][:, a:b], [bank], T.KT[0:1, :], T.ONE[0:1, a:b], ["KT", "ONE"], False, False)
+    def plain_out(i):
+        c = "cp%d" % i
+        ts(T[c][:], [c], T[c][:], [c], 12582912.0, OP.add, -12582913.0, OP.add)
+        dma("y", "h" + "ab"[i], [(T["P" + "AB"[i]][0:128:16, 0:WN], T[c][:])], [c], ["P" + "AB"[i]])
 
-        def raw2(a, b, bank):
-            mm(T[bank][:, a:b], [bank], T.UT[0:16, :], T.RU[0:16, a:b], ["UT", "RU"], False, False)
+    def near_update(t, tab):
+        own = T[tab][:, t:WN:16]
+        tt(own, [tab], T.IO[:, 0:WD + 8].indirect(T["PR%d" % t][:]), own, ["IO", "PR%d" % t, tab, "FA0", "FA1"], OP.add)
 
-        def raw3(a, b, bank, stop):
-            mm(T[bank][:, a:b], [bank], T.HT[0:16, :], T.RH[0:16, a:b], ["HT", "RH"], False, stop)
+    def begin(i, bank):
+        a, b = PORT[i][:2]
+        mm(ps(bank, 0, b - a), [bank], T.KT[0:2, :], T.ONE[0:2, a:b], ["KT", "KTc", "ONE"], True, False)
 
-        (a0, b0, s0, e0), (a1, b1, s1, e1) = PORTIONS
-        raw1(a0, b0, s0)
-        raw1(a1, b1, s1)
-        raw1(a0, b0, e0)
-        cp(T.ui[0:16, :], ["ui"], T.ph[0:16, 0:128], ["ph"])
-        ts(T.u[0:16, :], ["u"], T.ui[0:16, :], ["ui"], 4095, OP.bitwise_and)
-        tt(T.sq[0:16, :], ["sq"], T.u[0:16, :], T.u[0:16, :], ["u"], OP.mult)
-        ts(T.UT[0:16, :], ["UT"], T.u[0:16, :], ["u"], -2048.0, OP.add)
-        ts(T.hm[0:16, :], ["hm"], T.sq[0:16, :], ["sq"], 5, OP.arith_shift_right, 4095, OP.bitwise_and)
-        ts(T.HT[0:16, :], ["HT"], T.hm[0:16, :], ["hm"], -2048.0, OP.add)
-        raw2(a0, b0, s0)
-        raw2(a1, b1, s1)
-        raw2(a0, b0, e0)
-        raw3(a0, b0, s0, True)
-        raw3(a0, b0, e0, False)
-        raw3(a1, b1, s1, True)
+    def ahead():
+        mm(ps("ph", 0, 128, 1, 0, 48), ["ph"], T.ONE[0:1, 0:48], T.MH[0:1, 0:128], ["ONE", "MH"], True, False)
+        for i, (_, _, raw, rest) in enumerate(PORT):
+            for bank in (raw, rest):
+                if bank != "ph":
+                    begin(i, bank)
+
+    win = T.X[:, 0:WN]
+
+    def parts_of(buf, k):
+        n = CHUNKS[k][0]
+        return buf[:, MBASE[k]:MBASE[k] + 16 * n], buf[:, MBASE[k] + 16 * n:MBASE[k] + 17 * n], buf[:, MBASE[k]:MBASE[k] + 17 * n]
+
+    def put_far(k, t, d, far):
+        act(T[far][:, 0:WD].indirect(parts_of(T["MO%d" % d], k)[1]), [far, far + "d"], T["vs%d" % t][:, 16 * START[k]:16 * START[k + 1]], ["vs%d" % t, "MO%dl%d" % (d, k)], AF.Silu)
+
+    def put_records(k, d):
+        xn, l2, _ = parts_of(T["MO%d" % d], k)
+        cp(T.X[:, 0:WD].indirect(l2), ["X", "Xd"], xn, ["MO%dx%d" % (d, k), "MO%dl%d" % (d, k)])
+
+    def put_replica(k, t, d):
+        mi = "MI%d%d" % (t, d)
+        arrives("M%d%d%d" % (t, d, k), down if t == 0 else up, "%s%d" % (mi, k))
+        xn, l2, _ = parts_of(T[mi], k)
+        cp(T["XR%d" % t][:, 0:WD].indirect(l2), ["XR%d" % t], xn, ["%s%d" % (mi, k)])
+
+    QS, YC, YL = [["%s%d" % (x, k) for k in range(NC)] for x in ("qs", "yc", "yl")]
+    ends = T.qs[:, 15:256:16]
+
+    KB = zbanks(NC)[1]
+    cnt = ps(KB, 0, 1, 1, 0, 1)
+
+    def count_pairs():
+        act(T.wb[:], ["wb", "k0"], ends, QS, AF.Sign, bias=0.25 - FRAC / 4, scale=-1.0, accum_out=T.k0[:])
+        mm(cnt, [KB], T.CK[:, 0:1], one, ["CK0", "one"], True, False)
+        mm(cnt, [KB], T.k0[:], T.CK[:, 1:2], ["k0", "CK1"], False, True)
+
+    def kappa(kd):
+        act(T.k1[0:1, :], ["k1"], cnt, [KB], AF.Copy, bias=402653184.0)
+        act(T.kr[0:1, :], ["kr"], T.k1[0:1, :], ["k1"], AF.Copy, bias=402653184.0, scale=-1.0)
+        act(T.kf[0:1, :], ["kf"], cnt, [KB, "kr"], AF.Identity, bias=T.kr[0:1, :])
+        act(T.KT[0:1, :], ["KT"], T.ONE[0:1, 0:128], ["ONE", "kf"], AF.Identity, bias=T.kf[0:1, :], scale=float(kd) + 15.5)
+
+    def step(t, d, z, zr, far):
+        mo = "MO%d" % d
+
+        def spread_z(k):
+            n, z0 = 16 * CHUNKS[k][0], 16 * START[k]
+            first = zbanks(k)[0]
+            for i in range(1024 // n):
+                cuts = [n * i] + ([512] if n * i < 512 < n * (i + 1) else []) + [n * (i + 1)]
+                for a, b in zip(cuts, cuts[1:]):
+                    mm(ps(first, a, b), [zbanks(k)[a // 512]], T.IB[:], z[:, z0 + a - n * i:z0 + b - n * i], ["IB"] + zr, True, True)
+
+        def copy_z(k):
+            act(T.zp[:, 0:ZP], ["zp"], ps(zbanks(k)[0], 0, ZP), zbanks(k, ZP), AF.Copy)
+
+        def head():
+            for l in range(16):
+                mm(ps("ph", l, 128, 16, 0, 16), ["ph"], z[:, l:256:16], T.WG[:], ["WG"] + zr, False, False)
+            for l in range(16):
+                mm(ps("ph", l, 128, 16, 32, 48), ["ph"], z[:, l:256:16], T.GS[:], ["GS"] + zr, False, False)
+            mm(ps("ph", 0, 1, 1, 0, 48), ["ph"], T.ONE[0:1, 0:48], T.MH[0:1, 128:129], ["ONE", "MH"], False, True)
+
+        def remainder():
+            x = ps("ph", 0, 128, 1, 0, 48)
+            ts(T.ri[0:48, :], ["ri"], x, ["ph"], 2.0 ** -13, OP.add)
+            tt(T.UF[0:48, :], ["UF"], x, T.ri[0:48, :], ["ph", "ri"], OP.subtract)
+            act(T.SQ[0:16, :], ["SQ"], T.UF[0:16, :], ["UF"], AF.Square)
+            cp(T.UZ[0:48, :], ["UZ"], T.UF[0:48, :], ["UF"])
+
+        def terms(i, which):
+            a, b = PORT[i][:2]
+            bank = PORT[i][which]
+            if bank == "ph":
+                begin(i, bank)
+            mm(ps(bank, 0, b - a), [bank], T.UZ[0:16, :], T.RU[0:16, a:b], ["UZ", "RU"], False, False)
+            if b <= WIDE:
+                mm(ps(bank, 0, b - a), [bank], T.SQ[0:16, :], T.RQ[0:16, a:b], ["SQ", "RQ"], False, which == 2)
+            else:
+                mm(ps(bank, 0, b - a), [bank], T.HT[0:16, :], T.RH[0:16, a:b], ["HT", "RH"], False, which == 2)
+
+        def short_h(i):
+            if i == 0:
+                ts(T.ri[0:16, :], ["ri"], T.SQ[0:16, :], ["SQ"], 524288.0, OP.mult, 2048.0 - 15.0 / 32, OP.add)
+            elif i == 1:
+                ts(T.hm[0:16, :], ["hm"], T.ri[0:16, :], ["ri"], 4095, OP.bitwise_and)
+            else:
+                ts(T.HT[0:16, :], ["HT"], T.hm[0:16, :], ["hm"], -2048.0, OP.add)
 
         def near(i):
-            a, b, bank, rest = PORTIONS[i]
-            ts(T.RR[:, a:b], ["RR%d" % i], T[bank][:, a:b], [bank], 51539607552.0, OP.add, -51539607552.0, OP.add)
-            mm(T[rest][:, a:b], [rest], T.INB[:], T.RR[:, a:b], ["INB", "RR%d" % i], False, True)
+            a, b, raw, _ = PORT[i]
+            ts(T.RR[:, a:b], ["RR%d" % i], ps(raw, 0, b - a), [raw], 51539607552.0, OP.add, -51539607552.0, OP.add)
+
+        def take(i):
+            a, b, _, rest = PORT[i]
+            mm(ps(rest, 0, b - a), [rest], T.INB[:], T.RR[:, a:b], ["INB", "RR%d" % i], False, True)
 
         def lists(i):
-            a, b, _, rest = PORTIONS[i]
-            ts(T.LST[:, a:b], ["LST%d" % i], T[rest][:, a:b], [rest], 2047.5, OP.add)
+            a, b, _, rest = PORT[i]
+            ts(T.LST[:, a:b], ["LST%d" % i], ps(rest, 0, b - a), [rest], 2047.5, OP.add)
 
-        near(0)
-        raw1(a1, b1, e1)
-        raw2(a1, b1, e1)
-        raw3(a1, b1, e1, False)
-        ts(T.ZT[0:16, :], ["ZT"], T.pq[0:16, 0:128], ["pq"], -2048.0, OP.add)
-        for i in range(4):
-            mm(T.pz[:, 256 * i:256 * i + 256], ["pz"], T.IB[:], z[:], ["IB", zr], True, True)
-        lists(0)
-        near(1)
-        win = T.X[:, 0:WN]
-        for pieces in SCH:
-            for j0, j1 in pieces:
-                if 16 * j1 <= PORTIONS[0][1]:
-                    act(T.A[:, 256 * j0:256 * j1], ["A%d" % j0], win.indirect(T.LST[:, 16 * j0:16 * j1]), ["X", "LST0"], AF.Copy)
-        mm(T.pk[:], ["pk"], T.KC[0:4, :], T.RO[0:4, :], ["KC", "RO"], True, False)
-        mm(T.pk[:], ["pk"], T.ZT[0:16, :], T.RZ[0:16, :], ["ZT", "RZ"], False, False)
-        if d > 0:
-            mm(T.pc[:], ["pc"], T.LT[0:16, :], T.RH[0:16, :], ["LT", "RH"], True, True)
+        def gather(i):
+            k, eng, c0, c1 = pieces[i]
+            act(T.A[:, 16 * c0:16 * c1], ["A%d" % i], win.indirect(T.LST[:, c0:c1]), ["X"] + lst(c0, c1), AF.Copy)
 
-        def sums(src, sel, pieces):
-            j0, j1 = pieces[0][0], pieces[-1][1]
+        def subs(i):
+            k, eng, c0, c1 = pieces[i]
+            nl = CHUNKS[k][0]
+            w = nl * ((64 if eng == "s" else ZP // 16) // nl)
+            return [(c, min(c + w, c1)) for c in range(c0, c1, w)]
+
+        def gather_v(i, h):
+            c, e = subs(i)[h]
+            tt(T.A[:, 16 * c:16 * e], ["A%d_%d" % (i, h)], win.indirect(T.LST[:, c:e]), T.zp[:, 0:16 * (e - c)], ["X", "zp"] + lst(c, e), OP.subtract)
+
+        def relu(i):
+            k, eng, c0, c1 = pieces[i]
+            names = ["A%d_%d" % (i, h) for h in range(len(subs(i)))]
+            if eng == "c":
+                act(T.M[:, 16 * c0:16 * c1], ["M%d" % i], T.A[:, 16 * c0:16 * c1], names, AF.Abs)
+            else:
+                ts(T.M[:, 16 * c0:16 * c1], ["M%d" % i], T.A[:, 16 * c0:16 * c1], names, 0.0, OP.max)
+
+        def maxima(i, h=0):
+            c, e = subs(i)[h]
+            banks = zbanks(pieces[i][0], 16 * (e - c))
+            tt(T.M[:, 16 * c:16 * e], ["M%d_%d" % (i, h)], T.A[:, 16 * c:16 * e], ps(banks[0], 0, 16 * (e - c)), ["A%d" % i] + banks, OP.max)
+
+        def sums(src, i, j=None):
+            k, c0, c1 = pieces[i][0], pieces[i][2], pieces[j or i][3]
+            bank, base = "pk%d" % (k % 2), 32 * START[k]
+            names = []
+            for p in range(i, (j or i) + 1):
+                whole = (src, pieces[p][1]) in (("A", "s"), ("M", "v"), ("M", "c"))
+                names += ["%s%d" % (src, p)] if whole else ["%s%d_%d" % (src, p, h) for h in range(len(subs(p)))]
+            sel = "E4n" if src == "A" else "E4" if pieces[i][1] == "c" else "E8"
             for l in range(16):
-                mm(T.pk[:, 16 * j0:16 * j1], ["pk"], T[sel][:, 15 - l:143 - l], T[src][:, 256 * j0 + l:256 * j1:16], [sel] + ["%s%d" % (src, a) for a, _ in pieces], False, False)
+                mm(ps(bank, c0 - base, c1 - base), [bank], T[sel][:, 15 - l:143 - l], T[src][:, 16 * c0 + l:16 * c1:16], [sel] + names, False, False)
 
-        if NR:
-            for j in range(NR):
-                if j == NR // 2:
-                    lists(1)
-                    for pieces in SCH:
-                        for j0, j1 in pieces:
-                            if 16 * j1 > PORTIONS[0][1]:
-                                act(T.A[:, 256 * j0:256 * j1], ["A%d" % j0], win.indirect(T.LST[:, 16 * j0:16 * j1]), ["X", "LST1"], AF.Copy)
-                tt(T.A[:, 256 * j:256 * j + 256], ["A0"], win.indirect(T.LST[:, 16 * j:16 * j + 16]), z[:], ["X", "LST0", zr], OP.subtract)
-            ts(T.M[:, 0:256 * NR], ["M0"], T.A[:, 0:256 * NR], ["A0"], 0.0, OP.max)
-        sums("A", "E4n", SCH[0])
-        if NR:
-            sums("A", "E4n", [(0, NR)])
-            sums("M", "E8", [(0, NR)])
-        ts(T.c16[:], ["c16"], T.LST[:], ["LST0", "LST1"], -2048.0, OP.add)
-        if d > 0:
-            tt(T.bar[:], ["bar"], T.c16[:], T.pc[:], ["c16", "pc"], OP.is_equal)
-        else:
-            ts(T.sm[:], ["sm"], z[:], [zr], -0.5, OP.add)
-        for k, pieces in enumerate(SCH):
-            for j0, j1 in pieces:
-                tt(T.M[:, 256 * j0:256 * j1], ["M%d" % j0], T.A[:, 256 * j0:256 * j1], T.pz[:, 0:256 * (j1 - j0)], ["A%d" % j0, "pz"], OP.max)
-            if k == 0 and d > 0:
-                mm(T.pk[:], ["pk"], T.IBAR[:], T.bar[:], ["IBAR", "bar"], False, False)
-            if k < EARLY:
-                sums("A", "E4n", SCH[k + 1])
-            sums("M", "E8", pieces)
-            if k == len(SCH) - 2:
-                mm(T.pk[:, 0:16 * SCH[-1][0][0]], ["pk"], T.I16[:], T.c16[:, 0:16 * SCH[-1][0][0]], ["I16", "c16"], False, False)
-            if EARLY <= k < len(SCH) - 1:
-                sums("A", "E4n", SCH[k + 1])
-            if k == 4:
-                for h in hooks:
-                    h()
-        mm(T.pk[:, 16 * SCH[-1][0][0]:512], ["pk"], T.I16[:], T.c16[:, 16 * SCH[-1][0][0]:512], ["I16", "c16"], False, True)
-        for L in range(16):
-            op("v", g.vector.tensor_reduce, ["pk"], ["ym"], out=T.ym[:, L:L + 1], in_=T.pk[:, L:512:16], axis=AxisListType.X, op=OP.min)
+        def keys(k, lhsT, rhs, r, start=False, stop=False):
+            bank, c0, c1 = "pk%d" % (k % 2), 32 * START[k], 32 * START[k + 1]
+            mm(ps(bank, 0, c1 - c0), [bank], lhsT, rhs(c0, c1), r, start, stop)
 
-    def pair(t, d, far, kd):
-        xn, l2 = "XN%d" % d, "L2%d" % d
+        def open_keys(k):
+            keys(k, T.UZ[0:48, :], lambda a, b: T.RZ[0:48, a:b], ["UZ", "RZ"], start=True)
+
+        def bar_keys(k):
+            if d > 0:
+                keys(k, T.IBAR[:], lambda a, b: T.bar[:, a:b], ["IBAR", "bar"])
+
+        def close_keys(k):
+            keys(k, T.I16[:], lambda a, b: T.c16[:, a:b], ["I16", "c16"], stop=True)
+
+        def places():
+            ts(T.c16[:], ["c16"], T.LST[:], lst(0, 512), -2048.0, OP.add)
+
+        def old_places():
+            if d > 0:
+                mm(ps("pr", 0, 512), ["pr"], T.LT[0:16, :], T.RH[0:16, :], ["LT", "RH"], True, True)
+
+        def barred():
+            if d > 0:
+                tt(T.bar[:], ["bar"], T.c16[:], ps("pr", 0, 512), ["c16", "pr"], OP.is_equal)
+
+        def choose(k):
+            a, b = START[k], START[k + 1]
+            bank = "pk%d" % (k % 2)
+            for L in range(a, b):
+                op("v", g.vector.tensor_reduce, [bank], ["ym%d" % L], out=T.ym[:, L:L + 1], in_=ps(bank, L - a, 32 * (b - a), b - a), axis=AxisListType.X, op=OP.min)
+            ts(T.y[:, a:b], ["y%d" % k], T.ym[:, a:b], ["ym%d" % L for L in range(a, b)], 4095, OP.bitwise_and)
+            if k == NC - 1:
+                cp(T.yl[:, a:b], ["yl%d" % k], T.y[:, a:b], ["y%d" % k])
+            tt(T.yc[:, a:b], ["yc%d" % k], T.y[:, a:b], T.DD[:, a:b], ["y%d" % k, "DD"], OP.max)
+            if k < NC - 1:
+                cp(T.yl[:, a:b], ["yl%d" % k], T.yc[:, a:b], ["yc%d" % k])
+
+        def fetch(k):
+            a, b = START[k], START[k + 1]
+            act(T.FG[:, 16 * a:16 * b], ["FG%d" % k], T[far][:, 0:WD].indirect(T.yl[:, a:b]), [far, far + "d", "yl%d" % k], AF.Copy)
+            act(T.XG[:, 16 * a:16 * b], ["XG%d" % k], T.X[:, 0:WD].indirect(T.yl[:, a:b]), ["X", "Xd", "yl%d" % k], AF.Copy)
+
+        def prepare(k):
+            a, b = START[k], START[k + 1]
+            n = 16 * (b - a)
+            pq, pt = zbanks(k)
+            mm(ps(pq, 0, n), [pq], T.IB[:], T.OFFB[:, 0:n], ["IB", "OFFB"], True, False)
+            mm(ps(pt, 0, n), [pt], T.IB[:], T["SR%d" % t][:, 16 * a:16 * b], ["IB", "SR%d" % t], True, False)
+            if k == NC - 1:
+                for l in range(16):
+                    mm(ps(pq, l, n, 16), [pq], T.IB[:], T.DD[:, a:b], ["IB", "DD"], False, False)
+
+        def compare(k):
+            a, b = START[k], START[k + 1]
+            n = 16 * (b - a)
+            pq, pt = zbanks(k)
+            mm(ps(pq, 0, n), [pq], T.I32[:], T.FG[:, 16 * a:16 * b], ["I32", "FG%d" % k], False, False)
+            base = 0
+            for L in range(a, b):
+                w, e, o = 16 * (b - L), "EQ%d" % (L - a), 16 * (L - a)
+                ts(T.EQ[:, base:base + w], [e], T.FG[:, 16 * L:16 * b], ["FG%d" % k, "yc%d" % k], 1.0 / FRAC, OP.mult, T.yc[:, L:L + 1], OP.is_equal)
+                if L == min(a + 2, b - 1):
+                    mm(ps(pt, 0, n), [pt], T.IB[:], T.XG[:, 16 * a:16 * b], ["IB", "XG%d" % k], False, True)
+                if w > 16:
+                    mm(ps(pq, o + 16, n), [pq], T.BO[:], T.EQ[:, base + 16:base + w], ["BO", e], False, False)
+                mm(ps(pq, o, o + 16), [pq], T.TRI[:], T.EQ[:, base:base + 16], ["TRI", e], False, L == b - 1)
+                base += w
+
+        def settle(k):
+            a, b = START[k], START[k + 1]
+            n = 16 * (b - a)
+            pq, pt = zbanks(k)
+            xn, l2, whole = parts_of(T[mo], k)
+            ts(xn, ["%sx%d" % (mo, k)], ps(pt, 0, n), [pt], 0.5, OP.mult, -0.25, OP.add)
+            scan(T.qs[:, 16 * a:16 * b], ["qs%d" % k], T.SEG[:, 16 * a:16 * b], ps(pq, 0, n), ["SEG", pq], 0.0, OP.max, OP.min)
+            ts(l2, ["%sl%d" % (mo, k)], T.qs[:, 16 * a + 15:16 * b:16], ["qs%d" % k], 1.0 / FRAC, OP.mult)
+            if d < STEPS - 1:
+                send("M%d%d%d" % (t, d, k), up if t == 0 else down, parts_of(T["MI%d%d" % (t, d)], k)[2], whole, ["%sx%d" % (mo, k), "%sl%d" % (mo, k)])
+
         dr = "DR%d" % t
-        ts(T.yi[:], ["yi"], T.ym[:], ["ym"], 2048.0, OP.add)
-        ts(T.y[:], ["y"], T.yi[:], ["yi"], 4095, OP.bitwise_and)
-        tt(T.yc[:], ["yc"], T.y[:], T[dr][:], ["y", dr], OP.max)
-        cp(T.yl[:], ["yl"], T.yc[:], ["yc"])
-        ow = T[far][:, 0:WD]
-        act(T.XG[:], ["XG"], T.X[:, 0:WD].indirect(T.yl[:]), ["X", "Xd", "yl"], AF.Copy)
-        cp(T.Yr[:], ["Yr"], T.IOTA[:, 0:WD].indirect(T.yl[:]), ["IOTA", "yl"])
-        mm(T.pq[:, 0:256], ["pq"], T.IB[:], T.OFFB[:], ["IB", "OFFB"], True, False)
-        mm(T.ph[:, 0:256], ["ph"], T.I16[:], T.sm[:], ["I16", "sm"], True, False)
-        mm(T.ph[:, 0:256], ["ph"], T.IB[:], T.XG[:], ["IB", "XG"], False, True)
-        act(T.t2[:], ["t2"], T.ph[:, 0:256], ["ph"], AF.Copy, bias=8388608.0, scale=0.5)
-        act(T[xn][:], [xn], T.t2[:], ["t2"], AF.Copy, bias=-8388608.0)
-        act(T.Or[:], ["Or"], ow.indirect(T.yl[:]), [far, far + "d", "yl"], AF.Copy)
-        base = 0
-        for L in range(16):
-            n = 256 - 16 * L
-            e = "EQ%d" % L
-            ts(T.EQ[:, base:base + n], [e], T.Yr[:, 16 * L:256], ["Yr"], T.yc[:, L:L + 1], OP.is_equal, cols=["yc"])
-            if n > 16:
-                mm(T.pq[:, 16 * L + 16:256], ["pq"], T.BO[:], T.EQ[:, base + 16:base + n], ["BO", e], False, False)
-            if L == 15:
-                mm(T.pq[:, 0:256], ["pq"], T.IB8[:], T.Or[:], ["IB8", "Or"], False, False)
-            mm(T.pq[:, 16 * L:16 * L + 16], ["pq"], T.TRI[:], T.EQ[:, base:base + 16], ["TRI", e], False, L == 15)
-            base += n
-        tell = d < STEPS - 1
-        dst = up if t == 0 else down
-        if tell:
-            send("X%d%d" % (t, d), dst, T["XI%d%d" % (t, d)][:], T[xn][:], [xn])
-        scan(T.qs[:], ["qs"], T.SEGB[:], T.pq[:, 0:256], ["SEGB", "pq"], 1.0e10, OP.max, OP.min)
-        tt(T.nw[:], ["nw"], T.qs[:, 15:256:16], T.DC[:], ["qs", "DC"], OP.min)
-        tt(T.lf[:], ["lf"], T.yc[:], T.nw[:], ["yc", "nw"], OP.max)
-        cp(T[l2][:], [l2], T.lf[:], ["lf"])
-        if tell:
-            send("L%d%d" % (t, d), dst, T["LI%d%d" % (t, d)][:], T[l2][:], [l2])
+
+        def partners():
+            act(T.FP[:], ["FP"], T[far][:, 0:WD].indirect(T.yl[:]), [far, far + "d"] + YL, AF.Copy)
+
+        def own_column():
+            scan(T.ps[:], ["ps"], T.DX[:], T.FP[:], ["DX", "FP"], 0.0, OP.mult, OP.add)
+            ts(T.pl16[:], ["pl16"], T.ps[:, 15:256:16], ["ps", "dn20"], dn20, OP.mult, -1.0, OP.add)
+
+        def turn():
+            ts(T.TB[:], ["TB"], T.yc[:], YC, -2048.0, OP.add)
+            mm(ps("z0a", 0, 128, 1, 0, 16), ["z0a"], T.TB[:], T.I16[:], ["TB", "I16"], True, True)
+
+        def turned():
+            cp(T.LT[0:16, :], ["LT"], ps("z0a", 0, 128, 1, 0, 16), ["z0a"])
+
+        def next_z():
+            xr = T["XR%d" % t][:, 0:WN]
+            act(T.zb[:, 0:16 * ZS], ["zb0"], xr.indirect(T.pl16[:, 0:ZS]), ["XR%d" % t, "pl16"], AF.Copy)
+            if ZS < 16:
+                cp(T.zb[:, 16 * ZS:256], ["zb1"], xr.indirect(T.pl16[:, ZS:16]), ["XR%d" % t, "pl16"])
+
+        def paired():
+            tt(T[dr][:], [dr], T[dr][:], ends, [dr] + QS, OP.min)
+            if t == 1:
+                tt(T.PL[:], ["PL"], T.PL[:], ends, ["PL"] + QS, OP.min)
 
         def home():
-            tt(T.PLf[:], ["PLf"], T.PLf[:], T.lf[:], ["PLf", "lf"], OP.min)
-            if d == STEPS - 1:
-                ts(T.wd[:], ["wd"], T.PLf[:], ["PLf"], float(WN), OP.is_ge, 8192.0, OP.mult)
-                tt(T.wd[:], ["wd"], T.wd[:], T.PLf[:], ["wd", "PLf"], OP.max)
-                ts(T["PS%d" % t][:], ["PS%d" % t], T.wd[:], ["wd"], float(WD), OP.min)
-                fill(T.PLf[:], "PLf", 8192.0)
+            ts(T["PS%d" % t][:], ["PS%d" % t], T[dr][:], [dr], 1.0 / FRAC, OP.mult, 1.0, OP.add)
+            send("P%d" % t, down if t == 0 else up, T["PR%d" % t][:], T["PS%d" % t][:], ["PS%d" % t])
+            arrives("P%d" % t, up if t == 0 else down, "PR%d" % t)
 
-        def put_records():
-            cp(T.X[:, 0:WD].indirect(T[l2][:]), ["X", "Xd"], T[xn][:], [xn, l2])
+        def flags():
+            scan(T.ps[:], ["ps"], T.DX[:], T.FB[:, 1:WN:16], ["DX", "FB"], 0.0, OP.mult, OP.add)
+            ts(T.DS1[:], ["DS1"], T.ps[:, 15:256:16], ["ps", "nd20"], nd20, OP.mult, 0.75, OP.add)
+            send("D1", down, T.DR1[:], T.DS1[:], ["DS1"])
+            arrives("D1", up, "DR1")
 
-        def put_far():
-            cp(ow.indirect(T[l2][:]), [far, far + "d"], T["vr%d" % t][:], ["vr%d" % t, l2])
+        def starts():
+            send_starts(1, down)
+            arrives("S1", up, "SR1")
 
-        def small():
-            if tell:
-                ts(T.TB[:], ["TB"], T.y[:], ["y"], -2048.0, OP.add)
-                mm(T.pc[0:16, 0:128], ["pc"], T.TB[:], T.I16[:], ["TB", "I16"], True, True)
-                tt(T.wd[:], ["wd"], T.DC[:], T.nw[:], ["DC", "nw"], OP.subtract)
-                cp(T.LT[0:16, :], ["LT"], T.pc[0:16, 0:128], ["pc"])
-                tt(T[dr][:], [dr], T[dr][:], T.wd[:], [dr, "wd"], OP.max)
+        def whole():
+            send_all(1, down)
+            arrives("B1", up, "XR1")
 
-        def kappa():
-            act(T.wb[:], ["wb"], T.qs[:, 15:256:16], ["qs"], AF.Relu, bias=1.0, scale=-1.0)
-            mm(T.pt[:, 0:1], ["pt"], T.ONE[:, 0:128], T.CK[:, 0:1], ["ONE", "CK"], True, False)
-            for L in range(16):
-                mm(T.pt[:, 0:1], ["pt"], T.ONE[:, 0:128], T.wb[:, L:L + 1], ["ONE", "wb"], False, L == 15)
-            act(T.k1[:], ["k1"], T.pt[:, 0:1], ["pt"], AF.Identity, bias=402653184.0)
-            act(T.kr[:], ["kr"], T.k1[:], ["k1"], AF.Copy, bias=402653184.0, scale=-1.0)
-            act(T.kf[:], ["kf"], T.pt[:, 0:1], ["pt", "kr"], AF.Identity, bias=T.kr[:])
-            act(T.KT[0:1, :], ["KT"], T.ONE[0:1, 0:128], ["ONE", "kf"], AF.Identity, bias=T.kf[0:1, :], scale=float(kd) + 15.5)
+        def out_a():
+            ts(T.PLl[:], ["PLl"], T.PL[:], ["PL"], 1.0 / FRAC, OP.mult)
+            cp(T.PA[:, 0:WD].indirect(T.PLl[:]), ["PA"], T.vr0[:], ["vr0", "PLl"])
+            dma("s", "outa", [(T.ya[:], T.PA[0:128:16, 0:WN])], ["PA"], [])
 
-        return home, put_records, put_far, small, kappa
+        def out_b():
+            near_update(1, "PB")
+            dma("s", "outb", [(T.yb[:], T.PB[0:128:16, 0:WN])], ["PB"], [])
 
-    def next_z(t, d):
-        src = down if t == 0 else up
-        xr = "XR%d" % t
-        arrives("X%d%d" % (t, d), src, "XI%d%d" % (t, d))
-        arrives("L%d%d" % (t, d), src, "LI%d%d" % (t, d))
-        cp(T[xr][:, 0:WD].indirect(T["LI%d%d" % (t, d)][:]), [xr], T["XI%d%d" % (t, d)][:], [xr, "XI%d%d" % (t, d), "LI%d%d" % (t, d)])
-        act(T.zb[:], ["zb"], T[xr][:, 0:WN].indirect(T.pl16[:]), [xr, "pl16"], AF.Copy)
+        return {"x": lambda k: put_records(k, d), "r": lambda k: put_replica(k, t, d), "f": lambda k: put_far(k, t, d, far),
+                "fp": partners, "pl": own_column, "tb": turn, "lt": turned, "z": next_z, "won": paired, "dead": lambda: dead(t),
+                "kappa": lambda: kappa(97 * (d + 1) % (97 * STEPS)), "ahead": ahead, "home": home, "flags": flags, "starts": starts, "whole": whole,
+                "outx": lambda: dma("y", "outx", [(T.yx[:], T.X[:, 0:WN])], ["X"], []), "outa": out_a, "outb": out_b,
+                "W": lambda i: terms(i, 2), "E": lambda i: terms(i, 3), "N": near, "T": take, "L": lists, "G": gather, "V": gather_v, "R": relu,
+                "count": count_pairs, "X": maxima, "A": lambda *i: sums("A", *i), "M": lambda *i: sums("M", *i), "O": open_keys, "B": bar_keys, "C": close_keys,
+                "Z": spread_z, "Y": copy_z, "H": choose, "F": fetch, "P": prepare, "Q": compare, "U": settle,
+                "h": short_h, "hash": head, "u": remainder, "c16": places, "last": old_places, "bar": barred}
 
+    before_ = None
+    ahead()
     for t in range(2):
-        far = "OB" if t == 0 else "OA"
-        near = "OA" if t == 0 else "OB"
+        far = "FB" if t == 0 else "FA"
         for d in range(STEPS):
-            hooks = []
+            extra = []
+            if d == 0:
+                extra.append(lambda: dead(t))
             if (t, d) == (0, 0):
-                hooks.append(lambda: run_flags(0, "OA", up))
-                hooks.append(lambda: arrives("D0", down, "DR0"))
+                extra += [late_constants, store_a]
+            if t == 0 and d > 0:
+                extra.append(lambda: spread_a(d - 1))
+                h = 2048 * (d - 1)
+                iota(T.IO[:, h:h + 2048 + d - 1], "IO", [[1, 2048 + d - 1]], h)
             if (t, d) == (1, 0):
-                hooks.append(lambda: near_update(0, "OA"))
-            zn = "SR%d" % t if d == 0 else "zb"
-            search(t, d, T[zn], zn, hooks)
-            home, put_records, put_far, small, kappa = pair(t, d, far, 97 * (d + 1) if d < STEPS - 1 else 0)
-            if d < STEPS - 1:
-                put_far()
-                tt(T.pm[:], ["pm"], T[far][:, 0:WD].indirect(T.yl[:]), T.DM[:], [far, far + "d", "yl", "DM"], OP.mult)
-                scan(T.ps[:], ["ps"], T.SEG[:], T.pm[:], ["SEG", "pm"], 0.0, OP.mult, OP.add)
-                cp(T.pl16[:], ["pl16"], T.ps[:, 15:256:16], ["ps"])
-                kappa()
-                small()
-                home()
-                next_z(t, d)
-                put_records()
-            elif t == 0:
-                put_records()
-                send_starts(1, down)
-                kappa()
-                put_far()
-                home()
-                send("P0", down, T.PR0[:], T.PS0[:], ["PS0"])
-                run_flags(1, "OB", down)
-                arrives("S1", up, "SR1")
-                arrives("B1", up, "XR1")
-                arrives("D1", up, "DR1")
-                arrives("P0", up, "PR0")
-            else:
-                put_records()
-                dma("y", "outx", [(T.yx[:], T.X[:, 0:WN])], ["X"], [])
-                home()
-                send("P1", up, T.PR1[:], T.PS1[:], ["PS1"])
-                arrives("P1", down, "PR1")
-                put_far()
-                dma("y", "outa", [(T.ya[:], T.OA[0:128:16, 0:WN])], ["OA"], [])
-                near_update(1, "OB")
-                dma("y", "outb", [(T.yb[:], T.OB[0:128:16, 0:WN])], ["OB"], [])
+                iota(T.PB[:, 1:WN:16], "PB", [[0, 256]], 0)
+                plain_in("FB", 1)
+                extra += [lambda: near_update(0, "FA"), lambda: plain_in("FA", 0)]
+            if (t, d) == (1, 1):
+                extra += [lambda: plain_out(0), lambda: plain_out(1)]
+            z, zr = (T["SR%d" % t], ["SR%d" % t]) if d == 0 else (T.zb, ["zb0", "zb1"])
+            call = step(t, d, z, zr, far)
+            call["extra"] = lambda: [f() for f in extra]
+            for w in (ORDER + " " + (NEXT if d < STEPS - 1 else END[t])).split():
+                calls = call
+                if w[0] == "<":
+                    calls, w = before_, w[1:]
+                    if d == 0:
+                        continue
+                if w in calls:
+                    calls[w]()
+                else:
+                    calls[w[0]](*[int(x) for x in w[1:].split(".")])
+            before_ = call
     for sem in sorted(count):
         wait("g", [("", sem, count[sem])])

@@ -6,16 +6,16 @@ WD = 4352
 STEPS = 3
 CHUNKS = ((8, (("s", 8), ("c", 8), ("s", 8), ("c", 8))),
           (8, (("s", 8), ("s", 8), ("s", 8), ("s", 4), ("s", 4))))
-PORT = ((0, 64, "pr", "pk0"), (64, 192, "pk1", "ph"), (192, 512, "z1a", "z1b"))
-ORDER = """hash Z0 <x1 u Y0 W0 E0 h0 N0 W1 T0 h1 L0 G0 E1 h2 N1 T1 W2 L1 G2 E2 V1.0 N2 T2 O0 last A0 V1.1 L2 R1 G4 X0 M0 A2
-           V3.0 V3.1 M1 Z1 R3 G5 c16 X2 M2 bar M3 B0 C0 O1 B1 A4 extra X4 H0 G6 F0 P0 A5 M4 X5 Q0 G7 G8 U0 f0
-           A6 M5 X6 X7 A7.8 M6 X8 M7.8 C1 P1"""
-NEXT = "r0 H1 F1 Q1 U1 count f1 fp kappa tb x0 lt ahead won pl dead r1 z"
-END = ("x0 H1 F1 Q1 U1 x1 starts count f1 kappa ahead won home flags whole",
-       "x0 H1 F1 Q1 U1 won home x1 outx outa outb")
+PORT = ((0, 64, "pr", None), (64, 192, "pk1", None), (192, 512, "z1a", "z1b"))
+ORDER = """hash <won <dead Z0 u Y0 h0 W0 D0.0 W1 D0.1 D0.2 G0 D1.0 h1 D1.1 D1.2 G2 h2 W2 V1.0 N2 V1.1 E2 O0 last T2 L2 R1 A0 X0
+           V3.0 O1 Z1 M1 A2 V3.1 X2 c16 G4 M0 extra R3 M2 M3 bar B0 C0.3 A4 G5 G6 X4 B1 A5 G7 M4 H0 P0 K0 X5 A6 Q0
+           X6 J0 M5 X7 G8 X8 U0 f0 M6 C4.6 A7.8 M7.8 C7.8 P1"""
+NEXT = "x0 H1 J1 K1 Q1 U1 count f1 r0 fp x1 kappa ahead pl r1 tb z lt"
+END = ("x0 H1 J1 K1 Q1 U1 x1 starts count f1 won home kappa ahead flags whole",
+       "x0 H1 J1 K1 Q1 U1 won home x1 outx outa outb")
 WIDE = 192
 ZS = 8
-ZP = 512
+ZP = (512, 128)
 FRAC = 1.0 / 16384
 NC = len(CHUNKS)
 START = [sum(c[0] for c in CHUNKS[:k]) for k in range(NC + 1)]
@@ -28,18 +28,18 @@ for _n, _c, _d in (
         ("zb", 256, "bfloat16"), ("zp", 1024, "bfloat16"),
         ("pai", 256, "int32"), ("pbi", 256, "int32"), ("wti", 1, "int32"), ("wf", 1, "float32"), ("wg", 1, "float32"),
         ("pidx", 1, "int32"), ("pmi", 1, "int32"), ("pgi", 1, "int32"), ("poi", 1, "int32"), ("kc", 24, "float32"),
-        ("col", 512, "float32"), ("colL", 512, "bfloat16"), ("colJ", 512, "bfloat16"), ("colg", 128, "bfloat16"), ("coll", 256, "bfloat16"),
-        ("SEL", 2048, "bfloat16"), ("hi", 256, "bfloat16"), ("lo", 256, "bfloat16"), ("FR", 512, "float16"), ("cf", 256, "float32"), ("cp0", 256, "float32"), ("cp1", 256, "float32"),
+        ("col", 256, "float32"), ("colL", 512, "bfloat16"), ("colJ", 512, "bfloat16"), ("colg", 128, "bfloat16"), ("coll", 256, "bfloat16"),
+        ("SEL", 2048, "bfloat16"), ("hi", 256, "bfloat16"), ("lo", 256, "float16"), ("cf", 256, "float32"), ("cp0", 256, "float32"), ("cp1", 256, "float32"),
         ("TD", 32, "float32"), ("TE", 32, "float32"), ("colb", 144, "bfloat16"),
-        ("E8", 144, "bfloat16"), ("E4n", 144, "bfloat16"), ("E4", 144, "bfloat16"), ("WG", 8, "float16"), ("GS", 8, "bfloat16"), ("CK", 2, "float32"),
-        ("I16", 128, "float16"), ("IB", 128, "bfloat16"), ("I32", 128, "float32"), ("INB", 128, "bfloat16"), ("IBAR", 128, "bfloat16"),
-        ("BO", 128, "bfloat16"), ("TRI", 128, "bfloat16"), ("ONE", 512, "bfloat16"), ("MH", 144, "bfloat16"),
+        ("E8", 144, "bfloat16"), ("E4n", 144, "bfloat16"), ("E4", 144, "bfloat16"), ("WG", 16, "float16"), ("ZT", 144, "float16"), ("CK", 2, "float32"),
+        ("I16", 128, "float16"), ("IB", 128, "bfloat16"), ("IB2", 128, "bfloat16"), ("INB", 128, "bfloat16"), ("IBAR", 128, "bfloat16"),
+        ("BO", 128, "bfloat16"), ("TRI", 128, "bfloat16"), ("ONE", 512, "bfloat16"),
         ("OFFB", 256, "bfloat16"), ("SEG", 256, "float32"), ("DX", 256, "bfloat16"), ("DY", 256, "bfloat16"),
         ("RH", 512, "bfloat16"), ("RQ", 512, "float32"), ("RU", 512, "bfloat16"), ("RZ", 512, "bfloat16"), ("RO", 512, "bfloat16"), ("KT", 128, "bfloat16"),
         ("vr0", 256, "float32"), ("vs0", 256, "float32"), ("vs1", 256, "float32"),
-        ("ri", 128, "int32"), ("hm", 128, "int32"), ("HT", 128, "float16"), ("UF", 128, "float32"), ("UZ", 128, "float16"), ("SQ", 128, "float32"), ("LT", 128, "float16"), ("TB", 16, "float16"),
+        ("li", 192, "int32"), ("lj", 192, "int32"), ("ri", 128, "int32"), ("hm", 128, "int32"), ("HT", 128, "float16"), ("UF", 128, "float32"), ("UZ", 128, "float16"), ("SQ", 128, "float32"), ("LT", 128, "float16"), ("TB", 16, "float16"),
         ("RR", 512, "bfloat16"), ("LST", 512, "uint16"), ("c16", 512, "float16"), ("bar", 512, "bfloat16"),
-        ("ym", 16, "int32"), ("y", 16, "int32"), ("yc", 16, "float32"), ("yl", 16, "uint16"), ("FG", 256, "float32"), ("FP", 256, "float32"),
+        ("ym", 16, "int32"), ("y", 16, "int32"), ("yc", 16, "float32"), ("yl", 16, "uint16"), ("FG", 256, "float16"), ("FP", 256, "float32"),
         ("XG", 256, "bfloat16"), ("qs", 256, "float32"), ("ps", 256, "float32"), ("EQ", 2176, "bfloat16"),
         ("pl16", 16, "uint16"), ("DD", 16, "bfloat16"), ("PL", 16, "float32"), ("PLl", 16, "uint16"), ("wb", 16, "float32"),
         ("k0", 1, "float32"), ("k1", 1, "float32"), ("kr", 1, "float32"), ("kf", 1, "float32")):
@@ -54,7 +54,7 @@ for _t in range(2):
 SCRATCH["fad"] = ("dram", [8, WN], "float32")
 PSUM = ("z0a", "z0b", "z1a", "z1b", "pk0", "pk1", "ph", "pr")
 SCRATCH["acc"] = ("psum", [128, 512 * len(PSUM)], "float32")
-PARTS = tuple("SEL%d" % _i for _i in range(8)) + ("RO", "RZ", "MH", "colL", "colJ", "FB", "TD", "IO")
+PARTS = tuple("SEL%d" % _i for _i in range(8)) + ("RZ", "ZTc", "colL", "colJ", "FB", "TD", "IO")
 
 MSG = []
 for _t in range(2):
@@ -190,59 +190,61 @@ def rank_program(g, core, T, topo):
 
     dma("s", "lda", [(T.pai[:], T.pa[:])], [], ["pai"])
     dma("y", "ldb", [(T.pbi[:], T.pb[:])], [], ["pbi"])
+    dma("s", "ldw", [(T.wti[:], T.wt[:])], [], ["wti"])
     dma("s", "ldx", [(T.X[:, 0:WN], T.x[:])], [], ["X"])
-    dma("y", "ldw", [(T.wti[:], T.wt[:])], [], ["wti"])
 
     iota(T.pidx[:], "pidx", [[0, 1]], 0, 1, True)
     iota(T.colg[:], "colg", [[16, 8], [0, 16]], 0)
-    iota(T.col[:], "col", [[1, 512]], 0)
+    iota(T.col[:], "col", [[1, 256]], 0)
     for k, (nl, _) in enumerate(CHUNKS):
         iota(T.colL[:, 32 * START[k]:32 * START[k + 1]], "colL", [[0, 32], [1, nl]], START[k])
     pid, pm, pg16, pg, pg15, ev, od, p32, pf, up20, dn20, nd20, pm1, dc, one, r16, r17, rs, rv = [T.kc[:, i:i + 1] for i in range(19)]
     fill(T.ONE[:], "ONE", 1.0)
-    fill(T.MH[:, 128:144], "MH", 0.0)
-    fill(T.MH[:, 0:128], "MH", -0.5)
     ts(T.pmi[:], ["pmi"], T.pidx[:], ["pidx"], 15, OP.bitwise_and)
     ts(T.poi[:], ["poi"], T.pidx[:], ["pidx"], 16, OP.bitwise_and)
     ts(T.pgi[:], ["pgi"], T.pidx[:], ["pidx"], 4, OP.arith_shift_right)
     cp(pid, ["pid"], T.pidx[:], ["pidx"])
     cp(pm, ["pm"], T.pmi[:], ["pmi"])
     cp(pg, ["pg"], T.pgi[:], ["pgi"])
-    ts(od, ["od"], T.poi[:], ["poi"], -1.0 / 16, OP.mult)
-    ts(ev, ["ev"], T.poi[:], ["poi"], 1.0 / 16, OP.mult, -1.0, OP.add)
+    ts(od, ["od"], T.poi[:], ["poi"], -512.0, OP.mult)
+    ts(ev, ["ev"], T.poi[:], ["poi"], 512.0, OP.mult, -8192.0, OP.add)
     def selectors(a, b):
         for m in range(a, b):
             ts(T.SEL[:, 128 * m:128 * m + 128], ["SEL%d" % (m // 2)], T.colg[:], ["colg", "pid"], float(m), OP.add, pid, OP.is_equal)
 
     selectors(0, 4)
-    ts(T.FR[0:1, :], ["FR"], T.col[0:1, :], ["col"], FRAC, OP.mult)
+    ts(T.pmi[:], ["pmi"], T.pidx[:], ["pidx"], 7, OP.bitwise_and)
+    ts(pf, ["pf"], T.pmi[:], ["pmi"], 256 * FRAC, OP.mult, 1.0, OP.add)
+    ts(T.cf[:], ["cf"], T.col[:, 0:256], ["col", "pf"], FRAC, OP.mult, pf, OP.add)
     act(T.FB[:, WN:WD], ["FBd"], T.ONE[:, 0:256], ["ONE"], AF.Silu, scale=2.0)
-    ts(T.hi[:], ["hi"], T.pbi[:], ["pbi"], 805306368.0, OP.add, -805306368.0, OP.add)
     ts(pg16, ["pg16"], pg, ["pg"], 16.0, OP.mult)
-    tt(T.lo[:], ["lo"], T.pbi[:], T.hi[:], ["pbi", "hi"], OP.subtract)
-    selectors(4, 8)
-
-    ts(T.TD[:, 0:16], ["TD"], T.pai[:, 0:256:16], ["pai", "ev"], 0.5, OP.add, ev, OP.mult)
-    ts(T.TD[:, 16:32], ["TD"], T.pai[:, 0:256:16], ["pai", "od"], 0.5, OP.add, od, OP.mult)
     ts(pg15, ["pg15"], pg, ["pg"], 16.0, OP.mult, 15.0, OP.add)
-    op("v", g.vector.transpose, ["TD"], ["TE"], out=T.TE[:], in_=T.TD[:])
     cp(T.colb[:], ["colb"], T.col[:, 0:144], ["col"])
-    tt(T.DS0[:], ["DS0"], T.TE[:, 0:16], T.TE[:, 16:32], ["TE"], OP.add)
-    send("D0", up, T.DR0[:], T.DS0[:], ["DS0"])
-    arrives("D0", down, "DR0")
-    ts(p32, ["p32"], pid, ["pid"], -32.0, OP.add)
-    selectors(8, 16)
+    selectors(4, 8)
     for k, (nl, _) in enumerate(CHUNKS):
         iota(T.colJ[:, 32 * START[k]:32 * START[k + 1]], "colJ", [[8192, 32], [0, nl]], 129 * 4096)
 
+    ts(T.TD[:, 0:16], ["TD"], T.pai[:, 0:256:16], ["pai", "ev"], 0.5, OP.add, ev, OP.mult)
+    ts(T.TD[:, 16:32], ["TD"], T.pai[:, 0:256:16], ["pai", "od"], 0.5, OP.add, od, OP.mult)
+    selectors(8, 10)
+    op("v", g.vector.transpose, ["TD"], ["TE"], out=T.TE[:], in_=T.TD[:])
+    selectors(10, 12)
+    tt(T.DS0[:], ["DS0"], T.TE[:, 0:16], T.TE[:, 16:32], ["TE"], OP.add)
+    send("D0", up, T.DR0[:], T.DS0[:], ["DS0"])
+    arrives("D0", down, "DR0")
+    tt(T.cp1[:], ["cp1"], T.pbi[:], T.cf[:], ["pbi", "cf"], OP.add)
+    ts(T.hi[:], ["hi"], T.pbi[:], ["pbi"], 805306368.0, OP.add, -805306368.0, OP.add)
+    tt(T.lo[:], ["lo"], T.cp1[:], T.hi[:], ["cp1", "hi"], OP.subtract)
+    selectors(12, 16)
+    iota(T.coll[:], "coll", [[0, 16], [1, 16]], 0)
+
     def spread_b(i):
-        bank = PSUM[i % 6]
-        mm(ps(bank, 0, 512), [bank], T.ONE[0:1, 0:128], T.FR[0:1, :], ["ONE", "FR"], True, False)
+        bank = ("z0a", "pk0", "z0b")[i % 3]
         for h in range(2):
             m = 2 * i + h
-            mm(ps(bank, 256 * h, 256 * h + 256), [bank], T.SEL[:, 128 * m:128 * m + 128], T.lo[:], ["SEL%d" % i, "lo"], False, False)
-            mm(ps(bank, 256 * h, 256 * h + 256), [bank], T.SEL[:, 128 * m:128 * m + 128], T.hi[:], ["SEL%d" % i, "hi"], False, h == 1)
-        act(T.FB[:, 512 * i:512 * i + 512], ["FB"], ps(bank, 0, 512), [bank], AF.Copy, bias=1.0 + 512 * i * FRAC)
+            mm(ps(bank, 256 * h, 256 * h + 256), [bank], T.SEL[:, 128 * m:128 * m + 128], T.hi[:], ["SEL%d" % i, "hi"], True, False)
+            mm(ps(bank, 256 * h, 256 * h + 256), [bank], T.SEL[:, 128 * m:128 * m + 128], T.lo[:], ["SEL%d" % i, "lo"], False, True)
+        act(T.FB[:, 512 * i:512 * i + 512], ["FB"], ps(bank, 0, 512), [bank], AF.Copy, bias=2048 * (i // 4 - 1) * FRAC)
 
     def send_starts(t, dst):
         act(T["SS%d" % t][:], ["SS%d" % t], T.X[:, t:WN:16], ["X"], AF.Copy)
@@ -251,16 +253,17 @@ def rank_program(g, core, T, topo):
     def send_all(t, dst):
         send("B%d" % t, dst, T["XR%d" % t][:, 0:WN], T.X[:, 0:WN], ["X"])
 
-    for i in range(8):
+    for i in range(4):
         if i == 2:
             send_starts(0, up)
             send_all(0, up)
         spread_b(i)
     arrives("S0", down, "SR0")
     arrives("B0", down, "XR0")
-    iota(T.coll[:], "coll", [[0, 16], [1, 16]], 0)
-    iota(T.SEG[:], "SEG", [[0, 256]], -4)
+    iota(T.SEG[:], "SEG", [[0, 256]], -8192)
     iota(T.X[:, WN:WD], "Xd", [[0, 256]], 0)
+    iota(one, "one", [[0, 1]], 1)
+    iota(T.PL[:], "PL", [[0, 16]], 8192)
     for t in range(2):
         iota(T["vs%d" % t][:], "vs%d" % t, [[16, 256]], t + 1)
     iota(T.vr0[:], "vr0", [[16, 256]], 1)
@@ -268,59 +271,58 @@ def rank_program(g, core, T, topo):
     iota(T.IO[:, WN + 1:WD + 8], "IO", [[0, WD + 7 - WN]], 0)
 
     cp(T.wf[:], ["wf"], T.wti[:], ["wti"])
-    ts(T.GS[:], ["GS"], T.col[:, 0:8], ["col", "pg"], pg, OP.is_equal, 1.0 / 4096, OP.mult)
+    ts(T.WG[:, 8:16], ["GS"], T.col[:, 0:8], ["col", "pg"], pg, OP.is_equal, 1.0 / 4096, OP.mult)
+    ts(T.ZT[:], ["ZTc"], T.ONE[:, 0:144], ["ONE"], -0.5, OP.mult)
     ts(T.wg[:], ["wg"], T.wf[:], ["wf"], 2048.0, OP.is_gt, -4096.0, OP.mult)
     fill(T.KT[:], "KTc", 3.0 / 32)
     tt(T.wg[:], ["wg"], T.wg[:], T.wf[:], ["wg", "wf"], OP.add)
     ts(T.RH[:], ["RH"], T.colL[:], ["colL", "pid"], pid, OP.is_equal)
-    ts(T.WG[:], ["WG"], T.GS[:], ["GS", "wg"], T.wg[:], OP.mult)
+    ts(T.WG[:, 0:8], ["WG"], T.WG[:, 8:16], ["GS", "wg"], T.wg[:], OP.mult)
     fill(T.KT[0:1, :], "KT", 0.0, ["KTc"])
     ts(T.RQ[:, 0:WIDE], ["RQ"], T.RH[:, 0:WIDE], ["RH"], 524288.0, OP.mult)
-    for nm, val in (("IB", 1.0), ("INB", -1.0), ("I16", 1.0), ("IBAR", 16777216.0), ("I32", 1.0)):
+    for nm, val in (("IB", 1.0), ("INB", -1.0), ("I16", 1.0), ("IBAR", 16777216.0), ("IB2", 2.0)):
         ts(T[nm][:], [nm], T.colb[:, 0:128], ["colb", "pid"], pid, OP.is_equal, val, OP.mult)
     tt(T.RU[:], ["RU"], T.colJ[:], T.RH[:], ["colJ", "RH"], OP.mult)
     for nm, val in (("E8", 8192.0), ("E4n", -4096.0), ("E4", 4096.0)):
         ts(T[nm][:], [nm], T.colb[:], ["colb", "pg15"], pg15, OP.is_equal, val, OP.mult)
     ts(r17, ["r17"], pid, ["pid"], 17.0, OP.is_equal, -69632.0, OP.mult)
     ts(r16, ["r16"], pid, ["pid"], 16.0, OP.is_equal, 16777216.0, OP.mult)
-    ts(T.RO[:], ["RO"], T.colL[:], ["colL", "p32"], p32, OP.is_equal, -16777216.0, OP.mult)
     ts(rs, ["rs"], r16, ["r16", "r17"], 3.0, OP.mult, r17, OP.add)
     ts(rv, ["rv"], r16, ["r16", "r17"], 2.0, OP.mult, r17, OP.add)
     for eng, c0, c1 in runs:
-        ts(T.RZ[:, c0:c1], ["RZ"], T.RO[:, c0:c1], ["RO", "rs", "rv"], float(eng == "s"), OP.mult, rs if eng == "s" else rv, OP.add)
-    ts(T.BO[:], ["BO"], T.colg[:], ["colg", "pg16"], pg16, OP.is_equal)
+        ts(T.RZ[:, c0:c1], ["RZ"], T.RH[:, c0:c1], ["RH", "rs", "rv"], -16777216.0 * (eng == "s"), OP.mult, rs if eng == "s" else rv, OP.add)
+    ts(T.BO[:], ["BO"], T.colg[:], ["colg", "pg16"], pg16, OP.is_equal, 8192.0, OP.mult)
     ts(T.TRI[:], ["TRI"], T.coll[:, 0:128], ["coll", "pm"], pm, OP.is_gt)
-    ts(T.OFFB[:], ["OFFB"], T.coll[:], ["coll", "pm"], pm, OP.not_equal, 4.0, OP.mult)
-    ts(dc, ["dc"], pm, ["pm"], float(WN), OP.add, FRAC, OP.mult)
+    ts(T.OFFB[:], ["OFFB"], T.coll[:], ["coll", "pm"], pm, OP.not_equal, 8192.0, OP.mult)
+    ts(dc, ["dc"], pm, ["pm"], WN - 2048.0, OP.add)
     tt(T.TRI[:], ["TRI"], T.TRI[:], T.BO[:], ["TRI", "BO"], OP.mult)
-    ts(T.SEG[:, 0:256:16], ["SEG"], T.col[:, 0:16], ["col", "dc"], 16 * FRAC, OP.mult, dc, OP.add)
+
+    ts(pm1, ["pm1"], pm, ["pm"], 1.0, OP.add)
+    ts(up20, ["up20"], pm, ["pm"], 15.0, OP.is_equal, 1.0 - 2.0 ** -20, OP.mult)
+    fill(T.CK[:, 0:1], "CK0", -15.5 / 128)
+    fill(T.CK[:, 1:2], "CK1", 0.5)
+    ts(T.DY[:], ["DY"], T.coll[:], ["coll", "pm1"], pm1, OP.is_equal, 1048576.0, OP.mult)
+    ts(T.DX[:], ["DX"], T.coll[:], ["coll", "pm"], pm, OP.not_equal)
+    ts(dn20, ["dn20"], up20, ["up20"], 2.0 ** -20, OP.add)
 
     def late_constants():
+        ts(T.SEG[:, 0:256:16], ["SEG"], T.col[:, 0:16], ["col", "dc"], 16.0, OP.mult, dc, OP.add)
         for t, v in enumerate((1.278465, 2.217715)):
             fill(T["vs%d" % t][:, 0:1], "vs%d" % t, v)
-        fill(T.PL[:], "PL", 1.0)
-        fill(T.CK[:, 0:1], "CK0", -15.5 / 128)
-        fill(T.CK[:, 1:2], "CK1", 0.5)
-        fill(one, "one", 1.0)
-        ts(pm1, ["pm1"], pm, ["pm"], 1.0, OP.add)
-        ts(up20, ["up20"], pm, ["pm"], 15.0, OP.is_equal, 1.0 - 2.0 ** -20, OP.mult)
-        ts(T.DY[:], ["DY"], T.coll[:], ["coll", "pm1"], pm1, OP.is_equal, 1048576.0, OP.mult)
-        ts(T.DX[:], ["DX"], T.coll[:], ["coll", "pm"], pm, OP.not_equal)
-        ts(dn20, ["dn20"], up20, ["up20"], 2.0 ** -20, OP.add)
         tt(T.DX[:], ["DX"], T.DX[:], T.DY[:], ["DX", "DY"], OP.max)
-        ts(nd20, ["nd20"], dn20, ["dn20"], -1.0, OP.mult)
+        ts(nd20, ["nd20"], dn20, ["dn20"], -1.0 / FRAC, OP.mult)
 
     def store_a():
-        ts(pf, ["pf"], pm, ["pm"], 256 * FRAC, OP.mult, 1.0, OP.add)
-        ts(T.cf[:], ["cf"], T.col[:, 0:256], ["col", "pf"], FRAC, OP.mult, pf, OP.add)
+        ts(p32, ["p32"], pm, ["pm"], 8.0, OP.is_ge, 2048 * FRAC, OP.mult)
         tt(T.cp0[:], ["cp0"], T.pai[:], T.cf[:], ["pai", "cf"], OP.add)
+        ts(T.cp0[:], ["cp0"], T.cp0[:], ["cp0", "p32"], p32, OP.add, -2048 * FRAC, OP.add)
         dma("y", "sta", [(T.fad[:], T.cp0[:])], ["cp0"], ["fad"])
 
     def spread_a(h):
         dma("y", "ro" + "ab"[h], [(T.FA[m::16, 0:WN], T.fad[:]) for m in range(8 * h, 8 * h + 8)], ["fad", "LST0"], ["FA%d" % h])
 
     def dead(t):
-        ts(T.DD[:], ["DD"], T["DR%d" % t][:], ["DR%d" % t], 0.25, OP.is_lt, float(WN), OP.mult)
+        ts(T.DD[:], ["DD"], T["DR%d" % t][:], ["DR%d" % t], 2047.5, OP.is_lt, float(WN), OP.mult)
 
     def plain_in(tab, i):
         dma("y", "g" + "ab"[i], [(T["cp%d" % i][:], T[tab][0:128:16, 0:WN])], [tab], ["cp%d" % i])
@@ -339,10 +341,10 @@ def rank_program(g, core, T, topo):
         mm(ps(bank, 0, b - a), [bank], T.KT[0:2, :], T.ONE[0:2, a:b], ["KT", "KTc", "ONE"], True, False)
 
     def ahead():
-        mm(ps("ph", 0, 128, 1, 0, 48), ["ph"], T.ONE[0:1, 0:48], T.MH[0:1, 0:128], ["ONE", "MH"], True, False)
+        mm(ps("ph", 0, 256, 1, 0, 16), ["ph"], T.ZT[0:1, 128:144], T.ONE[0:1, 0:256], ["ONE", "ZTc"], True, False)
         for i, (_, _, raw, rest) in enumerate(PORT):
             for bank in (raw, rest):
-                if bank != "ph":
+                if bank not in ("ph", None):
                     begin(i, bank)
 
     win = T.X[:, 0:WN]
@@ -354,9 +356,11 @@ def rank_program(g, core, T, topo):
     def put_far(k, t, d, far):
         act(T[far][:, 0:WD].indirect(parts_of(T["MO%d" % d], k)[1]), [far, far + "d"], T["vs%d" % t][:, 16 * START[k]:16 * START[k + 1]], ["vs%d" % t, "MO%dl%d" % (d, k)], AF.Silu)
 
-    def put_records(k, d):
-        xn, l2, _ = parts_of(T["MO%d" % d], k)
-        cp(T.X[:, 0:WD].indirect(l2), ["X", "Xd"], xn, ["MO%dx%d" % (d, k), "MO%dl%d" % (d, k)])
+    def put_records(d, k, a=0, b=None):
+        n, o = CHUNKS[k][0], MBASE[k]
+        b = b or n
+        mo = T["MO%d" % d]
+        cp(T.X[:, 0:WD].indirect(mo[:, o + 16 * n + a:o + 16 * n + b]), ["X", "Xd"], mo[:, o + 16 * a:o + 16 * b], ["MO%dx%d" % (d, k), "MO%dl%d" % (d, k)])
 
     def put_replica(k, t, d):
         mi = "MI%d%d" % (t, d)
@@ -371,7 +375,7 @@ def rank_program(g, core, T, topo):
     cnt = ps(KB, 0, 1, 1, 0, 1)
 
     def count_pairs():
-        act(T.wb[:], ["wb", "k0"], ends, QS, AF.Sign, bias=0.25 - FRAC / 4, scale=-1.0, accum_out=T.k0[:])
+        act(T.wb[:], ["wb", "k0"], ends, QS, AF.Sign, bias=2047.5, scale=-1.0, accum_out=T.k0[:])
         mm(cnt, [KB], T.CK[:, 0:1], one, ["CK0", "one"], True, False)
         mm(cnt, [KB], T.k0[:], T.CK[:, 1:2], ["k0", "CK1"], False, True)
 
@@ -393,21 +397,21 @@ def rank_program(g, core, T, topo):
                     mm(ps(first, a, b), [zbanks(k)[a // 512]], T.IB[:], z[:, z0 + a - n * i:z0 + b - n * i], ["IB"] + zr, True, True)
 
         def copy_z(k):
-            act(T.zp[:, 0:ZP], ["zp"], ps(zbanks(k)[0], 0, ZP), zbanks(k, ZP), AF.Copy)
+            act(T.zp[:, 0:ZP[k]], ["zp"], ps(zbanks(k)[0], 0, ZP[k]), zbanks(k, ZP[k]), AF.Copy)
 
         def head():
             for l in range(16):
-                mm(ps("ph", l, 128, 16, 0, 16), ["ph"], z[:, l:256:16], T.WG[:], ["WG"] + zr, False, False)
-            for l in range(16):
-                mm(ps("ph", l, 128, 16, 32, 48), ["ph"], z[:, l:256:16], T.GS[:], ["GS"] + zr, False, False)
-            mm(ps("ph", 0, 1, 1, 0, 48), ["ph"], T.ONE[0:1, 0:48], T.MH[0:1, 128:129], ["ONE", "MH"], False, True)
+                mm(ps("ph", l, 256, 16, 0, 16), ["ph"], z[:, l:256:16], T.WG[:], ["WG", "GS"] + zr, False, l == 15)
+            if (t, d) == (0, 0):
+                spread_b(7)
 
         def remainder():
-            x = ps("ph", 0, 128, 1, 0, 48)
-            ts(T.ri[0:48, :], ["ri"], x, ["ph"], 2.0 ** -13, OP.add)
-            tt(T.UF[0:48, :], ["UF"], x, T.ri[0:48, :], ["ph", "ri"], OP.subtract)
+            x = ps("ph", 0, 128, 1, 0, 16)
+            ts(T.ri[0:16, :], ["ri"], x, ["ph"], 2.0 ** -13, OP.add)
+            tt(T.UF[0:16, :], ["UF"], x, T.ri[0:16, :], ["ph", "ri"], OP.subtract)
             act(T.SQ[0:16, :], ["SQ"], T.UF[0:16, :], ["UF"], AF.Square)
-            cp(T.UZ[0:48, :], ["UZ"], T.UF[0:48, :], ["UF"])
+            cp(T.UZ[0:16, :], ["UZ"], T.UF[0:16, :], ["UF"])
+            cp(T.ZT[0:16, 0:128], ["ZT"], ps("ph", 128, 256, 1, 0, 16), ["ph", "ZTc"])
 
         def terms(i, which):
             a, b = PORT[i][:2]
@@ -428,6 +432,15 @@ def rank_program(g, core, T, topo):
             else:
                 ts(T.HT[0:16, :], ["HT"], T.hm[0:16, :], ["hm"], -2048.0, OP.add)
 
+        def direct(i, j):
+            a, b, raw, _ = PORT[i]
+            if j == 0:
+                ts(T.li[:, a:b], ["li%d" % i], ps(raw, 0, b - a), [raw], 2047.5, OP.add)
+            elif j == 1:
+                ts(T.lj[:, a:b], ["lj%d" % i], T.li[:, a:b], ["li%d" % i], 4095, OP.bitwise_and)
+            else:
+                cp(T.LST[:, a:b], ["LST%d" % i], T.lj[:, a:b], ["lj%d" % i])
+
         def near(i):
             a, b, raw, _ = PORT[i]
             ts(T.RR[:, a:b], ["RR%d" % i], ps(raw, 0, b - a), [raw], 51539607552.0, OP.add, -51539607552.0, OP.add)
@@ -447,12 +460,17 @@ def rank_program(g, core, T, topo):
         def subs(i):
             k, eng, c0, c1 = pieces[i]
             nl = CHUNKS[k][0]
-            w = nl * ((64 if eng == "s" else ZP // 16) // nl)
+            w = nl * ((64 if eng == "s" else ZP[k] // 16) // nl)
             return [(c, min(c + w, c1)) for c in range(c0, c1, w)]
 
         def gather_v(i, h):
             c, e = subs(i)[h]
-            tt(T.A[:, 16 * c:16 * e], ["A%d_%d" % (i, h)], win.indirect(T.LST[:, c:e]), T.zp[:, 0:16 * (e - c)], ["X", "zp"] + lst(c, e), OP.subtract)
+            k = pieces[i][0]
+            if ZP[k] == 16 * CHUNKS[k][0]:
+                zz, names = z[:, 16 * START[k]:16 * START[k + 1]], zr
+            else:
+                zz, names = T.zp[:, 0:16 * (e - c)], ["zp"]
+            tt(T.A[:, 16 * c:16 * e], ["A%d_%d" % (i, h)], win.indirect(T.LST[:, c:e]), zz, ["X"] + names + lst(c, e), OP.subtract)
 
         def relu(i):
             k, eng, c0, c1 = pieces[i]
@@ -483,14 +501,16 @@ def rank_program(g, core, T, topo):
             mm(ps(bank, 0, c1 - c0), [bank], lhsT, rhs(c0, c1), r, start, stop)
 
         def open_keys(k):
-            keys(k, T.UZ[0:48, :], lambda a, b: T.RZ[0:48, a:b], ["UZ", "RZ"], start=True)
+            keys(k, T.ZT[0:18, 0:128], lambda a, b: T.RZ[0:18, a:b], ["ZT", "RZ"], start=True)
 
         def bar_keys(k):
             if d > 0:
                 keys(k, T.IBAR[:], lambda a, b: T.bar[:, a:b], ["IBAR", "bar"])
 
-        def close_keys(k):
-            keys(k, T.I16[:], lambda a, b: T.c16[:, a:b], ["I16", "c16"], stop=True)
+        def close_keys(i, j):
+            k, c0, c1 = pieces[i][0], pieces[i][2], pieces[j][3]
+            bank, base = "pk%d" % (k % 2), 32 * START[k]
+            mm(ps(bank, c0 - base, c1 - base), [bank], T.I16[:], T.c16[:, c0:c1], ["I16", "c16"], False, c1 == 32 * START[k + 1])
 
         def places():
             ts(T.c16[:], ["c16"], T.LST[:], lst(0, 512), -2048.0, OP.add)
@@ -515,9 +535,12 @@ def rank_program(g, core, T, topo):
             if k < NC - 1:
                 cp(T.yl[:, a:b], ["yl%d" % k], T.yc[:, a:b], ["yc%d" % k])
 
-        def fetch(k):
+        def fetch_far(k):
             a, b = START[k], START[k + 1]
-            act(T.FG[:, 16 * a:16 * b], ["FG%d" % k], T[far][:, 0:WD].indirect(T.yl[:, a:b]), [far, far + "d", "yl%d" % k], AF.Copy)
+            ts(T.FG[:, 16 * a:16 * b], ["FG%d" % k], T[far][:, 0:WD].indirect(T.yl[:, a:b]), [far, far + "d", "yl%d" % k], 1.0 / FRAC, OP.mult, 4096.0, OP.min)
+
+        def fetch_records(k):
+            a, b = START[k], START[k + 1]
             act(T.XG[:, 16 * a:16 * b], ["XG%d" % k], T.X[:, 0:WD].indirect(T.yl[:, a:b]), ["X", "Xd", "yl%d" % k], AF.Copy)
 
         def prepare(k):
@@ -528,19 +551,17 @@ def rank_program(g, core, T, topo):
             mm(ps(pt, 0, n), [pt], T.IB[:], T["SR%d" % t][:, 16 * a:16 * b], ["IB", "SR%d" % t], True, False)
             if k == NC - 1:
                 for l in range(16):
-                    mm(ps(pq, l, n, 16), [pq], T.IB[:], T.DD[:, a:b], ["IB", "DD"], False, False)
+                    mm(ps(pq, l, n, 16), [pq], T.IB2[:], T.DD[:, a:b], ["IB2", "DD"], False, False)
 
         def compare(k):
             a, b = START[k], START[k + 1]
             n = 16 * (b - a)
             pq, pt = zbanks(k)
-            mm(ps(pq, 0, n), [pq], T.I32[:], T.FG[:, 16 * a:16 * b], ["I32", "FG%d" % k], False, False)
+            mm(ps(pq, 0, n), [pq], T.I16[:], T.FG[:, 16 * a:16 * b], ["I16", "FG%d" % k], False, False)
             base = 0
             for L in range(a, b):
                 w, e, o = 16 * (b - L), "EQ%d" % (L - a), 16 * (L - a)
-                ts(T.EQ[:, base:base + w], [e], T.FG[:, 16 * L:16 * b], ["FG%d" % k, "yc%d" % k], 1.0 / FRAC, OP.mult, T.yc[:, L:L + 1], OP.is_equal)
-                if L == min(a + 2, b - 1):
-                    mm(ps(pt, 0, n), [pt], T.IB[:], T.XG[:, 16 * a:16 * b], ["IB", "XG%d" % k], False, True)
+                ts(T.EQ[:, base:base + w], [e], T.FG[:, 16 * L:16 * b], ["FG%d" % k, "yc%d" % k], 2048.0, OP.add, T.yc[:, L:L + 1], OP.is_equal)
                 if w > 16:
                     mm(ps(pq, o + 16, n), [pq], T.BO[:], T.EQ[:, base + 16:base + w], ["BO", e], False, False)
                 mm(ps(pq, o, o + 16), [pq], T.TRI[:], T.EQ[:, base:base + 16], ["TRI", e], False, L == b - 1)
@@ -551,9 +572,10 @@ def rank_program(g, core, T, topo):
             n = 16 * (b - a)
             pq, pt = zbanks(k)
             xn, l2, whole = parts_of(T[mo], k)
+            mm(ps(pt, 0, n), [pt], T.IB[:], T.XG[:, 16 * a:16 * b], ["IB", "XG%d" % k], False, True)
+            scan(T.qs[:, 16 * a:16 * b], ["qs%d" % k], T.SEG[:, 16 * a:16 * b], ps(pq, 0, n), ["SEG", pq], -8192.0, OP.max, OP.min)
             ts(xn, ["%sx%d" % (mo, k)], ps(pt, 0, n), [pt], 0.5, OP.mult, -0.25, OP.add)
-            scan(T.qs[:, 16 * a:16 * b], ["qs%d" % k], T.SEG[:, 16 * a:16 * b], ps(pq, 0, n), ["SEG", pq], 0.0, OP.max, OP.min)
-            ts(l2, ["%sl%d" % (mo, k)], T.qs[:, 16 * a + 15:16 * b:16], ["qs%d" % k], 1.0 / FRAC, OP.mult)
+            ts(l2, ["%sl%d" % (mo, k)], T.qs[:, 16 * a + 15:16 * b:16], ["qs%d" % k], 2048.0, OP.add)
             if d < STEPS - 1:
                 send("M%d%d%d" % (t, d, k), up if t == 0 else down, parts_of(T["MI%d%d" % (t, d)], k)[2], whole, ["%sx%d" % (mo, k), "%sl%d" % (mo, k)])
 
@@ -585,13 +607,13 @@ def rank_program(g, core, T, topo):
                 tt(T.PL[:], ["PL"], T.PL[:], ends, ["PL"] + QS, OP.min)
 
         def home():
-            ts(T["PS%d" % t][:], ["PS%d" % t], T[dr][:], [dr], 1.0 / FRAC, OP.mult, 1.0, OP.add)
+            ts(T["PS%d" % t][:], ["PS%d" % t], T[dr][:], [dr], 2049.0, OP.add)
             send("P%d" % t, down if t == 0 else up, T["PR%d" % t][:], T["PS%d" % t][:], ["PS%d" % t])
             arrives("P%d" % t, up if t == 0 else down, "PR%d" % t)
 
         def flags():
             scan(T.ps[:], ["ps"], T.DX[:], T.FB[:, 1:WN:16], ["DX", "FB"], 0.0, OP.mult, OP.add)
-            ts(T.DS1[:], ["DS1"], T.ps[:, 15:256:16], ["ps", "nd20"], nd20, OP.mult, 0.75, OP.add)
+            ts(T.DS1[:], ["DS1"], T.ps[:, 15:256:16], ["ps", "nd20"], nd20, OP.mult, 8192.0, OP.add)
             send("D1", down, T.DR1[:], T.DS1[:], ["DS1"])
             arrives("D1", up, "DR1")
 
@@ -604,7 +626,7 @@ def rank_program(g, core, T, topo):
             arrives("B1", up, "XR1")
 
         def out_a():
-            ts(T.PLl[:], ["PLl"], T.PL[:], ["PL"], 1.0 / FRAC, OP.mult)
+            ts(T.PLl[:], ["PLl"], T.PL[:], ["PL"], 2048.0, OP.add)
             cp(T.PA[:, 0:WD].indirect(T.PLl[:]), ["PA"], T.vr0[:], ["vr0", "PLl"])
             dma("s", "outa", [(T.ya[:], T.PA[0:128:16, 0:WN])], ["PA"], [])
 
@@ -612,17 +634,19 @@ def rank_program(g, core, T, topo):
             near_update(1, "PB")
             dma("s", "outb", [(T.yb[:], T.PB[0:128:16, 0:WN])], ["PB"], [])
 
-        return {"x": lambda k: put_records(k, d), "r": lambda k: put_replica(k, t, d), "f": lambda k: put_far(k, t, d, far),
+        return {"x": lambda *k: put_records(d, *k), "r": lambda k: put_replica(k, t, d), "f": lambda k: put_far(k, t, d, far),
                 "fp": partners, "pl": own_column, "tb": turn, "lt": turned, "z": next_z, "won": paired, "dead": lambda: dead(t),
                 "kappa": lambda: kappa(97 * (d + 1) % (97 * STEPS)), "ahead": ahead, "home": home, "flags": flags, "starts": starts, "whole": whole,
                 "outx": lambda: dma("y", "outx", [(T.yx[:], T.X[:, 0:WN])], ["X"], []), "outa": out_a, "outb": out_b,
                 "W": lambda i: terms(i, 2), "E": lambda i: terms(i, 3), "N": near, "T": take, "L": lists, "G": gather, "V": gather_v, "R": relu,
                 "count": count_pairs, "X": maxima, "A": lambda *i: sums("A", *i), "M": lambda *i: sums("M", *i), "O": open_keys, "B": bar_keys, "C": close_keys,
-                "Z": spread_z, "Y": copy_z, "H": choose, "F": fetch, "P": prepare, "Q": compare, "U": settle,
-                "h": short_h, "hash": head, "u": remainder, "c16": places, "last": old_places, "bar": barred}
+                "Z": spread_z, "Y": copy_z, "H": choose, "P": prepare, "Q": compare, "U": settle,
+                "D": direct, "K": fetch_far, "J": fetch_records, "h": short_h, "hash": head, "u": remainder, "c16": places, "last": old_places, "bar": barred}
 
     before_ = None
     ahead()
+    for i in range(4, 7):
+        spread_b(i)
     for t in range(2):
         far = "FB" if t == 0 else "FA"
         for d in range(STEPS):

from concourse.mybir import AluOpType as OP, AxisListType, ActivationFunctionType as AF

N = 5
WN = 4096
WD = 4352
STEPS = 3
CHUNKS = ((8, (("s", 8), ("c", 8), ("s", 8), ("c", 8))),
          (8, (("s", 8), ("s", 8), ("s", 8), ("s", 4), ("s", 4))))
PORT = ((0, 64, "pr", None), (64, 192, "pk1", None), (192, 512, "z1a", "z1b"))
ORDER = """hash <won <dead Z0 u Y0 h0 W0 D0.0 W1 D0.1 D0.2 G0 D1.0 h1 D1.1 D1.2 G2 h2 W2 V1.0 N2 V1.1 E2 O0 last T2 L2 R1 A0 X0
           V3.0 O1 Z1 M1 A2 V3.1 X2 c16 G4 M0 extra R3 M2 M3 bar B0 C0.3 A4 G5 G6 X4 B1 A5 G7 M4 H0 P0 K0 X5 A6 Q0
           X6 J0 M5 X7 G8 X8 U0 f0 M6 C4.6 A7.8 M7.8 C7.8 P1"""
NEXT = "x0 H1 J1 K1 Q1 U1 count f1 r0 fp x1 kappa ahead pl r1 tb z lt"
END = ("x0 H1 J1 K1 Q1 U1 x1 starts count f1 won home kappa ahead flags whole",
       "x0 H1 J1 K1 Q1 U1 won home x1 outx outa outb")
WIDE = 192
ZS = 8
ZP = (512, 128)
FRAC = 1.0 / 16384
NC = len(CHUNKS)
START = [sum(c[0] for c in CHUNKS[:k]) for k in range(NC + 1)]
MBASE = [sum(16 * c[0] + 8 * ((c[0] + 7) // 8) for c in CHUNKS[:k]) for k in range(NC + 1)]

SCRATCH = {}
for _n, _c, _d in (
        ("X", WD, "bfloat16"), ("XR0", WD, "bfloat16"), ("XR1", WD, "bfloat16"), ("FA", WD, "float32"), ("FB", WD, "float32"),
        ("PA", WD, "float32"), ("PB", WN, "float32"), ("IO", WD + 8, "float32"), ("A", 8192, "bfloat16"), ("M", 8192, "bfloat16"),
        ("zb", 256, "bfloat16"), ("zp", 1024, "bfloat16"),
        ("pai", 256, "int32"), ("pbi", 256, "int32"), ("wti", 1, "int32"), ("wf", 1, "float32"), ("wg", 1, "float32"),
        ("pidx", 1, "int32"), ("pmi", 1, "int32"), ("pgi", 1, "int32"), ("poi", 1, "int32"), ("kc", 24, "float32"),
        ("col", 256, "float32"), ("colL", 512, "bfloat16"), ("colJ", 512, "bfloat16"), ("colg", 128, "bfloat16"), ("coll", 256, "bfloat16"),
        ("SEL", 2048, "bfloat16"), ("hi", 256, "bfloat16"), ("lo", 256, "float16"), ("cf", 256, "float32"), ("cp0", 256, "float32"), ("cp1", 256, "float32"),
        ("TD", 32, "float32"), ("TE", 32, "float32"), ("colb", 144, "bfloat16"),
        ("E8", 144, "bfloat16"), ("E4n", 144, "bfloat16"), ("E4", 144, "bfloat16"), ("WG", 16, "float16"), ("ZT", 144, "float16"), ("CK", 2, "float32"),
        ("I16", 128, "float16"), ("IB", 128, "bfloat16"), ("IB2", 128, "bfloat16"), ("INB", 128, "bfloat16"), ("IBAR", 128, "bfloat16"),
        ("BO", 128, "bfloat16"), ("TRI", 128, "bfloat16"), ("ONE", 512, "bfloat16"),
        ("OFFB", 256, "bfloat16"), ("SEG", 256, "float32"), ("DX", 256, "bfloat16"), ("DY", 256, "bfloat16"),
        ("RH", 512, "bfloat16"), ("RQ", 512, "float32"), ("RU", 512, "bfloat16"), ("RZ", 512, "bfloat16"), ("RO", 512, "bfloat16"), ("KT", 128, "bfloat16"),
        ("vr0", 256, "float32"), ("vs0", 256, "float32"), ("vs1", 256, "float32"),
        ("li", 192, "int32"), ("lj", 192, "int32"), ("ri", 128, "int32"), ("hm", 128, "int32"), ("HT", 128, "float16"), ("UF", 128, "float32"), ("UZ", 128, "float16"), ("SQ", 128, "float32"), ("LT", 128, "float16"), ("TB", 16, "float16"),
        ("RR", 512, "bfloat16"), ("LST", 512, "uint16"), ("c16", 512, "float16"), ("bar", 512, "bfloat16"),
        ("ym", 16, "int32"), ("y", 16, "int32"), ("yc", 16, "float32"), ("yl", 16, "uint16"), ("FG", 256, "float16"), ("FP", 256, "float32"),
        ("XG", 256, "bfloat16"), ("qs", 256, "float32"), ("ps", 256, "float32"), ("EQ", 2176, "bfloat16"),
        ("pl16", 16, "uint16"), ("DD", 16, "bfloat16"), ("PL", 16, "float32"), ("PLl", 16, "uint16"), ("wb", 16, "float32"),
        ("k0", 1, "float32"), ("k1", 1, "float32"), ("kr", 1, "float32"), ("kf", 1, "float32")):
    SCRATCH[_n] = ("sbuf", [128, _c], _d)
for _t in range(2):
    for _n, _c, _d in (("SS", 256, "bfloat16"), ("SR", 256, "bfloat16"), ("DS", 16, "float32"), ("DR", 16, "float32"), ("PS", 16, "uint16"), ("PR", 16, "uint16")):
        SCRATCH["%s%d" % (_n, _t)] = ("sbuf", [128, _c], _d)
    for _s in range(STEPS):
        SCRATCH["MO%d" % _s] = ("sbuf", [128, MBASE[NC]], "uint16")
        if _s < STEPS - 1:
            SCRATCH["MI%d%d" % (_t, _s)] = ("sbuf", [128, MBASE[NC]], "uint16")
SCRATCH["fad"] = ("dram", [8, WN], "float32")
PSUM = ("z0a", "z0b", "z1a", "z1b", "pk0", "pk1", "ph", "pr")
SCRATCH["acc"] = ("psum", [128, 512 * len(PSUM)], "float32")
PARTS = tuple("SEL%d" % _i for _i in range(8)) + ("RZ", "ZTc", "colL", "colJ", "FB", "TD", "IO")

MSG = []
for _t in range(2):
    MSG += ["S%d" % _t, "B%d" % _t, "D%d" % _t, "P%d" % _t]
    for _s in range(STEPS - 1):
        MSG += ["M%d%d%d" % (_t, _s, _k) for _k in range(NC)]
SEMAPHORES = ["cv", "cs", "cp", "cg", "ldx", "ldw", "lda", "ldb", "sta", "roa", "rob", "ga", "gb", "ha", "hb", "outx", "outa", "outb"]
SEMAPHORES += ["a" + m for m in MSG] + ["d" + m for m in MSG]


def rank_program(g, core, T, topo):
    me = T.rank_of(core)
    if me is None:
        return
    queues = {"v": g.vector, "s": g.scalar, "p": g.tensor, "g": g, "y": g.sync}
    csem = {"v": "cv", "s": "cs", "p": "cp", "g": "cg"}
    count, waited, wr, rd = {}, {q: {} for q in queues}, {}, {}

    def wait(q, toks):
        for _, sem, val in toks:
            if waited[q].get(sem, 0) < val:
                waited[q][sem] = val
                queues[q].wait_ge(T.sem[sem], val)

    def before(q, reads, writes):
        toks = []
        for x in reads:
            toks += wr.get(x, [])
            if x in PSUM:
                toks += [k for k in rd.get(x, []) if k[0] != q]
        for x in writes:
            toks += [k for k in wr.get(x, []) if k[0] != q or (q != "p" and x not in PARTS)]
            toks += [k for k in rd.get(x, []) if k[0] != q or (q != "p" and x not in PARTS)]
        best = {}
        for k in toks:
            if k[1] not in best or best[k[1]][2] < k[2]:
                best[k[1]] = k
        wait(q, best.values())

    def after(tok, reads, writes):
        for x in reads:
            if x not in writes:
                rd.setdefault(x, [])
                rd[x] = [k for k in rd[x] if k[1] != tok[1]] + [tok]
        for x in writes:
            wr[x] = [tok]
            rd[x] = []

    def op(q, fn, reads, writes, **kw):
        before(q, reads, writes)
        sem = csem[q]
        fn(**kw).then_inc(T.sem[sem], 1)
        count[sem] = count.get(sem, 0) + 1
        after((q, sem, count[sem]), reads, writes)

    def dma(q, sem, pairs, reads, writes):
        before(q, reads, writes)
        for out, in_ in pairs:
            queues[q].dma_start(out, in_).then_inc(T.sem[sem], 16)
            count[sem] = count.get(sem, 0) + 16
        after(("dma" + sem, sem, count[sem]), reads, writes)

    def send(msg, dst, out, in_, reads):
        before("g", reads, [])
        eng = topo.engines(core, dst)[:8]
        rid, pid, _ = topo.addr(dst)
        g.remote_dma(out, in_, T.sem["a" + msg], T.sem["d" + msg], pid, rid, sum(1 << e for e in eng))
        count["d" + msg] = len(eng)
        after(("rdma" + msg, "d" + msg, len(eng)), reads, [])

    def arrives(msg, src, buf):
        n = len(topo.engines(src, core)[:8])
        count["a" + msg] = n
        after(("arr" + msg, "a" + msg, n), [], [buf])

    def ts(out, w, in0, r, s1, op0, s2=None, op1=None):
        kw = {"out": out, "in0": in0, "scalar1": s1, "scalar2": s2, "op0": op0}
        if op1 is not None:
            kw["op1"] = op1
        op("v", g.vector.tensor_scalar, r, w, **kw)

    def tt(out, w, in0, in1, r, o):
        op("v", g.vector.tensor_tensor, r, w, out=out, in0=in0, in1=in1, op=o)

    def cp(out, w, in_, r):
        op("v", g.vector.tensor_copy, r, w, out=out, in_=in_)

    def mm(out, w, lhsT, rhs, r, start, stop):
        op("p", g.tensor.matmul, r, w, out=out, lhsT=lhsT, rhs=rhs, start=start, stop=stop)

    def act(out, w, in_, r, func, **kw):
        op("s", g.scalar.activation, r, w, out=out, in_=in_, func=func, **kw)

    def scan(out, w, d0, d1, r, init, o0, o1):
        op("v", g.vector.tensor_tensor_scan, r, w, out=out, data0=d0, data1=d1, initial=init, op0=o0, op1=o1)

    def fill(ap, w, c, over=()):
        before("v", over, [w])
        g.vector.memset(ap, c).then_inc(T.sem.cv, 1)
        count["cv"] = count.get("cv", 0) + 1
        after(("v", "cv", count["cv"]), over, [w])

    def iota(out, w, pattern, base, mult=0, whole=False):
        kw = {"out": out, "pattern": pattern, "base": base, "channel_multiplier": mult}
        if not whole:
            kw["allow_small_or_imprecise_dtypes"] = True
        op("g", g.iota, [], [w], **kw)

    def ps(bank, a, b, step=1, p0=0, p1=128):
        o = 512 * PSUM.index(bank)
        return T.acc[p0:p1, o + a:o + b:step]

    def zbanks(k, n=1024):
        return ["z%d%s" % (k % 2, x) for x in "ab"[:(n + 511) // 512]]

    up, down = T.cores[(me + 1) % N], T.cores[(me - 1) % N]

    pieces = []
    for k, (nl, parts) in enumerate(CHUNKS):
        c = 32 * START[k]
        for eng, nj in parts:
            pieces.append((k, eng, c, c + nj * nl))
            c += nj * nl
    runs = []
    for _, eng, c0, c1 in pieces:
        if runs and runs[-1][0] == eng:
            runs[-1][2] = c1
        else:
            runs.append([eng, c0, c1])

    def lst(c0, c1, name="LST"):
        return ["%s%d" % (name, i) for i, p in enumerate(PORT) if p[0] < c1 and c0 < p[1]]

    dma("s", "lda", [(T.pai[:], T.pa[:])], [], ["pai"])
    dma("y", "ldb", [(T.pbi[:], T.pb[:])], [], ["pbi"])
    dma("s", "ldw", [(T.wti[:], T.wt[:])], [], ["wti"])
    dma("s", "ldx", [(T.X[:, 0:WN], T.x[:])], [], ["X"])

    iota(T.pidx[:], "pidx", [[0, 1]], 0, 1, True)
    iota(T.colg[:], "colg", [[16, 8], [0, 16]], 0)
    iota(T.col[:], "col", [[1, 256]], 0)
    for k, (nl, _) in enumerate(CHUNKS):
        iota(T.colL[:, 32 * START[k]:32 * START[k + 1]], "colL", [[0, 32], [1, nl]], START[k])
    pid, pm, pg16, pg, pg15, ev, od, p32, pf, up20, dn20, nd20, pm1, dc, one, r16, r17, rs, rv = [T.kc[:, i:i + 1] for i in range(19)]
    fill(T.ONE[:], "ONE", 1.0)
    ts(T.pmi[:], ["pmi"], T.pidx[:], ["pidx"], 15, OP.bitwise_and)
    ts(T.poi[:], ["poi"], T.pidx[:], ["pidx"], 16, OP.bitwise_and)
    ts(T.pgi[:], ["pgi"], T.pidx[:], ["pidx"], 4, OP.arith_shift_right)
    cp(pid, ["pid"], T.pidx[:], ["pidx"])
    cp(pm, ["pm"], T.pmi[:], ["pmi"])
    cp(pg, ["pg"], T.pgi[:], ["pgi"])
    ts(od, ["od"], T.poi[:], ["poi"], -512.0, OP.mult)
    ts(ev, ["ev"], T.poi[:], ["poi"], 512.0, OP.mult, -8192.0, OP.add)
    def selectors(a, b):
        for m in range(a, b):
            ts(T.SEL[:, 128 * m:128 * m + 128], ["SEL%d" % (m // 2)], T.colg[:], ["colg", "pid"], float(m), OP.add, pid, OP.is_equal)

    selectors(0, 4)
    ts(T.pmi[:], ["pmi"], T.pidx[:], ["pidx"], 7, OP.bitwise_and)
    ts(pf, ["pf"], T.pmi[:], ["pmi"], 256 * FRAC, OP.mult, 1.0, OP.add)
    ts(T.cf[:], ["cf"], T.col[:, 0:256], ["col", "pf"], FRAC, OP.mult, pf, OP.add)
    act(T.FB[:, WN:WD], ["FBd"], T.ONE[:, 0:256], ["ONE"], AF.Silu, scale=2.0)
    ts(pg16, ["pg16"], pg, ["pg"], 16.0, OP.mult)
    ts(pg15, ["pg15"], pg, ["pg"], 16.0, OP.mult, 15.0, OP.add)
    cp(T.colb[:], ["colb"], T.col[:, 0:144], ["col"])
    selectors(4, 8)
    for k, (nl, _) in enumerate(CHUNKS):
        iota(T.colJ[:, 32 * START[k]:32 * START[k + 1]], "colJ", [[8192, 32], [0, nl]], 129 * 4096)

    ts(T.TD[:, 0:16], ["TD"], T.pai[:, 0:256:16], ["pai", "ev"], 0.5, OP.add, ev, OP.mult)
    ts(T.TD[:, 16:32], ["TD"], T.pai[:, 0:256:16], ["pai", "od"], 0.5, OP.add, od, OP.mult)
    selectors(8, 10)
    op("v", g.vector.transpose, ["TD"], ["TE"], out=T.TE[:], in_=T.TD[:])
    selectors(10, 12)
    tt(T.DS0[:], ["DS0"], T.TE[:, 0:16], T.TE[:, 16:32], ["TE"], OP.add)
    send("D0", up, T.DR0[:], T.DS0[:], ["DS0"])
    arrives("D0", down, "DR0")
    tt(T.cp1[:], ["cp1"], T.pbi[:], T.cf[:], ["pbi", "cf"], OP.add)
    ts(T.hi[:], ["hi"], T.pbi[:], ["pbi"], 805306368.0, OP.add, -805306368.0, OP.add)
    tt(T.lo[:], ["lo"], T.cp1[:], T.hi[:], ["cp1", "hi"], OP.subtract)
    selectors(12, 16)
    iota(T.coll[:], "coll", [[0, 16], [1, 16]], 0)

    def spread_b(i):
        bank = ("z0a", "pk0", "z0b")[i % 3]
        for h in range(2):
            m = 2 * i + h
            mm(ps(bank, 256 * h, 256 * h + 256), [bank], T.SEL[:, 128 * m:128 * m + 128], T.hi[:], ["SEL%d" % i, "hi"], True, False)
            mm(ps(bank, 256 * h, 256 * h + 256), [bank], T.SEL[:, 128 * m:128 * m + 128], T.lo[:], ["SEL%d" % i, "lo"], False, True)
        act(T.FB[:, 512 * i:512 * i + 512], ["FB"], ps(bank, 0, 512), [bank], AF.Copy, bias=2048 * (i // 4 - 1) * FRAC)

    def send_starts(t, dst):
        act(T["SS%d" % t][:], ["SS%d" % t], T.X[:, t:WN:16], ["X"], AF.Copy)
        send("S%d" % t, dst, T["SR%d" % t][:], T["SS%d" % t][:], ["SS%d" % t])

    def send_all(t, dst):
        send("B%d" % t, dst, T["XR%d" % t][:, 0:WN], T.X[:, 0:WN], ["X"])

    for i in range(4):
        if i == 2:
            send_starts(0, up)
            send_all(0, up)
        spread_b(i)
    arrives("S0", down, "SR0")
    arrives("B0", down, "XR0")
    iota(T.SEG[:], "SEG", [[0, 256]], -8192)
    iota(T.X[:, WN:WD], "Xd", [[0, 256]], 0)
    iota(one, "one", [[0, 1]], 1)
    iota(T.PL[:], "PL", [[0, 16]], 8192)
    for t in range(2):
        iota(T["vs%d" % t][:], "vs%d" % t, [[16, 256]], t + 1)
    iota(T.vr0[:], "vr0", [[16, 256]], 1)
    iota(T.FA[:, WN:WD], "FAd", [[0, 256]], 1)
    iota(T.IO[:, WN + 1:WD + 8], "IO", [[0, WD + 7 - WN]], 0)

    cp(T.wf[:], ["wf"], T.wti[:], ["wti"])
    ts(T.WG[:, 8:16], ["GS"], T.col[:, 0:8], ["col", "pg"], pg, OP.is_equal, 1.0 / 4096, OP.mult)
    ts(T.ZT[:], ["ZTc"], T.ONE[:, 0:144], ["ONE"], -0.5, OP.mult)
    ts(T.wg[:], ["wg"], T.wf[:], ["wf"], 2048.0, OP.is_gt, -4096.0, OP.mult)
    fill(T.KT[:], "KTc", 3.0 / 32)
    tt(T.wg[:], ["wg"], T.wg[:], T.wf[:], ["wg", "wf"], OP.add)
    ts(T.RH[:], ["RH"], T.colL[:], ["colL", "pid"], pid, OP.is_equal)
    ts(T.WG[:, 0:8], ["WG"], T.WG[:, 8:16], ["GS", "wg"], T.wg[:], OP.mult)
    fill(T.KT[0:1, :], "KT", 0.0, ["KTc"])
    ts(T.RQ[:, 0:WIDE], ["RQ"], T.RH[:, 0:WIDE], ["RH"], 524288.0, OP.mult)
    for nm, val in (("IB", 1.0), ("INB", -1.0), ("I16", 1.0), ("IBAR", 16777216.0), ("IB2", 2.0)):
        ts(T[nm][:], [nm], T.colb[:, 0:128], ["colb", "pid"], pid, OP.is_equal, val, OP.mult)
    tt(T.RU[:], ["RU"], T.colJ[:], T.RH[:], ["colJ", "RH"], OP.mult)
    for nm, val in (("E8", 8192.0), ("E4n", -4096.0), ("E4", 4096.0)):
        ts(T[nm][:], [nm], T.colb[:], ["colb", "pg15"], pg15, OP.is_equal, val, OP.mult)
    ts(r17, ["r17"], pid, ["pid"], 17.0, OP.is_equal, -69632.0, OP.mult)
    ts(r16, ["r16"], pid, ["pid"], 16.0, OP.is_equal, 16777216.0, OP.mult)
    ts(rs, ["rs"], r16, ["r16", "r17"], 3.0, OP.mult, r17, OP.add)
    ts(rv, ["rv"], r16, ["r16", "r17"], 2.0, OP.mult, r17, OP.add)
    for eng, c0, c1 in runs:
        ts(T.RZ[:, c0:c1], ["RZ"], T.RH[:, c0:c1], ["RH", "rs", "rv"], -16777216.0 * (eng == "s"), OP.mult, rs if eng == "s" else rv, OP.add)
    ts(T.BO[:], ["BO"], T.colg[:], ["colg", "pg16"], pg16, OP.is_equal, 8192.0, OP.mult)
    ts(T.TRI[:], ["TRI"], T.coll[:, 0:128], ["coll", "pm"], pm, OP.is_gt)
    ts(T.OFFB[:], ["OFFB"], T.coll[:], ["coll", "pm"], pm, OP.not_equal, 8192.0, OP.mult)
    ts(dc, ["dc"], pm, ["pm"], WN - 2048.0, OP.add)
    tt(T.TRI[:], ["TRI"], T.TRI[:], T.BO[:], ["TRI", "BO"], OP.mult)

    ts(pm1, ["pm1"], pm, ["pm"], 1.0, OP.add)
    ts(up20, ["up20"], pm, ["pm"], 15.0, OP.is_equal, 1.0 - 2.0 ** -20, OP.mult)
    fill(T.CK[:, 0:1], "CK0", -15.5 / 128)
    fill(T.CK[:, 1:2], "CK1", 0.5)
    ts(T.DY[:], ["DY"], T.coll[:], ["coll", "pm1"], pm1, OP.is_equal, 1048576.0, OP.mult)
    ts(T.DX[:], ["DX"], T.coll[:], ["coll", "pm"], pm, OP.not_equal)
    ts(dn20, ["dn20"], up20, ["up20"], 2.0 ** -20, OP.add)

    def late_constants():
        ts(T.SEG[:, 0:256:16], ["SEG"], T.col[:, 0:16], ["col", "dc"], 16.0, OP.mult, dc, OP.add)
        for t, v in enumerate((1.278465, 2.217715)):
            fill(T["vs%d" % t][:, 0:1], "vs%d" % t, v)
        tt(T.DX[:], ["DX"], T.DX[:], T.DY[:], ["DX", "DY"], OP.max)
        ts(nd20, ["nd20"], dn20, ["dn20"], -1.0 / FRAC, OP.mult)

    def store_a():
        ts(p32, ["p32"], pm, ["pm"], 8.0, OP.is_ge, 2048 * FRAC, OP.mult)
        tt(T.cp0[:], ["cp0"], T.pai[:], T.cf[:], ["pai", "cf"], OP.add)
        ts(T.cp0[:], ["cp0"], T.cp0[:], ["cp0", "p32"], p32, OP.add, -2048 * FRAC, OP.add)
        dma("y", "sta", [(T.fad[:], T.cp0[:])], ["cp0"], ["fad"])

    def spread_a(h):
        dma("y", "ro" + "ab"[h], [(T.FA[m::16, 0:WN], T.fad[:]) for m in range(8 * h, 8 * h + 8)], ["fad", "LST0"], ["FA%d" % h])

    def dead(t):
        ts(T.DD[:], ["DD"], T["DR%d" % t][:], ["DR%d" % t], 2047.5, OP.is_lt, float(WN), OP.mult)

    def plain_in(tab, i):
        dma("y", "g" + "ab"[i], [(T["cp%d" % i][:], T[tab][0:128:16, 0:WN])], [tab], ["cp%d" % i])

    def plain_out(i):
        c = "cp%d" % i
        ts(T[c][:], [c], T[c][:], [c], 12582912.0, OP.add, -12582913.0, OP.add)
        dma("y", "h" + "ab"[i], [(T["P" + "AB"[i]][0:128:16, 0:WN], T[c][:])], [c], ["P" + "AB"[i]])

    def near_update(t, tab):
        own = T[tab][:, t:WN:16]
        tt(own, [tab], T.IO[:, 0:WD + 8].indirect(T["PR%d" % t][:]), own, ["IO", "PR%d" % t, tab, "FA0", "FA1"], OP.add)

    def begin(i, bank):
        a, b = PORT[i][:2]
        mm(ps(bank, 0, b - a), [bank], T.KT[0:2, :], T.ONE[0:2, a:b], ["KT", "KTc", "ONE"], True, False)

    def ahead():
        mm(ps("ph", 0, 256, 1, 0, 16), ["ph"], T.ZT[0:1, 128:144], T.ONE[0:1, 0:256], ["ONE", "ZTc"], True, False)
        for i, (_, _, raw, rest) in enumerate(PORT):
            for bank in (raw, rest):
                if bank not in ("ph", None):
                    begin(i, bank)

    win = T.X[:, 0:WN]

    def parts_of(buf, k):
        n = CHUNKS[k][0]
        return buf[:, MBASE[k]:MBASE[k] + 16 * n], buf[:, MBASE[k] + 16 * n:MBASE[k] + 17 * n], buf[:, MBASE[k]:MBASE[k] + 17 * n]

    def put_far(k, t, d, far):
        act(T[far][:, 0:WD].indirect(parts_of(T["MO%d" % d], k)[1]), [far, far + "d"], T["vs%d" % t][:, 16 * START[k]:16 * START[k + 1]], ["vs%d" % t, "MO%dl%d" % (d, k)], AF.Silu)

    def put_records(d, k, a=0, b=None):
        n, o = CHUNKS[k][0], MBASE[k]
        b = b or n
        mo = T["MO%d" % d]
        cp(T.X[:, 0:WD].indirect(mo[:, o + 16 * n + a:o + 16 * n + b]), ["X", "Xd"], mo[:, o + 16 * a:o + 16 * b], ["MO%dx%d" % (d, k), "MO%dl%d" % (d, k)])

    def put_replica(k, t, d):
        mi = "MI%d%d" % (t, d)
        arrives("M%d%d%d" % (t, d, k), down if t == 0 else up, "%s%d" % (mi, k))
        xn, l2, _ = parts_of(T[mi], k)
        cp(T["XR%d" % t][:, 0:WD].indirect(l2), ["XR%d" % t], xn, ["%s%d" % (mi, k)])

    QS, YC, YL = [["%s%d" % (x, k) for k in range(NC)] for x in ("qs", "yc", "yl")]
    ends = T.qs[:, 15:256:16]

    KB = zbanks(NC)[1]
    cnt = ps(KB, 0, 1, 1, 0, 1)

    def count_pairs():
        act(T.wb[:], ["wb", "k0"], ends, QS, AF.Sign, bias=2047.5, scale=-1.0, accum_out=T.k0[:])
        mm(cnt, [KB], T.CK[:, 0:1], one, ["CK0", "one"], True, False)
        mm(cnt, [KB], T.k0[:], T.CK[:, 1:2], ["k0", "CK1"], False, True)

    def kappa(kd):
        act(T.k1[0:1, :], ["k1"], cnt, [KB], AF.Copy, bias=402653184.0)
        act(T.kr[0:1, :], ["kr"], T.k1[0:1, :], ["k1"], AF.Copy, bias=402653184.0, scale=-1.0)
        act(T.kf[0:1, :], ["kf"], cnt, [KB, "kr"], AF.Identity, bias=T.kr[0:1, :])
        act(T.KT[0:1, :], ["KT"], T.ONE[0:1, 0:128], ["ONE", "kf"], AF.Identity, bias=T.kf[0:1, :], scale=float(kd) + 15.5)

    def step(t, d, z, zr, far):
        mo = "MO%d" % d

        def spread_z(k):
            n, z0 = 16 * CHUNKS[k][0], 16 * START[k]
            first = zbanks(k)[0]
            for i in range(1024 // n):
                cuts = [n * i] + ([512] if n * i < 512 < n * (i + 1) else []) + [n * (i + 1)]
                for a, b in zip(cuts, cuts[1:]):
                    mm(ps(first, a, b), [zbanks(k)[a // 512]], T.IB[:], z[:, z0 + a - n * i:z0 + b - n * i], ["IB"] + zr, True, True)

        def copy_z(k):
            act(T.zp[:, 0:ZP[k]], ["zp"], ps(zbanks(k)[0], 0, ZP[k]), zbanks(k, ZP[k]), AF.Copy)

        def head():
            for l in range(16):
                mm(ps("ph", l, 256, 16, 0, 16), ["ph"], z[:, l:256:16], T.WG[:], ["WG", "GS"] + zr, False, l == 15)
            if (t, d) == (0, 0):
                spread_b(7)

        def remainder():
            x = ps("ph", 0, 128, 1, 0, 16)
            ts(T.ri[0:16, :], ["ri"], x, ["ph"], 2.0 ** -13, OP.add)
            tt(T.UF[0:16, :], ["UF"], x, T.ri[0:16, :], ["ph", "ri"], OP.subtract)
            act(T.SQ[0:16, :], ["SQ"], T.UF[0:16, :], ["UF"], AF.Square)
            cp(T.UZ[0:16, :], ["UZ"], T.UF[0:16, :], ["UF"])
            cp(T.ZT[0:16, 0:128], ["ZT"], ps("ph", 128, 256, 1, 0, 16), ["ph", "ZTc"])

        def terms(i, which):
            a, b = PORT[i][:2]
            bank = PORT[i][which]
            if bank == "ph":
                begin(i, bank)
            mm(ps(bank, 0, b - a), [bank], T.UZ[0:16, :], T.RU[0:16, a:b], ["UZ", "RU"], False, False)
            if b <= WIDE:
                mm(ps(bank, 0, b - a), [bank], T.SQ[0:16, :], T.RQ[0:16, a:b], ["SQ", "RQ"], False, which == 2)
            else:
                mm(ps(bank, 0, b - a), [bank], T.HT[0:16, :], T.RH[0:16, a:b], ["HT", "RH"], False, which == 2)

        def short_h(i):
            if i == 0:
                ts(T.ri[0:16, :], ["ri"], T.SQ[0:16, :], ["SQ"], 524288.0, OP.mult, 2048.0 - 15.0 / 32, OP.add)
            elif i == 1:
                ts(T.hm[0:16, :], ["hm"], T.ri[0:16, :], ["ri"], 4095, OP.bitwise_and)
            else:
                ts(T.HT[0:16, :], ["HT"], T.hm[0:16, :], ["hm"], -2048.0, OP.add)

        def direct(i, j):
            a, b, raw, _ = PORT[i]
            if j == 0:
                ts(T.li[:, a:b], ["li%d" % i], ps(raw, 0, b - a), [raw], 2047.5, OP.add)
            elif j == 1:
                ts(T.lj[:, a:b], ["lj%d" % i], T.li[:, a:b], ["li%d" % i], 4095, OP.bitwise_and)
            else:
                cp(T.LST[:, a:b], ["LST%d" % i], T.lj[:, a:b], ["lj%d" % i])

        def near(i):
            a, b, raw, _ = PORT[i]
            ts(T.RR[:, a:b], ["RR%d" % i], ps(raw, 0, b - a), [raw], 51539607552.0, OP.add, -51539607552.0, OP.add)

        def take(i):
            a, b, _, rest = PORT[i]
            mm(ps(rest, 0, b - a), [rest], T.INB[:], T.RR[:, a:b], ["INB", "RR%d" % i], False, True)

        def lists(i):
            a, b, _, rest = PORT[i]
            ts(T.LST[:, a:b], ["LST%d" % i], ps(rest, 0, b - a), [rest], 2047.5, OP.add)

        def gather(i):
            k, eng, c0, c1 = pieces[i]
            act(T.A[:, 16 * c0:16 * c1], ["A%d" % i], win.indirect(T.LST[:, c0:c1]), ["X"] + lst(c0, c1), AF.Copy)

        def subs(i):
            k, eng, c0, c1 = pieces[i]
            nl = CHUNKS[k][0]
            w = nl * ((64 if eng == "s" else ZP[k] // 16) // nl)
            return [(c, min(c + w, c1)) for c in range(c0, c1, w)]

        def gather_v(i, h):
            c, e = subs(i)[h]
            k = pieces[i][0]
            if ZP[k] == 16 * CHUNKS[k][0]:
                zz, names = z[:, 16 * START[k]:16 * START[k + 1]], zr
            else:
                zz, names = T.zp[:, 0:16 * (e - c)], ["zp"]
            tt(T.A[:, 16 * c:16 * e], ["A%d_%d" % (i, h)], win.indirect(T.LST[:, c:e]), zz, ["X"] + names + lst(c, e), OP.subtract)

        def relu(i):
            k, eng, c0, c1 = pieces[i]
            names = ["A%d_%d" % (i, h) for h in range(len(subs(i)))]
            if eng == "c":
                act(T.M[:, 16 * c0:16 * c1], ["M%d" % i], T.A[:, 16 * c0:16 * c1], names, AF.Abs)
            else:
                ts(T.M[:, 16 * c0:16 * c1], ["M%d" % i], T.A[:, 16 * c0:16 * c1], names, 0.0, OP.max)

        def maxima(i, h=0):
            c, e = subs(i)[h]
            banks = zbanks(pieces[i][0], 16 * (e - c))
            tt(T.M[:, 16 * c:16 * e], ["M%d_%d" % (i, h)], T.A[:, 16 * c:16 * e], ps(banks[0], 0, 16 * (e - c)), ["A%d" % i] + banks, OP.max)

        def sums(src, i, j=None):
            k, c0, c1 = pieces[i][0], pieces[i][2], pieces[j or i][3]
            bank, base = "pk%d" % (k % 2), 32 * START[k]
            names = []
            for p in range(i, (j or i) + 1):
                whole = (src, pieces[p][1]) in (("A", "s"), ("M", "v"), ("M", "c"))
                names += ["%s%d" % (src, p)] if whole else ["%s%d_%d" % (src, p, h) for h in range(len(subs(p)))]
            sel = "E4n" if src == "A" else "E4" if pieces[i][1] == "c" else "E8"
            for l in range(16):
                mm(ps(bank, c0 - base, c1 - base), [bank], T[sel][:, 15 - l:143 - l], T[src][:, 16 * c0 + l:16 * c1:16], [sel] + names, False, False)

        def keys(k, lhsT, rhs, r, start=False, stop=False):
            bank, c0, c1 = "pk%d" % (k % 2), 32 * START[k], 32 * START[k + 1]
            mm(ps(bank, 0, c1 - c0), [bank], lhsT, rhs(c0, c1), r, start, stop)

        def open_keys(k):
            keys(k, T.ZT[0:18, 0:128], lambda a, b: T.RZ[0:18, a:b], ["ZT", "RZ"], start=True)

        def bar_keys(k):
            if d > 0:
                keys(k, T.IBAR[:], lambda a, b: T.bar[:, a:b], ["IBAR", "bar"])

        def close_keys(i, j):
            k, c0, c1 = pieces[i][0], pieces[i][2], pieces[j][3]
            bank, base = "pk%d" % (k % 2), 32 * START[k]
            mm(ps(bank, c0 - base, c1 - base), [bank], T.I16[:], T.c16[:, c0:c1], ["I16", "c16"], False, c1 == 32 * START[k + 1])

        def places():
            ts(T.c16[:], ["c16"], T.LST[:], lst(0, 512), -2048.0, OP.add)

        def old_places():
            if d > 0:
                mm(ps("pr", 0, 512), ["pr"], T.LT[0:16, :], T.RH[0:16, :], ["LT", "RH"], True, True)

        def barred():
            if d > 0:
                tt(T.bar[:], ["bar"], T.c16[:], ps("pr", 0, 512), ["c16", "pr"], OP.is_equal)

        def choose(k):
            a, b = START[k], START[k + 1]
            bank = "pk%d" % (k % 2)
            for L in range(a, b):
                op("v", g.vector.tensor_reduce, [bank], ["ym%d" % L], out=T.ym[:, L:L + 1], in_=ps(bank, L - a, 32 * (b - a), b - a), axis=AxisListType.X, op=OP.min)
            ts(T.y[:, a:b], ["y%d" % k], T.ym[:, a:b], ["ym%d" % L for L in range(a, b)], 4095, OP.bitwise_and)
            if k == NC - 1:
                cp(T.yl[:, a:b], ["yl%d" % k], T.y[:, a:b], ["y%d" % k])
            tt(T.yc[:, a:b], ["yc%d" % k], T.y[:, a:b], T.DD[:, a:b], ["y%d" % k, "DD"], OP.max)
            if k < NC - 1:
                cp(T.yl[:, a:b], ["yl%d" % k], T.yc[:, a:b], ["yc%d" % k])

        def fetch_far(k):
            a, b = START[k], START[k + 1]
            ts(T.FG[:, 16 * a:16 * b], ["FG%d" % k], T[far][:, 0:WD].indirect(T.yl[:, a:b]), [far, far + "d", "yl%d" % k], 1.0 / FRAC, OP.mult, 4096.0, OP.min)

        def fetch_records(k):
            a, b = START[k], START[k + 1]
            act(T.XG[:, 16 * a:16 * b], ["XG%d" % k], T.X[:, 0:WD].indirect(T.yl[:, a:b]), ["X", "Xd", "yl%d" % k], AF.Copy)

        def prepare(k):
            a, b = START[k], START[k + 1]
            n = 16 * (b - a)
            pq, pt = zbanks(k)
            mm(ps(pq, 0, n), [pq], T.IB[:], T.OFFB[:, 0:n], ["IB", "OFFB"], True, False)
            mm(ps(pt, 0, n), [pt], T.IB[:], T["SR%d" % t][:, 16 * a:16 * b], ["IB", "SR%d" % t], True, False)
            if k == NC - 1:
                for l in range(16):
                    mm(ps(pq, l, n, 16), [pq], T.IB2[:], T.DD[:, a:b], ["IB2", "DD"], False, False)

        def compare(k):
            a, b = START[k], START[k + 1]
            n = 16 * (b - a)
            pq, pt = zbanks(k)
            mm(ps(pq, 0, n), [pq], T.I16[:], T.FG[:, 16 * a:16 * b], ["I16", "FG%d" % k], False, False)
            base = 0
            for L in range(a, b):
                w, e, o = 16 * (b - L), "EQ%d" % (L - a), 16 * (L - a)
                ts(T.EQ[:, base:base + w], [e], T.FG[:, 16 * L:16 * b], ["FG%d" % k, "yc%d" % k], 2048.0, OP.add, T.yc[:, L:L + 1], OP.is_equal)
                if w > 16:
                    mm(ps(pq, o + 16, n), [pq], T.BO[:], T.EQ[:, base + 16:base + w], ["BO", e], False, False)
                mm(ps(pq, o, o + 16), [pq], T.TRI[:], T.EQ[:, base:base + 16], ["TRI", e], False, L == b - 1)
                base += w

        def settle(k):
            a, b = START[k], START[k + 1]
            n = 16 * (b - a)
            pq, pt = zbanks(k)
            xn, l2, whole = parts_of(T[mo], k)
            mm(ps(pt, 0, n), [pt], T.IB[:], T.XG[:, 16 * a:16 * b], ["IB", "XG%d" % k], False, True)
            scan(T.qs[:, 16 * a:16 * b], ["qs%d" % k], T.SEG[:, 16 * a:16 * b], ps(pq, 0, n), ["SEG", pq], -8192.0, OP.max, OP.min)
            ts(xn, ["%sx%d" % (mo, k)], ps(pt, 0, n), [pt], 0.5, OP.mult, -0.25, OP.add)
            ts(l2, ["%sl%d" % (mo, k)], T.qs[:, 16 * a + 15:16 * b:16], ["qs%d" % k], 2048.0, OP.add)
            if d < STEPS - 1:
                send("M%d%d%d" % (t, d, k), up if t == 0 else down, parts_of(T["MI%d%d" % (t, d)], k)[2], whole, ["%sx%d" % (mo, k), "%sl%d" % (mo, k)])

        dr = "DR%d" % t

        def partners():
            act(T.FP[:], ["FP"], T[far][:, 0:WD].indirect(T.yl[:]), [far, far + "d"] + YL, AF.Copy)

        def own_column():
            scan(T.ps[:], ["ps"], T.DX[:], T.FP[:], ["DX", "FP"], 0.0, OP.mult, OP.add)
            ts(T.pl16[:], ["pl16"], T.ps[:, 15:256:16], ["ps", "dn20"], dn20, OP.mult, -1.0, OP.add)

        def turn():
            ts(T.TB[:], ["TB"], T.yc[:], YC, -2048.0, OP.add)
            mm(ps("z0a", 0, 128, 1, 0, 16), ["z0a"], T.TB[:], T.I16[:], ["TB", "I16"], True, True)

        def turned():
            cp(T.LT[0:16, :], ["LT"], ps("z0a", 0, 128, 1, 0, 16), ["z0a"])

        def next_z():
            xr = T["XR%d" % t][:, 0:WN]
            act(T.zb[:, 0:16 * ZS], ["zb0"], xr.indirect(T.pl16[:, 0:ZS]), ["XR%d" % t, "pl16"], AF.Copy)
            if ZS < 16:
                cp(T.zb[:, 16 * ZS:256], ["zb1"], xr.indirect(T.pl16[:, ZS:16]), ["XR%d" % t, "pl16"])

        def paired():
            tt(T[dr][:], [dr], T[dr][:], ends, [dr] + QS, OP.min)
            if t == 1:
                tt(T.PL[:], ["PL"], T.PL[:], ends, ["PL"] + QS, OP.min)

        def home():
            ts(T["PS%d" % t][:], ["PS%d" % t], T[dr][:], [dr], 2049.0, OP.add)
            send("P%d" % t, down if t == 0 else up, T["PR%d" % t][:], T["PS%d" % t][:], ["PS%d" % t])
            arrives("P%d" % t, up if t == 0 else down, "PR%d" % t)

        def flags():
            scan(T.ps[:], ["ps"], T.DX[:], T.FB[:, 1:WN:16], ["DX", "FB"], 0.0, OP.mult, OP.add)
            ts(T.DS1[:], ["DS1"], T.ps[:, 15:256:16], ["ps", "nd20"], nd20, OP.mult, 8192.0, OP.add)
            send("D1", down, T.DR1[:], T.DS1[:], ["DS1"])
            arrives("D1", up, "DR1")

        def starts():
            send_starts(1, down)
            arrives("S1", up, "SR1")

        def whole():
            send_all(1, down)
            arrives("B1", up, "XR1")

        def out_a():
            ts(T.PLl[:], ["PLl"], T.PL[:], ["PL"], 2048.0, OP.add)
            cp(T.PA[:, 0:WD].indirect(T.PLl[:]), ["PA"], T.vr0[:], ["vr0", "PLl"])
            dma("s", "outa", [(T.ya[:], T.PA[0:128:16, 0:WN])], ["PA"], [])

        def out_b():
            near_update(1, "PB")
            dma("s", "outb", [(T.yb[:], T.PB[0:128:16, 0:WN])], ["PB"], [])

        return {"x": lambda *k: put_records(d, *k), "r": lambda k: put_replica(k, t, d), "f": lambda k: put_far(k, t, d, far),
                "fp": partners, "pl": own_column, "tb": turn, "lt": turned, "z": next_z, "won": paired, "dead": lambda: dead(t),
                "kappa": lambda: kappa(97 * (d + 1) % (97 * STEPS)), "ahead": ahead, "home": home, "flags": flags, "starts": starts, "whole": whole,
                "outx": lambda: dma("y", "outx", [(T.yx[:], T.X[:, 0:WN])], ["X"], []), "outa": out_a, "outb": out_b,
                "W": lambda i: terms(i, 2), "E": lambda i: terms(i, 3), "N": near, "T": take, "L": lists, "G": gather, "V": gather_v, "R": relu,
                "count": count_pairs, "X": maxima, "A": lambda *i: sums("A", *i), "M": lambda *i: sums("M", *i), "O": open_keys, "B": bar_keys, "C": close_keys,
                "Z": spread_z, "Y": copy_z, "H": choose, "P": prepare, "Q": compare, "U": settle,
                "D": direct, "K": fetch_far, "J": fetch_records, "h": short_h, "hash": head, "u": remainder, "c16": places, "last": old_places, "bar": barred}

    before_ = None
    ahead()
    for i in range(4, 7):
        spread_b(i)
    for t in range(2):
        far = "FB" if t == 0 else "FA"
        for d in range(STEPS):
            extra = []
            if d == 0:
                extra.append(lambda: dead(t))
            if (t, d) == (0, 0):
                extra += [late_constants, store_a]
            if t == 0 and d > 0:
                extra.append(lambda: spread_a(d - 1))
                h = 2048 * (d - 1)
                iota(T.IO[:, h:h + 2048 + d - 1], "IO", [[1, 2048 + d - 1]], h)
            if (t, d) == (1, 0):
                iota(T.PB[:, 1:WN:16], "PB", [[0, 256]], 0)
                plain_in("FB", 1)
                extra += [lambda: near_update(0, "FA"), lambda: plain_in("FA", 0)]
            if (t, d) == (1, 1):
                extra += [lambda: plain_out(0), lambda: plain_out(1)]
            z, zr = (T["SR%d" % t], ["SR%d" % t]) if d == 0 else (T.zb, ["zb0", "zb1"])
            call = step(t, d, z, zr, far)
            call["extra"] = lambda: [f() for f in extra]
            for w in (ORDER + " " + (NEXT if d < STEPS - 1 else END[t])).split():
                calls = call
                if w[0] == "<":
                    calls, w = before_, w[1:]
                    if d == 0:
                        continue
                if w in calls:
                    calls[w]()
                else:
                    calls[w[0]](*[int(x) for x in w[1:].split(".")])
            before_ = call
    for sem in sorted(count):
        wait("g", [("", sem, count[sem])])
